import numpy as np
import ml_dtypes


def mxq(x, axis, fmt="e4m3"):
    dtype, down = {"e4m3": (ml_dtypes.float8_e4m3fn, 7), "e5m2": (ml_dtypes.float8_e5m2, 14)}[fmt]
    v = np.moveaxis(np.asarray(x, np.float32).astype(ml_dtypes.bfloat16).astype(np.float64), axis, -1)
    blocks = v.reshape(v.shape[:-1] + (-1, 32))
    amax = np.abs(blocks).max(-1, keepdims=True)
    byte = np.maximum(np.where(amax > 0, np.frexp(amax)[1] - 1 + 127, 0) - down, 1)
    scale = np.exp2(byte - 127.0)
    codes = (blocks / scale).astype(np.float32).astype(dtype).astype(np.float64)
    return np.moveaxis((codes * scale).reshape(v.shape), -1, axis)


WIDE = False


def mx_kscale(k):
    if not WIDE:
        return np.ones(k)
    levels = np.array([18, -18])
    if k % 512:
        return np.exp2(np.random.permutation(np.resize(levels, k // 32))).repeat(32)
    a = np.empty((k // 512, 16))
    for p in range(k // 512):
        a[p, :8] = np.random.permutation(np.resize(levels, 8))
        for g in range(8):
            far = levels[np.abs(levels - a[p, g]) >= 10]
            a[p, g + 8] = far[np.random.randint(len(far))]
    return np.exp2(a.ravel()).repeat(32)


def f64(x):
    return np.asarray(x).astype(np.float64)


def striped(idx):
    return np.tile(np.asarray(idx).reshape(-1, 16).T, (8, 1)).astype(np.uint16)


def unstriped(offs):
    return offs[:16].T.reshape(-1).astype(np.int64)


B, N, T, D, R = 1, 512, 2048, 512, 1024


def setup_inputs():
    n = np.random.standard_normal
    idx = np.random.permutation(T)[:B * N]
    s = mx_kscale(D)[:, None]
    z = mx_kscale(R)[:, None]
    u = np.ones(T)
    u[idx] = mx_kscale(B * N)
    r = np.random.uniform(0.5, 2.0, T) * u
    x = n((B, D, R))
    return {
        "xT": (x * s).astype(np.float32),
        "wT": (n((D, T)) * (1.00 / np.sqrt(D)) / s / r).astype(np.float32),
        "y": (2 * np.random.randint(0, 2, (B, R, N)) - 1).astype(np.float32),
        "wt": (np.random.uniform(0.5, 1.5, (B, R, 1)) * 1.0 / np.sqrt(R) * z).astype(np.float32),
        "ts": np.tile(r, (128, 1)).astype(np.float32),
        "xm": (x.transpose(0, 2, 1) / z).astype(np.float32),
        "offs": striped(idx),
    }


def reference(xT, wT, y, wt, ts, xm, offs):
    idx = unstriped(offs)
    pick = lambda x: x[:, idx].reshape(x.shape[0], B, N).transpose(1, 0, 2)
    w = pick(f64(wT))
    a = mxq(f64(xT), 1, "e4m3").transpose(0, 2, 1) @ mxq(w, 1, "e4m3")
    ts_ = pick(f64(ts))[:, :1, :]
    a = a * ts_
    g = -f64(wt) * f64(y) * np.maximum(1.0 - f64(y) * a, 0.0)
    g = g * ts_
    dw = mxq(f64(xm), 1, "e4m3").transpose(0, 2, 1) @ mxq(g, 1, "e5m2")
    gw = np.zeros((D, T))
    gw[:, idx] = dw.transpose(1, 0, 2).reshape(D, B * N)
    gx = mxq(g, 2, "e5m2") @ mxq(w, 2, "e4m3").transpose(0, 2, 1)
    return gw, gx

@@ -1,0 +1,222 @@
+from contextlib import ExitStack
+
+import concourse.mybir as mybir
+from concourse.masks import make_identity
+
+N, T, D, R = 512, 2048, 512, 1024
+FLOPS = 3 * 2 * N * D * R
+
+F32 = mybir.dt.float32
+BF16 = mybir.dt.bfloat16
+U32 = mybir.dt.uint32
+U16 = mybir.dt.uint16
+U8 = mybir.dt.uint8
+E4 = mybir.dt.float8_e4m3fn_x4
+E5 = mybir.dt.float8_e5m2_x4
+MULT = mybir.AluOpType.mult
+RELU = mybir.ActivationFunctionType.Relu
+
+P = 128
+G = R // 512
+
+
+def tile_attend_gsqh_wx_ts_kernel(tc, xT, wT, y, wt, ts, xm, offs, out_0, out_1):
+    nc = tc.nc
+    with ExitStack() as ctx:
+        keep = ctx.enter_context(tc.tile_pool(name="keep", bufs=1))
+        ring = ctx.enter_context(tc.tile_pool(name="ring", bufs=3))
+        ps_a = ctx.enter_context(tc.psum_pool(name="ps_a", bufs=2))
+        ps_t = ctx.enter_context(tc.psum_pool(name="ps_t", bufs=2))
+        ps_w = ctx.enter_context(tc.psum_pool(name="ps_w", bufs=1))
+
+        def sb(name, shape, dtype, tag=None):
+            return keep.tile(shape, dtype, name=name, tag=tag or name, align_bytes=64)
+
+        def quantise(name, src, fmt):
+            width = src.shape[1] // 4
+            codes = sb(name + "_codes", [P, width], U32)
+            scales = sb(name + "_scales", [P, width], U8)
+            nc.vector.quantize_mx(out=codes[:].bitcast(fmt), scales=scales[:], in_=src)
+            return codes, scales
+
+        def mx(out, lhs, lhs_cols, lhs_fmt, rhs, rhs_fmt, start, stop):
+            nc.tensor.matmul_mx(
+                out=out,
+                lhsT=lhs[0][:, lhs_cols].bitcast(lhs_fmt),
+                lhsT_scale=lhs[1][:, lhs_cols],
+                rhs=rhs[0][:].bitcast(rhs_fmt),
+                rhs_scale=rhs[1][:],
+                start=start,
+                stop=stop,
+            )
+
+        offsets = keep.tile([P, N // 16], U16, name="offsets")
+        nc.sync.dma_start(offsets[:], offs)
+
+        w_planes = [sb(f"w_plane{j}", [P, T], F32) for j in range(4)]
+        x_raw = [sb(f"x_raw{g}", [P, 4, 512], F32) for g in range(G)]
+        y_sb = [sb(f"y_sb{g}", [P, 4, N], F32) for g in range(G)]
+        wt_sb = sb("wt_sb", [P, G, 4], F32)
+        ts_row = sb("ts_row", [P, T], F32)
+        windows = [sb(f"window{b}", [P, T], F32) for b in range(4)]
+        ident = sb("ident", [P, P], F32)
+
+        w_view = wT.rearrange("(p j) t -> j p t", j=4)
+        x_view = xT[0].rearrange("(p j) (g r) -> g p j r", j=4, g=G)
+        y_view = y[0].rearrange("(g p t) i -> g p t i", g=G, t=4)
+        xm_view = xm[0].rearrange("(g p t) d -> g p t d", g=G, t=4)
+        gx_view = out_1[0].rearrange("(g p t) d -> g p t d", g=G, t=4)
+
+        nc.vector.memset(ts_row[:], 0.0)
+        nc.scalar.dma_start(ts_row[0:1, :], ts[0:1, :])
+        make_identity(nc, ident[:])
+
+        for j in range(3):
+            nc.sync.dma_start(w_planes[j][:], w_view[j])
+        nc.sync.dma_start(x_raw[0][:], x_view[0])
+        nc.sync.dma_start(w_planes[3][:], w_view[3])
+        nc.sync.dma_start(wt_sb[:], wt[0].rearrange("(g p t) o -> p g (t o)", g=G, t=4))
+        nc.sync.dma_start(y_sb[0][:, 0:2, :], y_view[0][:, 0:2, :])
+        nc.sync.dma_start(y_sb[0][:, 2:4, :], y_view[0][:, 2:4, :])
+        nc.sync.dma_start(x_raw[1][:], x_view[1])
+        nc.sync.dma_start(y_sb[1][:], y_view[1])
+
+        nc.vector.memset(windows[0][:], 0.0)
+        for b in range(1, 4):
+            nc.gpsimd.memset(windows[b][:], 0.0)
+
+        w_il = sb("w_il", [P, N, 4], BF16)
+        nc.vector.tensor_copy(w_il[:, :, 0], w_planes[0][:].indirect(offsets[:]))
+        ts_g = sb("ts_g", [P, N], F32)
+        nc.vector.tensor_copy(ts_g[:], ts_row[:].indirect(offsets[:]))
+        for j in range(1, 3):
+            nc.vector.tensor_copy(w_il[:, :, j], w_planes[j][:].indirect(offsets[:]))
+
+        xm_raw = [sb(f"xm_raw{g}", [P, 4, D], F32, tag=f"w_plane{g}") for g in range(G)]
+        nc.sync.dma_start(xm_raw[0][:], xm_view[0])
+        nc.sync.dma_start(xm_raw[1][:], xm_view[1])
+
+        bank = ps_t.tile([P, 4, P], F32, name="tbank")
+        for c in range(4):
+            nc.tensor.transpose(bank[:, c, :], ts_g[:, c * P : (c + 1) * P], ident[:])
+        ts_col = sb("ts_col", [P, 4], F32)
+        nc.scalar.copy(ts_col[:], bank[:, :, 0])
+        bank = ps_t.tile([P, 4, P], F32, name="tbank")
+        for c in range(4):
+            nc.tensor.transpose(bank[:, c, :], ts_col[:, c : c + 1].to_broadcast([P, P]), ident[:])
+        ts_all = sb("ts_all", [P, N], F32)
+        nc.scalar.copy(ts_all[:], bank[:].rearrange("p c m -> p (c m)"))
+
+        def x_interleave(g):
+            x_il = sb(f"x_il{g}", [P, 4, P, 4], BF16)
+            nc.scalar.copy(
+                x_il[:].rearrange("p t m j -> p m j t"),
+                x_raw[g][:].rearrange("p j (m t) -> p m j t", t=4),
+            )
+            return x_il[:].rearrange("p t m j -> p (t m j)")
+
+        def interleave(engine_copy, name, src):
+            il = sb(name, [P, 512, 4], BF16)
+            engine_copy(
+                il[:].rearrange("p (c i) t -> p c t i", i=4),
+                src.rearrange("p t (c i) -> p c t i", i=4),
+            )
+            return il[:].rearrange("p c t -> p (c t)")
+
+        x_q = [None] * G
+        x_q[0] = quantise("x0", x_interleave(0), E4)
+        nc.vector.tensor_copy(w_il[:, :, 3], w_planes[3][:].indirect(offsets[:]))
+        w_q = quantise("w", w_il[:].rearrange("p i j -> p (i j)"), E4)
+
+        h_sb = [sb(f"h_sb{g}", [P, 4, N], BF16) for g in range(G)]
+        h_q = [None] * G
+        xm_q = [None] * G
+        dw_ps = [ps_w.tile([P, N], F32, name=f"dw_ps{b}") for b in range(4)]
+
+        state = {}
+
+        def front(g, t):
+            c = ring.tile([P, N], F32, name="c")
+            nc.vector.scalar_tensor_tensor(c[:], y_sb[g][:, t, :], -1.0, ts_all[:], MULT, MULT)
+            a = ps_a.tile([P, N], F32, name="acc")
+            mx(a[:], x_q[g], slice(t * P, (t + 1) * P), E4, w_q, E4, True, True)
+            z = ring.tile([P, N], F32, name="z")
+            nc.vector.tensor_tensor(z[:], a[:], c[:], MULT)
+            m = ring.tile([P, N], F32, name="m")
+            nc.scalar.activation(m[:], z[:], RELU, bias=1.0, scale=1.0)
+            state[(g, t)] = (c, m)
+
+        def back(g, t):
+            c, m = state[(g, t)]
+            nc.vector.scalar_tensor_tensor(h_sb[g][:, t, :], m[:], wt_sb[:, g, t : t + 1], c[:], MULT, MULT)
+
+        def dw_pass(g, b):
+            mx(dw_ps[b][:], xm_q[g], slice(b * P, (b + 1) * P), E4, h_q[g], E5, g == 0, g == G - 1)
+
+        front(0, 0)
+        front(0, 1)
+        back(0, 0)
+        x1 = x_interleave(1)
+        front(0, 2)
+        back(0, 1)
+        front(0, 3)
+        back(0, 2)
+        x_q[1] = quantise("x1", x1, E4)
+        back(0, 3)
+        front(1, 0)
+        h0 = interleave(nc.scalar.copy, "h_il0", h_sb[0][:])
+        front(1, 1)
+        back(1, 0)
+        xm0 = interleave(nc.scalar.copy, "xm_il0", xm_raw[0][:])
+        h_q[0] = quantise("h0", h0, E5)
+        front(1, 2)
+        back(1, 1)
+        front(1, 3)
+        xm1 = interleave(nc.scalar.copy, "xm_il1", xm_raw[1][:])
+        xm_q[0] = quantise("xm0", xm0, E4)
+        for b in range(4):
+            dw_pass(0, b)
+        back(1, 2)
+        back(1, 3)
+        xm_q[1] = quantise("xm1", xm1, E4)
+        h1 = interleave(nc.vector.tensor_copy, "h_il1", h_sb[1][:])
+        h_q[1] = quantise("h1", h1, E5)
+        for b in range(4):
+            dw_pass(1, b)
+            dw_sb = sb(f"dw_sb{b}", [P, N], F32)
+            nc.scalar.copy(dw_sb[:], dw_ps[b][:])
+            nc.vector.tensor_copy(windows[b][:].indirect(offsets[:]), dw_sb[:])
+            nc.sync.dma_start(out_0[b * P : (b + 1) * P, :], windows[b][:])
+
+        w_words = w_il[:].rearrange("p i j -> p (i j)").bitcast(F32)
+        ws_il = sb("ws_il", [P, 2, P, 2, 4], BF16)
+        for u in range(2):
+            bank = ps_t.tile([P, 4, P], F32, name="tbank")
+            for t in range(4):
+                nc.tensor.transpose(bank[:, t, :], w_words[:, 2 * t + u : 2 * N : 8], ident[:])
+            nc.scalar.copy(
+                ws_il[:, u, :, :, :],
+                bank[:].rearrange("p t q -> p (t q)").bitcast(BF16).rearrange("p (t q e) -> p q e t", t=4, e=2),
+            )
+        ws_q = quantise("ws", ws_il[:].rearrange("p u q e t -> p (u q e t)"), E4)
+
+        for g in range(G):
+            hs_il = sb(f"hs_il{g}", [P, 4, P, 2], F32)
+            for half in range(2):
+                bank = ps_t.tile([P, 2, 2, P], F32, name="tbank")
+                for s in range(2):
+                    words = h_sb[g][:, 2 * half + s, :].bitcast(F32)
+                    for u in range(2):
+                        nc.tensor.transpose(bank[:, s, u, :], words[:, u : N // 2 : 2], ident[:])
+                nc.scalar.copy(hs_il[:, 2 * half : 2 * half + 2, :, :], bank[:].rearrange("p s u r -> p s r u"))
+            hs_q = quantise(f"hs{g}", hs_il[:].rearrange("p t r u -> p (t r u)").bitcast(BF16), E5)
+            gx_sb = sb(f"gx_sb{g}", [P, 4, D], F32)
+            for t in range(4):
+                acc = ps_a.tile([P, D], F32, name="acc")
+                mx(acc[:], hs_q, slice(t * P, (t + 1) * P), E5, ws_q, E4, True, True)
+                nc.scalar.copy(
+                    gx_sb[:, t, :].rearrange("p (q u e) -> p q u e", u=2, e=2),
+                    acc[:].rearrange("p (u q e) -> p q u e", u=2, e=2),
+                )
+                if t % 2 == 1:
+                    nc.sync.dma_start(gx_view[g][:, t - 1 : t + 1, :], gx_sb[:, t - 1 : t + 1, :])

@@ -14,6 +14,8 @@ U8 = mybir.dt.uint8
 E4 = mybir.dt.float8_e4m3fn_x4
 E5 = mybir.dt.float8_e5m2_x4
 MULT = mybir.AluOpType.mult
+SIGN = mybir.ActivationFunctionType.Sign
+ABS = mybir.ActivationFunctionType.Abs
 RELU = mybir.ActivationFunctionType.Relu
 
 P = 128
@@ -32,23 +34,27 @@ def tile_attend_gsqh_wx_ts_kernel(tc, xT, wT, y, wt, ts, xm, offs, out_0, out_1)
         def sb(name, shape, dtype, tag=None):
             return keep.tile(shape, dtype, name=name, tag=tag or name, align_bytes=64)
 
-        def quantise(name, src, fmt):
-            width = src.shape[1] // 4
-            codes = sb(name + "_codes", [P, width], U32)
-            scales = sb(name + "_scales", [P, width], U8)
-            nc.vector.quantize_mx(out=codes[:].bitcast(fmt), scales=scales[:], in_=src)
-            return codes, scales
+        def mx_tiles(name, tag=None):
+            return sb(name + "_codes", [P, 512], U32, tag), sb(name + "_scales", [P, 512], U8)
 
-        def mx(out, lhs, lhs_cols, lhs_fmt, rhs, rhs_fmt, start, stop):
+        def quantise(dst, cols, src, fmt):
+            nc.vector.quantize_mx(out=dst[0][:, cols].bitcast(fmt), scales=dst[1][:, cols], in_=src)
+
+        def mx(out, lhs, k, lhs_fmt, rhs, rhs_fmt, start, stop):
             nc.tensor.matmul_mx(
                 out=out,
-                lhsT=lhs[0][:, lhs_cols].bitcast(lhs_fmt),
-                lhsT_scale=lhs[1][:, lhs_cols],
+                lhsT=lhs[0][:, block(k)].bitcast(lhs_fmt),
+                lhsT_scale=lhs[1][:, block(k)],
                 rhs=rhs[0][:].bitcast(rhs_fmt),
                 rhs_scale=rhs[1][:],
                 start=start,
                 stop=stop,
             )
+
+        def block(k):
+            return slice(k * P, (k + 1) * P)
+
+        whole = slice(0, 512)
 
         offsets = keep.tile([P, N // 16], U16, name="offsets")
         nc.sync.dma_start(offsets[:], offs)
@@ -56,9 +62,10 @@ def tile_attend_gsqh_wx_ts_kernel(tc, xT, wT, y, wt, ts, xm, offs, out_0, out_1)
         w_planes = [sb(f"w_plane{j}", [P, T], F32) for j in range(4)]
         x_raw = [sb(f"x_raw{g}", [P, 4, 512], F32) for g in range(G)]
         y_sb = [sb(f"y_sb{g}", [P, 4, N], F32) for g in range(G)]
+        xm_raw = [sb(f"xm_raw{g}", [P, 4, D], F32) for g in range(G)]
         wt_sb = sb("wt_sb", [P, G, 4], F32)
+        ts_stage = sb("ts_stage", [1, T], F32, tag="window3")
         ts_row = sb("ts_row", [P, T], F32)
-        windows = [sb(f"window{b}", [P, T], F32) for b in range(4)]
         ident = sb("ident", [P, P], F32)
 
         w_view = wT.rearrange("(p j) t -> j p t", j=4)
@@ -67,156 +74,222 @@ def tile_attend_gsqh_wx_ts_kernel(tc, xT, wT, y, wt, ts, xm, offs, out_0, out_1)
         xm_view = xm[0].rearrange("(g p t) d -> g p t d", g=G, t=4)
         gx_view = out_1[0].rearrange("(g p t) d -> g p t d", g=G, t=4)
 
-        nc.vector.memset(ts_row[:], 0.0)
-        nc.scalar.dma_start(ts_row[0:1, :], ts[0:1, :])
-        make_identity(nc, ident[:])
-
-        for j in range(3):
-            nc.sync.dma_start(w_planes[j][:], w_view[j])
-        nc.sync.dma_start(x_raw[0][:], x_view[0])
-        nc.sync.dma_start(w_planes[3][:], w_view[3])
+        nc.sync.dma_start(ts_stage[:], ts[0:1, :])
+        nc.sync.dma_start(w_planes[0][:], w_view[0])
+        nc.sync.dma_start(w_planes[1][:], w_view[1])
         nc.sync.dma_start(wt_sb[:], wt[0].rearrange("(g p t) o -> p g (t o)", g=G, t=4))
+        nc.sync.dma_start(w_planes[2][:], w_view[2])
         nc.sync.dma_start(y_sb[0][:, 0:2, :], y_view[0][:, 0:2, :])
+        nc.sync.dma_start(w_planes[3][:], w_view[3])
+        nc.sync.dma_start(x_raw[0][:, :, 0:256], x_view[0][:, :, 0:256])
+        nc.sync.dma_start(x_raw[0][:, :, 256:512], x_view[0][:, :, 256:512])
         nc.sync.dma_start(y_sb[0][:, 2:4, :], y_view[0][:, 2:4, :])
         nc.sync.dma_start(x_raw[1][:], x_view[1])
         nc.sync.dma_start(y_sb[1][:], y_view[1])
-
-        nc.vector.memset(windows[0][:], 0.0)
-        for b in range(1, 4):
-            nc.gpsimd.memset(windows[b][:], 0.0)
-
-        w_il = sb("w_il", [P, N, 4], BF16)
-        nc.vector.tensor_copy(w_il[:, :, 0], w_planes[0][:].indirect(offsets[:]))
-        ts_g = sb("ts_g", [P, N], F32)
-        nc.vector.tensor_copy(ts_g[:], ts_row[:].indirect(offsets[:]))
-        for j in range(1, 3):
-            nc.vector.tensor_copy(w_il[:, :, j], w_planes[j][:].indirect(offsets[:]))
-
-        xm_raw = [sb(f"xm_raw{g}", [P, 4, D], F32, tag=f"w_plane{g}") for g in range(G)]
         nc.sync.dma_start(xm_raw[0][:], xm_view[0])
         nc.sync.dma_start(xm_raw[1][:], xm_view[1])
 
-        bank = ps_t.tile([P, 4, P], F32, name="tbank")
-        for c in range(4):
-            nc.tensor.transpose(bank[:, c, :], ts_g[:, c * P : (c + 1) * P], ident[:])
+        nc.vector.memset(ts_row[:], 0.0)
+        nc.vector.tensor_copy(ts_row[0:1, :], ts_stage[:])
+        make_identity(nc, ident[:])
+        windows = [sb(f"window{b}", [P, T], F32) for b in range(4)]
+        for b in range(4):
+            nc.gpsimd.memset(windows[b][:], 0.0)
+
+        ts_g = sb("ts_g", [P, N], F32)
+        nc.vector.tensor_copy(ts_g[:], ts_row[:].indirect(offsets[:]))
+        w_il = sb("w_il", [P, N, 4], BF16)
+        for j in range(3):
+            nc.vector.tensor_copy(w_il[:, :, j], w_planes[j][:].indirect(offsets[:]))
+
+        bank = ps_t.tile([P, 4, P], F32, name="turn")
+        for s in range(4):
+            nc.tensor.transpose(bank[:, s, :], ts_g[:, block(s)], ident[:])
         ts_col = sb("ts_col", [P, 4], F32)
         nc.scalar.copy(ts_col[:], bank[:, :, 0])
-        bank = ps_t.tile([P, 4, P], F32, name="tbank")
-        for c in range(4):
-            nc.tensor.transpose(bank[:, c, :], ts_col[:, c : c + 1].to_broadcast([P, P]), ident[:])
-        ts_all = sb("ts_all", [P, N], F32)
-        nc.scalar.copy(ts_all[:], bank[:].rearrange("p c m -> p (c m)"))
+        ts_all = ps_w.tile([P, N], F32, name="ts_all", tag="dw_ps3")
+        for s in range(4):
+            nc.tensor.transpose(ts_all[:, block(s)], ts_col[:, s : s + 1].to_broadcast([P, P]), ident[:])
 
-        def x_interleave(g):
-            x_il = sb(f"x_il{g}", [P, 4, P, 4], BF16)
-            nc.scalar.copy(
-                x_il[:].rearrange("p t m j -> p m j t"),
-                x_raw[g][:].rearrange("p j (m t) -> p m j t", t=4),
-            )
-            return x_il[:].rearrange("p t m j -> p (t m j)")
-
-        def interleave(engine_copy, name, src):
-            il = sb(name, [P, 512, 4], BF16)
-            engine_copy(
-                il[:].rearrange("p (c i) t -> p c t i", i=4),
-                src.rearrange("p t (c i) -> p c t i", i=4),
-            )
-            return il[:].rearrange("p c t -> p (c t)")
-
-        x_q = [None] * G
-        x_q[0] = quantise("x0", x_interleave(0), E4)
-        nc.vector.tensor_copy(w_il[:, :, 3], w_planes[3][:].indirect(offsets[:]))
-        w_q = quantise("w", w_il[:].rearrange("p i j -> p (i j)"), E4)
-
+        x_il = [sb(f"x_il{g}", [P, 4, P, 4], BF16) for g in range(G)]
+        xm_il = [sb(f"xm_il{g}", [P, D, 4], BF16) for g in range(G)]
         h_sb = [sb(f"h_sb{g}", [P, 4, N], BF16) for g in range(G)]
-        h_q = [None] * G
-        xm_q = [None] * G
-        dw_ps = [ps_w.tile([P, N], F32, name=f"dw_ps{b}") for b in range(4)]
+        h_il = [[sb(f"h_il{g}{half}", [P, 256, 4], BF16) for half in range(2)] for g in range(G)]
+        x_q = [mx_tiles(f"x{g}") for g in range(G)]
+        xm_q = [mx_tiles(f"xm{g}") for g in range(G)]
+        h_q = [mx_tiles(f"h{g}") for g in range(G)]
+        w_q = mx_tiles("w")
+        sc, ve, gp = nc.scalar.copy, nc.vector.tensor_copy, nc.gpsimd
 
-        state = {}
+        def x_interleave(copy, g, half):
+            cols = slice(half * 64, (half + 1) * 64)
+            copy(
+                x_il[g][:].rearrange("p t m j -> p m j t")[:, cols],
+                x_raw[g][:].rearrange("p j (m t) -> p m j t", t=4)[:, cols],
+            )
+
+        def xm_interleave(copy, g, half):
+            cols = slice(half * 64, (half + 1) * 64)
+            copy(
+                xm_il[g][:].rearrange("p (c i) t -> p c t i", i=4)[:, cols],
+                xm_raw[g][:].rearrange("p t (c i) -> p c t i", i=4)[:, cols],
+            )
+
+        def h_interleave(copy, g, half):
+            copy(
+                h_il[g][half][:].rearrange("p (c i) t -> p c t i", i=4),
+                h_sb[g][:, :, half * 256 : (half + 1) * 256].rearrange("p t (c i) -> p c t i", i=4),
+            )
+
+        def quantise_x(g):
+            quantise(x_q[g], whole, x_il[g][:].rearrange("p t m j -> p (t m j)"), E4)
+
+        def quantise_xm(g):
+            quantise(xm_q[g], whole, xm_il[g][:].rearrange("p d t -> p (d t)"), E4)
+
+        def quantise_h(g, half):
+            cols = slice(half * 256, (half + 1) * 256)
+            quantise(h_q[g], cols, h_il[g][half][:].rearrange("p i t -> p (i t)"), E5)
+
+        c_of, m_of = {}, {}
+
+        def signs(g, t):
+            c = ring.tile([P, N], F32, name="c", bufs=6)
+            nc.vector.scalar_tensor_tensor(c[:], y_sb[g][:, t, :], -1.0, ts_all[:], MULT, MULT)
+            c_of[(g, t)] = c
 
         def front(g, t):
-            c = ring.tile([P, N], F32, name="c")
-            nc.vector.scalar_tensor_tensor(c[:], y_sb[g][:, t, :], -1.0, ts_all[:], MULT, MULT)
             a = ps_a.tile([P, N], F32, name="acc")
-            mx(a[:], x_q[g], slice(t * P, (t + 1) * P), E4, w_q, E4, True, True)
-            z = ring.tile([P, N], F32, name="z")
-            nc.vector.tensor_tensor(z[:], a[:], c[:], MULT)
+            mx(a[:], x_q[g], t, E4, w_q, E4, True, True)
+            z = ring.tile([P, N], F32, name="z", bufs=2)
+            nc.vector.tensor_tensor(z[:], a[:], c_of[(g, t)][:], MULT)
             m = ring.tile([P, N], F32, name="m")
             nc.scalar.activation(m[:], z[:], RELU, bias=1.0, scale=1.0)
-            state[(g, t)] = (c, m)
+            m_of[(g, t)] = m
 
         def back(g, t):
-            c, m = state[(g, t)]
-            nc.vector.scalar_tensor_tensor(h_sb[g][:, t, :], m[:], wt_sb[:, g, t : t + 1], c[:], MULT, MULT)
+            nc.vector.scalar_tensor_tensor(
+                h_sb[g][:, t, :], m_of[(g, t)][:], wt_sb[:, g, t : t + 1], c_of[(g, t)][:], MULT, MULT
+            )
+
+        dw_ps = [None] * 4
 
         def dw_pass(g, b):
-            mx(dw_ps[b][:], xm_q[g], slice(b * P, (b + 1) * P), E4, h_q[g], E5, g == 0, g == G - 1)
+            if g == 0:
+                dw_ps[b] = ps_w.tile([P, N], F32, name=f"dw_ps{b}")
+            mx(dw_ps[b][:], xm_q[g], b, E4, h_q[g], E5, g == 0, g == G - 1)
 
+        def gather_last():
+            nc.vector.tensor_copy(w_il[:, :, 3], w_planes[3][:].indirect(offsets[:]))
+            quantise(w_q, whole, w_il[:].rearrange("p i j -> p (i j)"), E4)
+
+        for t in range(4):
+            signs(0, t)
+        gather_last()
+        x_interleave(sc, 0, 0)
+        x_interleave(ve, 0, 1)
+        quantise_x(0)
         front(0, 0)
         front(0, 1)
         back(0, 0)
-        x1 = x_interleave(1)
+        x_interleave(sc, 1, 0)
         front(0, 2)
         back(0, 1)
+        x_interleave(sc, 1, 1)
         front(0, 3)
+        quantise_x(1)
         back(0, 2)
-        x_q[1] = quantise("x1", x1, E4)
-        back(0, 3)
+        signs(1, 0)
         front(1, 0)
-        h0 = interleave(nc.scalar.copy, "h_il0", h_sb[0][:])
+        back(0, 3)
+        signs(1, 1)
         front(1, 1)
+        h_interleave(sc, 0, 0)
         back(1, 0)
-        xm0 = interleave(nc.scalar.copy, "xm_il0", xm_raw[0][:])
-        h_q[0] = quantise("h0", h0, E5)
+        h_interleave(sc, 0, 1)
+        signs(1, 2)
         front(1, 2)
+        xm_interleave(sc, 0, 0)
         back(1, 1)
+        xm_interleave(sc, 0, 1)
+        signs(1, 3)
         front(1, 3)
-        xm1 = interleave(nc.scalar.copy, "xm_il1", xm_raw[1][:])
-        xm_q[0] = quantise("xm0", xm0, E4)
+        xm_interleave(sc, 1, 0)
+        xm_interleave(sc, 1, 1)
+        quantise_h(0, 0)
+        quantise_h(0, 1)
+        back(1, 2)
+        quantise_xm(0)
         for b in range(4):
             dw_pass(0, b)
-        back(1, 2)
         back(1, 3)
-        xm_q[1] = quantise("xm1", xm1, E4)
-        h1 = interleave(nc.vector.tensor_copy, "h_il1", h_sb[1][:])
-        h_q[1] = quantise("h1", h1, E5)
-        for b in range(4):
+        h_interleave(sc, 1, 0)
+        quantise_xm(1)
+        h_interleave(ve, 1, 1)
+        quantise_h(1, 0)
+        quantise_h(1, 1)
+
+        dw_sb = [None] * 4
+
+        def finish_dw(b, tag=None):
             dw_pass(1, b)
-            dw_sb = sb(f"dw_sb{b}", [P, N], F32)
-            nc.scalar.copy(dw_sb[:], dw_ps[b][:])
-            nc.vector.tensor_copy(windows[b][:].indirect(offsets[:]), dw_sb[:])
-            nc.sync.dma_start(out_0[b * P : (b + 1) * P, :], windows[b][:])
+            dw_sb[b] = sb(f"dw_sb{b}", [P, N], F32, tag)
+            nc.scalar.copy(dw_sb[b][:], dw_ps[b][:])
 
-        w_words = w_il[:].rearrange("p i j -> p (i j)").bitcast(F32)
-        ws_il = sb("ws_il", [P, 2, P, 2, 4], BF16)
-        for u in range(2):
-            bank = ps_t.tile([P, 4, P], F32, name="tbank")
-            for t in range(4):
-                nc.tensor.transpose(bank[:, t, :], w_words[:, 2 * t + u : 2 * N : 8], ident[:])
-            nc.scalar.copy(
-                ws_il[:, u, :, :, :],
-                bank[:].rearrange("p t q -> p (t q)").bitcast(BF16).rearrange("p (t q e) -> p q e t", t=4, e=2),
-            )
-        ws_q = quantise("ws", ws_il[:].rearrange("p u q e t -> p (u q e t)"), E4)
+        def scatter(b):
+            nc.vector.tensor_copy(windows[b][:].indirect(offsets[:]), dw_sb[b][:])
+            nc.sync.dma_start(out_0[block(b), :], windows[b][:])
 
-        for g in range(G):
-            hs_il = sb(f"hs_il{g}", [P, 4, P, 2], F32)
+        def slots_w():
+            w_words = w_il[:].rearrange("p i j -> p (i j)").bitcast(F32)
+            ws_il = sb("ws_il", [P, 2, P, 2, 4], BF16)
+            for u in range(2):
+                bank = ps_t.tile([P, 4, P], F32, name="turn")
+                for t in range(4):
+                    nc.tensor.transpose(bank[:, t, :], w_words[:, 2 * t + u : 2 * N : 8], ident[:])
+                nc.scalar.copy(
+                    ws_il[:, u, :, :, :],
+                    bank[:].rearrange("p t q -> p (t q)").bitcast(BF16).rearrange("p (t q e) -> p q e t", t=4, e=2),
+                )
+            ws_q = mx_tiles("ws")
+            quantise(ws_q, whole, ws_il[:].rearrange("p u q e t -> p (u q e t)"), E4)
+            return ws_q
+
+        def slots_h(g, tag):
+            hs_il = sb(f"hs_il{g}", [P, 4, P, 2], F32, f"x_il{g}")
             for half in range(2):
-                bank = ps_t.tile([P, 2, 2, P], F32, name="tbank")
+                bank = ps_t.tile([P, 2, 2, P], F32, name="turn")
                 for s in range(2):
                     words = h_sb[g][:, 2 * half + s, :].bitcast(F32)
                     for u in range(2):
                         nc.tensor.transpose(bank[:, s, u, :], words[:, u : N // 2 : 2], ident[:])
                 nc.scalar.copy(hs_il[:, 2 * half : 2 * half + 2, :, :], bank[:].rearrange("p s u r -> p s r u"))
-            hs_q = quantise(f"hs{g}", hs_il[:].rearrange("p t r u -> p (t r u)").bitcast(BF16), E5)
-            gx_sb = sb(f"gx_sb{g}", [P, 4, D], F32)
-            for t in range(4):
-                acc = ps_a.tile([P, D], F32, name="acc")
-                mx(acc[:], hs_q, slice(t * P, (t + 1) * P), E5, ws_q, E4, True, True)
-                nc.scalar.copy(
-                    gx_sb[:, t, :].rearrange("p (q u e) -> p q u e", u=2, e=2),
-                    acc[:].rearrange("p (u q e) -> p q u e", u=2, e=2),
-                )
-                if t % 2 == 1:
-                    nc.sync.dma_start(gx_view[g][:, t - 1 : t + 1, :], gx_sb[:, t - 1 : t + 1, :])
+            hs_q = mx_tiles(f"hs{g}", tag)
+            quantise(hs_q, whole, hs_il[:].rearrange("p t r u -> p (t r u)").bitcast(BF16), E5)
+            return hs_q
+
+        def rows_out(g, hs_q, ws_q):
+            for pair in range(2):
+                gx = ring.tile([P, 2, D], F32, name="gx", bufs=4)
+                for k in range(2):
+                    acc = ps_a.tile([P, D], F32, name="acc")
+                    mx(acc[:], hs_q, 2 * pair + k, E5, ws_q, E4, True, True)
+                    nc.scalar.copy(
+                        gx[:, k, :].rearrange("p (q u e) -> p q u e", u=2, e=2),
+                        acc[:].rearrange("p (u q e) -> p q u e", u=2, e=2),
+                    )
+                nc.scalar.dma_start(gx_view[g][:, 2 * pair : 2 * pair + 2, :], gx[:])
+
+        finish_dw(0)
+        ws_q = slots_w()
+        hs0 = slots_h(0, "h_il11")
+        hs1 = slots_h(1, "x_il0")
+        scatter(0)
+        rows_out(0, hs0, ws_q)
+        finish_dw(1)
+        scatter(1)
+        finish_dw(2)
+        scatter(2)
+        rows_out(1, hs1, ws_q)
+        finish_dw(3)
+        scatter(3)

@@ -64,7 +64,7 @@ def tile_attend_gsqh_wx_ts_kernel(tc, xT, wT, y, wt, ts, xm, offs, out_0, out_1)
         y_sb = [sb(f"y_sb{g}", [P, 4, N], F32) for g in range(G)]
         xm_raw = [sb(f"xm_raw{g}", [P, 4, D], F32) for g in range(G)]
         wt_sb = sb("wt_sb", [P, G, 4], F32)
-        ts_stage = sb("ts_stage", [1, T], F32, tag="window3")
+        ts_stage = sb("ts_stage", [1, T], F32)
         ts_row = sb("ts_row", [P, T], F32)
         ident = sb("ident", [P, P], F32)
 
@@ -75,9 +75,9 @@ def tile_attend_gsqh_wx_ts_kernel(tc, xT, wT, y, wt, ts, xm, offs, out_0, out_1)
         gx_view = out_1[0].rearrange("(g p t) d -> g p t d", g=G, t=4)
 
         nc.sync.dma_start(ts_stage[:], ts[0:1, :])
+        nc.scalar.dma_start(wt_sb[:], wt[0].rearrange("(g p t) o -> p g (t o)", g=G, t=4))
         nc.sync.dma_start(w_planes[0][:], w_view[0])
         nc.sync.dma_start(w_planes[1][:], w_view[1])
-        nc.sync.dma_start(wt_sb[:], wt[0].rearrange("(g p t) o -> p g (t o)", g=G, t=4))
         nc.sync.dma_start(w_planes[2][:], w_view[2])
         nc.sync.dma_start(y_sb[0][:, 0:2, :], y_view[0][:, 0:2, :])
         nc.sync.dma_start(w_planes[3][:], w_view[3])
@@ -90,11 +90,11 @@ def tile_attend_gsqh_wx_ts_kernel(tc, xT, wT, y, wt, ts, xm, offs, out_0, out_1)
         nc.sync.dma_start(xm_raw[1][:], xm_view[1])
 
         nc.vector.memset(ts_row[:], 0.0)
-        nc.vector.tensor_copy(ts_row[0:1, :], ts_stage[:])
+        nc.scalar.copy(ts_row[0:1, :], ts_stage[:])
         make_identity(nc, ident[:])
-        windows = [sb(f"window{b}", [P, T], F32) for b in range(4)]
-        for b in range(4):
-            nc.gpsimd.memset(windows[b][:], 0.0)
+        windows = [sb(f"window{b}", [P, T], F32) for b in range(3)]
+        for window in windows:
+            nc.vector.memset(window[:], 0.0)
 
         ts_g = sb("ts_g", [P, N], F32)
         nc.vector.tensor_copy(ts_g[:], ts_row[:].indirect(offsets[:]))
@@ -126,6 +126,12 @@ def tile_attend_gsqh_wx_ts_kernel(tc, xT, wT, y, wt, ts, xm, offs, out_0, out_1)
             copy(
                 x_il[g][:].rearrange("p t m j -> p m j t")[:, cols],
                 x_raw[g][:].rearrange("p j (m t) -> p m j t", t=4)[:, cols],
+            )
+
+        def x_interleave_vector(g, half):
+            cols = slice(half * 64, (half + 1) * 64)
+            nc.vector.tensor_copy(
+                x_il[g][:, :, cols, :], x_raw[g][:].rearrange("p j (m t) -> p t m j", t=4)[:, :, cols, :]
             )
 
         def xm_interleave(copy, g, half):
@@ -183,12 +189,14 @@ def tile_attend_gsqh_wx_ts_kernel(tc, xT, wT, y, wt, ts, xm, offs, out_0, out_1)
             nc.vector.tensor_copy(w_il[:, :, 3], w_planes[3][:].indirect(offsets[:]))
             quantise(w_q, whole, w_il[:].rearrange("p i j -> p (i j)"), E4)
 
-        for t in range(4):
-            signs(0, t)
+        signs(0, 0)
+        signs(0, 1)
         gather_last()
         x_interleave(sc, 0, 0)
-        x_interleave(ve, 0, 1)
+        x_interleave_vector(0, 1)
         quantise_x(0)
+        signs(0, 2)
+        signs(0, 3)
         front(0, 0)
         front(0, 1)
         back(0, 0)
@@ -237,8 +245,8 @@ def tile_attend_gsqh_wx_ts_kernel(tc, xT, wT, y, wt, ts, xm, offs, out_0, out_1)
             nc.scalar.copy(dw_sb[b][:], dw_ps[b][:])
 
         def scatter(b):
-            nc.vector.tensor_copy(windows[b][:].indirect(offsets[:]), dw_sb[b][:])
-            nc.sync.dma_start(out_0[block(b), :], windows[b][:])
+            nc.vector.tensor_copy(windows[b % 3][:].indirect(offsets[:]), dw_sb[b][:])
+            nc.sync.dma_start(out_0[block(b), :], windows[b % 3][:])
 
         def slots_w():
             w_words = w_il[:].rearrange("p i j -> p (i j)").bitcast(F32)

@@ -8,6 +8,7 @@ FLOPS = 3 * 2 * N * D * R
 
 F32 = mybir.dt.float32
 BF16 = mybir.dt.bfloat16
+I32 = mybir.dt.int32
 U32 = mybir.dt.uint32
 U16 = mybir.dt.uint16
 U8 = mybir.dt.uint8
@@ -64,8 +65,8 @@ def tile_attend_gsqh_wx_ts_kernel(tc, xT, wT, y, wt, ts, xm, offs, out_0, out_1)
         y_sb = [sb(f"y_sb{g}", [P, 4, N], F32) for g in range(G)]
         xm_raw = [sb(f"xm_raw{g}", [P, 4, D], F32) for g in range(G)]
         wt_sb = sb("wt_sb", [P, G, 4], F32)
-        ts_stage = sb("ts_stage", [1, T], F32)
-        ts_row = sb("ts_row", [P, T], F32)
+        ts_rows = sb("ts_rows", [P, P], F32)
+        ts_table = sb("ts_table", [P, T], F32)
         ident = sb("ident", [P, P], F32)
 
         w_view = wT.rearrange("(p j) t -> j p t", j=4)
@@ -74,42 +75,41 @@ def tile_attend_gsqh_wx_ts_kernel(tc, xT, wT, y, wt, ts, xm, offs, out_0, out_1)
         xm_view = xm[0].rearrange("(g p t) d -> g p t d", g=G, t=4)
         gx_view = out_1[0].rearrange("(g p t) d -> g p t d", g=G, t=4)
 
-        nc.sync.dma_start(ts_stage[:], ts[0:1, :])
+        nc.sync.dma_start(ts_rows[:], ts[0 : P * P // T, :].rearrange("r (c k) -> (r c) k", k=P))
         nc.scalar.dma_start(wt_sb[:], wt[0].rearrange("(g p t) o -> p g (t o)", g=G, t=4))
+        nc.sync.dma_start(x_raw[0][:], x_view[0])
         nc.sync.dma_start(w_planes[0][:], w_view[0])
         nc.sync.dma_start(w_planes[1][:], w_view[1])
         nc.sync.dma_start(w_planes[2][:], w_view[2])
-        nc.sync.dma_start(y_sb[0][:, 0:2, :], y_view[0][:, 0:2, :])
         nc.sync.dma_start(w_planes[3][:], w_view[3])
-        nc.sync.dma_start(x_raw[0][:, :, 0:256], x_view[0][:, :, 0:256])
-        nc.sync.dma_start(x_raw[0][:, :, 256:512], x_view[0][:, :, 256:512])
-        nc.sync.dma_start(y_sb[0][:, 2:4, :], y_view[0][:, 2:4, :])
+        nc.sync.dma_start(y_sb[0][:, 0:2, :], y_view[0][:, 0:2, :])
         nc.sync.dma_start(x_raw[1][:], x_view[1])
-        nc.sync.dma_start(y_sb[1][:], y_view[1])
+        nc.sync.dma_start(y_sb[0][:, 2:4, :], y_view[0][:, 2:4, :])
+        nc.sync.dma_start(y_sb[1][:, 0:2, :], y_view[1][:, 0:2, :])
         nc.sync.dma_start(xm_raw[0][:], xm_view[0])
         nc.sync.dma_start(xm_raw[1][:], xm_view[1])
+        nc.sync.dma_start(y_sb[1][:, 2:4, :], y_view[1][:, 2:4, :])
 
-        nc.vector.memset(ts_row[:], 0.0)
-        nc.scalar.copy(ts_row[0:1, :], ts_stage[:])
         make_identity(nc, ident[:])
         windows = [sb(f"window{b}", [P, T], F32) for b in range(3)]
         for window in windows:
-            nc.vector.memset(window[:], 0.0)
+            nc.vector.memset(window[:].bitcast(I32), 0)
 
-        ts_g = sb("ts_g", [P, N], F32)
-        nc.vector.tensor_copy(ts_g[:], ts_row[:].indirect(offsets[:]))
+        bank = ps_t.tile([P, P], F32, name="turn")
+        nc.tensor.transpose(bank[:], ts_rows[:], ident[:])
+        ts_col = sb("ts_col", [P, T // P], F32)
+        nc.scalar.copy(ts_col[:], bank[:, 0 : T // P])
+        for quarter in range(4):
+            bank = ps_t.tile([P, 4, P], F32, name="turn")
+            for s in range(4):
+                k = 4 * quarter + s
+                nc.tensor.transpose(bank[:, s, :], ts_col[:, k : k + 1].to_broadcast([P, P]), ident[:])
+            nc.scalar.copy(ts_table[:, quarter * 512 : (quarter + 1) * 512], bank[:].rearrange("p s k -> p (s k)"))
+        ts_all = sb("ts_all", [P, N], F32)
+        nc.vector.tensor_copy(ts_all[:], ts_table[:].indirect(offsets[:]))
         w_il = sb("w_il", [P, N, 4], BF16)
         for j in range(3):
             nc.vector.tensor_copy(w_il[:, :, j], w_planes[j][:].indirect(offsets[:]))
-
-        bank = ps_t.tile([P, 4, P], F32, name="turn")
-        for s in range(4):
-            nc.tensor.transpose(bank[:, s, :], ts_g[:, block(s)], ident[:])
-        ts_col = sb("ts_col", [P, 4], F32)
-        nc.scalar.copy(ts_col[:], bank[:, :, 0])
-        ts_all = ps_w.tile([P, N], F32, name="ts_all", tag="dw_ps3")
-        for s in range(4):
-            nc.tensor.transpose(ts_all[:, block(s)], ts_col[:, s : s + 1].to_broadcast([P, P]), ident[:])
 
         x_il = [sb(f"x_il{g}", [P, 4, P, 4], BF16) for g in range(G)]
         xm_il = [sb(f"xm_il{g}", [P, D, 4], BF16) for g in range(G)]
@@ -126,12 +126,6 @@ def tile_attend_gsqh_wx_ts_kernel(tc, xT, wT, y, wt, ts, xm, offs, out_0, out_1)
             copy(
                 x_il[g][:].rearrange("p t m j -> p m j t")[:, cols],
                 x_raw[g][:].rearrange("p j (m t) -> p m j t", t=4)[:, cols],
-            )
-
-        def x_interleave_vector(g, half):
-            cols = slice(half * 64, (half + 1) * 64)
-            nc.vector.tensor_copy(
-                x_il[g][:, :, cols, :], x_raw[g][:].rearrange("p j (m t) -> p t m j", t=4)[:, :, cols, :]
             )
 
         def xm_interleave(copy, g, half):
@@ -189,21 +183,21 @@ def tile_attend_gsqh_wx_ts_kernel(tc, xT, wT, y, wt, ts, xm, offs, out_0, out_1)
             nc.vector.tensor_copy(w_il[:, :, 3], w_planes[3][:].indirect(offsets[:]))
             quantise(w_q, whole, w_il[:].rearrange("p i j -> p (i j)"), E4)
 
+        x_interleave(sc, 0, 0)
+        x_interleave(sc, 0, 1)
+        quantise_x(0)
+        gather_last()
         signs(0, 0)
         signs(0, 1)
-        gather_last()
-        x_interleave(sc, 0, 0)
-        x_interleave_vector(0, 1)
-        quantise_x(0)
-        signs(0, 2)
-        signs(0, 3)
         front(0, 0)
         front(0, 1)
-        back(0, 0)
         x_interleave(sc, 1, 0)
+        x_interleave(sc, 1, 1)
+        back(0, 0)
+        signs(0, 2)
         front(0, 2)
         back(0, 1)
-        x_interleave(sc, 1, 1)
+        signs(0, 3)
         front(0, 3)
         quantise_x(1)
         back(0, 2)
@@ -212,30 +206,30 @@ def tile_attend_gsqh_wx_ts_kernel(tc, xT, wT, y, wt, ts, xm, offs, out_0, out_1)
         back(0, 3)
         signs(1, 1)
         front(1, 1)
-        h_interleave(sc, 0, 0)
+        xm_interleave(sc, 0, 0)
         back(1, 0)
-        h_interleave(sc, 0, 1)
+        xm_interleave(sc, 0, 1)
+        h_interleave(sc, 0, 0)
+        back(1, 1)
         signs(1, 2)
         front(1, 2)
-        xm_interleave(sc, 0, 0)
-        back(1, 1)
-        xm_interleave(sc, 0, 1)
+        h_interleave(sc, 0, 1)
         signs(1, 3)
         front(1, 3)
         xm_interleave(sc, 1, 0)
         xm_interleave(sc, 1, 1)
+        quantise_xm(0)
         quantise_h(0, 0)
         quantise_h(0, 1)
         back(1, 2)
-        quantise_xm(0)
         for b in range(4):
             dw_pass(0, b)
         back(1, 3)
         h_interleave(sc, 1, 0)
         quantise_xm(1)
         h_interleave(ve, 1, 1)
-        quantise_h(1, 0)
         quantise_h(1, 1)
+        quantise_h(1, 0)
 
         dw_sb = [None] * 4
 

@@ -28,7 +28,7 @@ def tile_attend_gsqh_wx_ts_kernel(tc, xT, wT, y, wt, ts, xm, offs, out_0, out_1)
     with ExitStack() as ctx:
         keep = ctx.enter_context(tc.tile_pool(name="keep", bufs=1))
         ring = ctx.enter_context(tc.tile_pool(name="ring", bufs=3))
-        ps_a = ctx.enter_context(tc.psum_pool(name="ps_a", bufs=2))
+        ps_a = ctx.enter_context(tc.psum_pool(name="ps_a", bufs=4))
         ps_t = ctx.enter_context(tc.psum_pool(name="ps_t", bufs=2))
         ps_w = ctx.enter_context(tc.psum_pool(name="ps_w", bufs=1))
 
@@ -77,14 +77,15 @@ def tile_attend_gsqh_wx_ts_kernel(tc, xT, wT, y, wt, ts, xm, offs, out_0, out_1)
 
         nc.sync.dma_start(ts_rows[:], ts[0 : P * P // T, :].rearrange("r (c k) -> (r c) k", k=P))
         nc.scalar.dma_start(wt_sb[:], wt[0].rearrange("(g p t) o -> p g (t o)", g=G, t=4))
-        nc.sync.dma_start(x_raw[0][:], x_view[0])
         nc.sync.dma_start(w_planes[0][:], w_view[0])
         nc.sync.dma_start(w_planes[1][:], w_view[1])
         nc.sync.dma_start(w_planes[2][:], w_view[2])
         nc.sync.dma_start(w_planes[3][:], w_view[3])
+        nc.sync.dma_start(x_raw[0][:, :, 0:256], x_view[0][:, :, 0:256])
+        nc.sync.dma_start(x_raw[0][:, :, 256:512], x_view[0][:, :, 256:512])
         nc.sync.dma_start(y_sb[0][:, 0:2, :], y_view[0][:, 0:2, :])
-        nc.sync.dma_start(x_raw[1][:], x_view[1])
         nc.sync.dma_start(y_sb[0][:, 2:4, :], y_view[0][:, 2:4, :])
+        nc.sync.dma_start(x_raw[1][:], x_view[1])
         nc.sync.dma_start(y_sb[1][:, 0:2, :], y_view[1][:, 0:2, :])
         nc.sync.dma_start(xm_raw[0][:], xm_view[0])
         nc.sync.dma_start(xm_raw[1][:], xm_view[1])
@@ -92,8 +93,9 @@ def tile_attend_gsqh_wx_ts_kernel(tc, xT, wT, y, wt, ts, xm, offs, out_0, out_1)
 
         make_identity(nc, ident[:])
         windows = [sb(f"window{b}", [P, T], F32) for b in range(3)]
-        for window in windows:
+        for window in windows[:2]:
             nc.vector.memset(window[:].bitcast(I32), 0)
+        nc.gpsimd.memset(windows[2][:].bitcast(I32), 0)
 
         bank = ps_t.tile([P, P], F32, name="turn")
         nc.tensor.transpose(bank[:], ts_rows[:], ident[:])
@@ -105,17 +107,17 @@ def tile_attend_gsqh_wx_ts_kernel(tc, xT, wT, y, wt, ts, xm, offs, out_0, out_1)
                 k = 4 * quarter + s
                 nc.tensor.transpose(bank[:, s, :], ts_col[:, k : k + 1].to_broadcast([P, P]), ident[:])
             nc.scalar.copy(ts_table[:, quarter * 512 : (quarter + 1) * 512], bank[:].rearrange("p s k -> p (s k)"))
-        ts_all = sb("ts_all", [P, N], F32)
-        nc.vector.tensor_copy(ts_all[:], ts_table[:].indirect(offsets[:]))
         w_il = sb("w_il", [P, N, 4], BF16)
         for j in range(3):
             nc.vector.tensor_copy(w_il[:, :, j], w_planes[j][:].indirect(offsets[:]))
+        ts_all = sb("ts_all", [P, N], F32, "w_plane1")
+        nc.vector.tensor_copy(ts_all[:], ts_table[:].indirect(offsets[:]))
 
         x_il = [sb(f"x_il{g}", [P, 4, P, 4], BF16) for g in range(G)]
         xm_il = [sb(f"xm_il{g}", [P, D, 4], BF16) for g in range(G)]
         h_sb = [sb(f"h_sb{g}", [P, 4, N], BF16) for g in range(G)]
         h_il = [[sb(f"h_il{g}{half}", [P, 256, 4], BF16) for half in range(2)] for g in range(G)]
-        x_q = [mx_tiles(f"x{g}") for g in range(G)]
+        x_q = [mx_tiles("x0"), mx_tiles("x1")]
         xm_q = [mx_tiles(f"xm{g}") for g in range(G)]
         h_q = [mx_tiles(f"h{g}") for g in range(G)]
         w_q = mx_tiles("w")
@@ -126,6 +128,12 @@ def tile_attend_gsqh_wx_ts_kernel(tc, xT, wT, y, wt, ts, xm, offs, out_0, out_1)
             copy(
                 x_il[g][:].rearrange("p t m j -> p m j t")[:, cols],
                 x_raw[g][:].rearrange("p j (m t) -> p m j t", t=4)[:, cols],
+            )
+
+        def x_interleave_vector(g, half):
+            cols = slice(half * 64, (half + 1) * 64)
+            nc.vector.tensor_copy(
+                x_il[g][:, :, cols, :], x_raw[g][:].rearrange("p j (m t) -> p t m j", t=4)[:, :, cols, :]
             )
 
         def xm_interleave(copy, g, half):
@@ -176,17 +184,17 @@ def tile_attend_gsqh_wx_ts_kernel(tc, xT, wT, y, wt, ts, xm, offs, out_0, out_1)
 
         def dw_pass(g, b):
             if g == 0:
-                dw_ps[b] = ps_w.tile([P, N], F32, name=f"dw_ps{b}")
+                dw_ps[b] = ps_w.tile([P, N], F32, name=f"dw_ps{b}", tag=f"dw_bank{b % 2}")
             mx(dw_ps[b][:], xm_q[g], b, E4, h_q[g], E5, g == 0, g == G - 1)
 
         def gather_last():
             nc.vector.tensor_copy(w_il[:, :, 3], w_planes[3][:].indirect(offsets[:]))
             quantise(w_q, whole, w_il[:].rearrange("p i j -> p (i j)"), E4)
 
-        x_interleave(sc, 0, 0)
-        x_interleave(sc, 0, 1)
-        quantise_x(0)
         gather_last()
+        x_interleave(sc, 0, 0)
+        x_interleave_vector(0, 1)
+        quantise_x(0)
         signs(0, 0)
         signs(0, 1)
         front(0, 0)
@@ -217,12 +225,12 @@ def tile_attend_gsqh_wx_ts_kernel(tc, xT, wT, y, wt, ts, xm, offs, out_0, out_1)
         signs(1, 3)
         front(1, 3)
         xm_interleave(sc, 1, 0)
-        xm_interleave(sc, 1, 1)
+        xm_interleave(ve, 1, 1)
         quantise_xm(0)
         quantise_h(0, 0)
         quantise_h(0, 1)
         back(1, 2)
-        for b in range(4):
+        for b in range(2):
             dw_pass(0, b)
         back(1, 3)
         h_interleave(sc, 1, 0)
@@ -234,6 +242,8 @@ def tile_attend_gsqh_wx_ts_kernel(tc, xT, wT, y, wt, ts, xm, offs, out_0, out_1)
         dw_sb = [None] * 4
 
         def finish_dw(b, tag=None):
+            if b >= 2:
+                dw_pass(0, b)
             dw_pass(1, b)
             dw_sb[b] = sb(f"dw_sb{b}", [P, N], F32, tag)
             nc.scalar.copy(dw_sb[b][:], dw_ps[b][:])

@@ -15,8 +15,9 @@ U8 = mybir.dt.uint8
 E4 = mybir.dt.float8_e4m3fn_x4
 E5 = mybir.dt.float8_e5m2_x4
 MULT = mybir.AluOpType.mult
-SIGN = mybir.ActivationFunctionType.Sign
-ABS = mybir.ActivationFunctionType.Abs
+ADD = mybir.AluOpType.add
+MAX = mybir.AluOpType.max
+IS_GE = mybir.AluOpType.is_ge
 RELU = mybir.ActivationFunctionType.Relu
 
 P = 128
@@ -84,18 +85,24 @@ def tile_attend_gsqh_wx_ts_kernel(tc, xT, wT, y, wt, ts, xm, offs, out_0, out_1)
         nc.sync.dma_start(x_raw[0][:, :, 0:256], x_view[0][:, :, 0:256])
         nc.sync.dma_start(x_raw[0][:, :, 256:512], x_view[0][:, :, 256:512])
         nc.sync.dma_start(y_sb[0][:, 0:2, :], y_view[0][:, 0:2, :])
-        nc.sync.dma_start(y_sb[0][:, 2:4, :], y_view[0][:, 2:4, :])
         nc.sync.dma_start(x_raw[1][:], x_view[1])
+        nc.sync.dma_start(y_sb[0][:, 2:4, :], y_view[0][:, 2:4, :])
         nc.sync.dma_start(y_sb[1][:, 0:2, :], y_view[1][:, 0:2, :])
+        nc.sync.dma_start(y_sb[1][:, 2:4, :], y_view[1][:, 2:4, :])
         nc.sync.dma_start(xm_raw[0][:], xm_view[0])
         nc.sync.dma_start(xm_raw[1][:], xm_view[1])
-        nc.sync.dma_start(y_sb[1][:, 2:4, :], y_view[1][:, 2:4, :])
 
         make_identity(nc, ident[:])
         windows = [sb(f"window{b}", [P, T], F32) for b in range(3)]
-        for window in windows[:2]:
+        for window in windows:
             nc.vector.memset(window[:].bitcast(I32), 0)
-        nc.gpsimd.memset(windows[2][:].bitcast(I32), 0)
+
+        wt_abs = sb("wt_abs", [P, G, 4], F32)
+        wt_step = sb("wt_step", [P, G, 4], F32)
+        minus_sign = sb("minus_sign", [P, G, 4], F32)
+        nc.vector.tensor_scalar(wt_step[:], wt_sb[:], 0.0, -2.0, IS_GE, MULT)
+        nc.vector.scalar_tensor_tensor(wt_abs[:], wt_sb[:], -1.0, wt_sb[:], MULT, MAX)
+        nc.vector.tensor_scalar(minus_sign[:], wt_step[:], 1.0, None, ADD)
 
         bank = ps_t.tile([P, P], F32, name="turn")
         nc.tensor.transpose(bank[:], ts_rows[:], ident[:])
@@ -115,25 +122,18 @@ def tile_attend_gsqh_wx_ts_kernel(tc, xT, wT, y, wt, ts, xm, offs, out_0, out_1)
 
         x_il = [sb(f"x_il{g}", [P, 4, P, 4], BF16) for g in range(G)]
         xm_il = [sb(f"xm_il{g}", [P, D, 4], BF16) for g in range(G)]
-        h_sb = [sb(f"h_sb{g}", [P, 4, N], BF16) for g in range(G)]
-        h_il = [[sb(f"h_il{g}{half}", [P, 256, 4], BF16) for half in range(2)] for g in range(G)]
+        h_il = [sb(f"h_il{g}", [P, N, 4], BF16) for g in range(G)]
+        margin = [sb(f"margin{g}", [P, 4, N], F32) for g in range(G)]
         x_q = [mx_tiles("x0"), mx_tiles("x1")]
         xm_q = [mx_tiles(f"xm{g}") for g in range(G)]
         h_q = [mx_tiles(f"h{g}") for g in range(G)]
         w_q = mx_tiles("w")
-        sc, ve, gp = nc.scalar.copy, nc.vector.tensor_copy, nc.gpsimd
+        sc, ve = nc.scalar.copy, nc.vector.tensor_copy
 
-        def x_interleave(copy, g, half):
-            cols = slice(half * 64, (half + 1) * 64)
+        def x_interleave(copy, g, lo, hi):
             copy(
-                x_il[g][:].rearrange("p t m j -> p m j t")[:, cols],
-                x_raw[g][:].rearrange("p j (m t) -> p m j t", t=4)[:, cols],
-            )
-
-        def x_interleave_vector(g, half):
-            cols = slice(half * 64, (half + 1) * 64)
-            nc.vector.tensor_copy(
-                x_il[g][:, :, cols, :], x_raw[g][:].rearrange("p j (m t) -> p t m j", t=4)[:, :, cols, :]
+                x_il[g][:].rearrange("p t m j -> p m j t")[:, lo:hi],
+                x_raw[g][:].rearrange("p j (m t) -> p m j t", t=4)[:, lo:hi],
             )
 
         def xm_interleave(copy, g, half):
@@ -143,41 +143,34 @@ def tile_attend_gsqh_wx_ts_kernel(tc, xT, wT, y, wt, ts, xm, offs, out_0, out_1)
                 xm_raw[g][:].rearrange("p t (c i) -> p c t i", i=4)[:, cols],
             )
 
-        def h_interleave(copy, g, half):
-            copy(
-                h_il[g][half][:].rearrange("p (c i) t -> p c t i", i=4),
-                h_sb[g][:, :, half * 256 : (half + 1) * 256].rearrange("p t (c i) -> p c t i", i=4),
-            )
-
         def quantise_x(g):
             quantise(x_q[g], whole, x_il[g][:].rearrange("p t m j -> p (t m j)"), E4)
 
         def quantise_xm(g):
             quantise(xm_q[g], whole, xm_il[g][:].rearrange("p d t -> p (d t)"), E4)
 
-        def quantise_h(g, half):
-            cols = slice(half * 256, (half + 1) * 256)
-            quantise(h_q[g], cols, h_il[g][half][:].rearrange("p i t -> p (i t)"), E5)
+        def quantise_h(g):
+            quantise(h_q[g], whole, h_il[g][:].rearrange("p i t -> p (i t)"), E5)
 
-        c_of, m_of = {}, {}
-
-        def signs(g, t):
-            c = ring.tile([P, N], F32, name="c", bufs=6)
-            nc.vector.scalar_tensor_tensor(c[:], y_sb[g][:, t, :], -1.0, ts_all[:], MULT, MULT)
-            c_of[(g, t)] = c
+        def factor(g, t):
+            c = y_sb[g][:, t, :]
+            nc.vector.scalar_tensor_tensor(c, c, minus_sign[:, g, t : t + 1], ts_all[:], MULT, MULT)
 
         def front(g, t):
             a = ps_a.tile([P, N], F32, name="acc")
             mx(a[:], x_q[g], t, E4, w_q, E4, True, True)
-            z = ring.tile([P, N], F32, name="z", bufs=2)
-            nc.vector.tensor_tensor(z[:], a[:], c_of[(g, t)][:], MULT)
-            m = ring.tile([P, N], F32, name="m")
-            nc.scalar.activation(m[:], z[:], RELU, bias=1.0, scale=1.0)
-            m_of[(g, t)] = m
+            z = ring.tile([P, N], F32, name="z", bufs=3)
+            nc.vector.tensor_tensor(z[:], a[:], y_sb[g][:, t, :], MULT)
+            nc.scalar.activation(
+                margin[g][:, t, :], z[:], RELU, bias=wt_abs[:, g, t : t + 1], scale=wt_sb[:, g, t : t + 1]
+            )
 
-        def back(g, t):
-            nc.vector.scalar_tensor_tensor(
-                h_sb[g][:, t, :], m_of[(g, t)][:], wt_sb[:, g, t : t + 1], c_of[(g, t)][:], MULT, MULT
+        def gradient(g):
+            nc.vector.tensor_tensor(
+                h_il[g][:].rearrange("p (c i) t -> p c t i", i=4),
+                margin[g][:].rearrange("p t (c i) -> p c t i", i=4),
+                y_sb[g][:].rearrange("p t (c i) -> p c t i", i=4),
+                MULT,
             )
 
         dw_ps = [None] * 4
@@ -187,57 +180,71 @@ def tile_attend_gsqh_wx_ts_kernel(tc, xT, wT, y, wt, ts, xm, offs, out_0, out_1)
                 dw_ps[b] = ps_w.tile([P, N], F32, name=f"dw_ps{b}", tag=f"dw_bank{b % 2}")
             mx(dw_ps[b][:], xm_q[g], b, E4, h_q[g], E5, g == 0, g == G - 1)
 
-        def gather_last():
-            nc.vector.tensor_copy(w_il[:, :, 3], w_planes[3][:].indirect(offsets[:]))
-            quantise(w_q, whole, w_il[:].rearrange("p i j -> p (i j)"), E4)
+        def turn_words(src_il, dst_il, pattern):
+            words = src_il[:].rearrange("p i j -> p (i j)").bitcast(F32)
+            for u in range(2):
+                bank = ps_t.tile([P, 4, P], F32, name="turn")
+                for e in range(4):
+                    nc.tensor.transpose(bank[:, e, :], words[:, 2 * e + u : 2 * N : 8], ident[:])
+                nc.scalar.copy(
+                    dst_il[:, u],
+                    bank[:].rearrange("p e q -> p (e q)").bitcast(BF16).rearrange(pattern, e=4, v=2),
+                )
 
-        gather_last()
-        x_interleave(sc, 0, 0)
-        x_interleave_vector(0, 1)
+        ws_il = sb("ws_il", [P, 2, P, 2, 4], BF16, "x_raw0")
+        hs_il = [sb("hs_il0", [P, 2, 2, P, 4], BF16, "xm_raw1"), sb("hs_il1", [P, 2, 2, P, 4], BF16)]
+        ws_q = mx_tiles("ws")
+        hs_q = [mx_tiles(f"hs{g}") for g in range(G)]
+
+        def turn_w():
+            turn_words(w_il, ws_il, "p (e q v) -> p q v e")
+
+        def turn_h(g):
+            turn_words(h_il[g], hs_il[g], "p (e q v) -> p v q e")
+
+        def quantise_ws():
+            quantise(ws_q, whole, ws_il[:].rearrange("p u q v e -> p (u q v e)"), E4)
+
+        def quantise_hs(g):
+            quantise(hs_q[g], whole, hs_il[g][:].rearrange("p u v q e -> p (u v q e)"), E5)
+
+        nc.vector.tensor_copy(w_il[:, :, 3], w_planes[3][:].indirect(offsets[:]))
+        quantise(w_q, whole, w_il[:].rearrange("p i j -> p (i j)"), E4)
+        x_interleave(sc, 0, 0, 64)
+        x_interleave(ve, 0, 64, 104)
+        x_interleave(sc, 0, 104, 128)
         quantise_x(0)
-        signs(0, 0)
-        signs(0, 1)
+        factor(0, 0)
+        factor(0, 1)
         front(0, 0)
         front(0, 1)
-        x_interleave(sc, 1, 0)
-        x_interleave(sc, 1, 1)
-        back(0, 0)
-        signs(0, 2)
+        x_interleave(sc, 1, 0, 64)
+        x_interleave(sc, 1, 64, 128)
+        factor(0, 2)
+        factor(0, 3)
         front(0, 2)
-        back(0, 1)
-        signs(0, 3)
         front(0, 3)
         quantise_x(1)
-        back(0, 2)
-        signs(1, 0)
-        front(1, 0)
-        back(0, 3)
-        signs(1, 1)
-        front(1, 1)
+        factor(1, 0)
+        factor(1, 1)
+        gradient(0)
         xm_interleave(sc, 0, 0)
-        back(1, 0)
         xm_interleave(sc, 0, 1)
-        h_interleave(sc, 0, 0)
-        back(1, 1)
-        signs(1, 2)
+        front(1, 0)
+        front(1, 1)
+        factor(1, 2)
+        factor(1, 3)
         front(1, 2)
-        h_interleave(sc, 0, 1)
-        signs(1, 3)
         front(1, 3)
         xm_interleave(sc, 1, 0)
-        xm_interleave(ve, 1, 1)
+        xm_interleave(sc, 1, 1)
+        quantise_h(0)
         quantise_xm(0)
-        quantise_h(0, 0)
-        quantise_h(0, 1)
-        back(1, 2)
         for b in range(2):
             dw_pass(0, b)
-        back(1, 3)
-        h_interleave(sc, 1, 0)
+        gradient(1)
         quantise_xm(1)
-        h_interleave(ve, 1, 1)
-        quantise_h(1, 1)
-        quantise_h(1, 0)
+        quantise_h(1)
 
         dw_sb = [None] * 4
 
@@ -252,56 +259,31 @@ def tile_attend_gsqh_wx_ts_kernel(tc, xT, wT, y, wt, ts, xm, offs, out_0, out_1)
             nc.vector.tensor_copy(windows[b % 3][:].indirect(offsets[:]), dw_sb[b][:])
             nc.sync.dma_start(out_0[block(b), :], windows[b % 3][:])
 
-        def slots_w():
-            w_words = w_il[:].rearrange("p i j -> p (i j)").bitcast(F32)
-            ws_il = sb("ws_il", [P, 2, P, 2, 4], BF16)
-            for u in range(2):
-                bank = ps_t.tile([P, 4, P], F32, name="turn")
-                for t in range(4):
-                    nc.tensor.transpose(bank[:, t, :], w_words[:, 2 * t + u : 2 * N : 8], ident[:])
-                nc.scalar.copy(
-                    ws_il[:, u, :, :, :],
-                    bank[:].rearrange("p t q -> p (t q)").bitcast(BF16).rearrange("p (t q e) -> p q e t", t=4, e=2),
-                )
-            ws_q = mx_tiles("ws")
-            quantise(ws_q, whole, ws_il[:].rearrange("p u q e t -> p (u q e t)"), E4)
-            return ws_q
-
-        def slots_h(g, tag):
-            hs_il = sb(f"hs_il{g}", [P, 4, P, 2], F32, f"x_il{g}")
-            for half in range(2):
-                bank = ps_t.tile([P, 2, 2, P], F32, name="turn")
-                for s in range(2):
-                    words = h_sb[g][:, 2 * half + s, :].bitcast(F32)
-                    for u in range(2):
-                        nc.tensor.transpose(bank[:, s, u, :], words[:, u : N // 2 : 2], ident[:])
-                nc.scalar.copy(hs_il[:, 2 * half : 2 * half + 2, :, :], bank[:].rearrange("p s u r -> p s r u"))
-            hs_q = mx_tiles(f"hs{g}", tag)
-            quantise(hs_q, whole, hs_il[:].rearrange("p t r u -> p (t r u)").bitcast(BF16), E5)
-            return hs_q
-
-        def rows_out(g, hs_q, ws_q):
+        def rows_out(g):
             for pair in range(2):
                 gx = ring.tile([P, 2, D], F32, name="gx", bufs=4)
                 for k in range(2):
                     acc = ps_a.tile([P, D], F32, name="acc")
-                    mx(acc[:], hs_q, 2 * pair + k, E5, ws_q, E4, True, True)
+                    mx(acc[:], hs_q[g], 2 * pair + k, E5, ws_q, E4, True, True)
                     nc.scalar.copy(
                         gx[:, k, :].rearrange("p (q u e) -> p q u e", u=2, e=2),
                         acc[:].rearrange("p (u q e) -> p q u e", u=2, e=2),
                     )
                 nc.scalar.dma_start(gx_view[g][:, 2 * pair : 2 * pair + 2, :], gx[:])
 
+        turn_w()
+        turn_h(0)
         finish_dw(0)
-        ws_q = slots_w()
-        hs0 = slots_h(0, "h_il11")
-        hs1 = slots_h(1, "x_il0")
+        quantise_ws()
+        quantise_hs(0)
         scatter(0)
-        rows_out(0, hs0, ws_q)
+        rows_out(0)
         finish_dw(1)
         scatter(1)
+        turn_h(1)
+        quantise_hs(1)
         finish_dw(2)
         scatter(2)
-        rows_out(1, hs1, ws_q)
         finish_dw(3)
+        rows_out(1)
         scatter(3)

@@ -16,8 +16,8 @@ E4 = mybir.dt.float8_e4m3fn_x4
 E5 = mybir.dt.float8_e5m2_x4
 MULT = mybir.AluOpType.mult
 ADD = mybir.AluOpType.add
-MAX = mybir.AluOpType.max
 IS_GE = mybir.AluOpType.is_ge
+ABS = mybir.ActivationFunctionType.Abs
 RELU = mybir.ActivationFunctionType.Relu
 
 P = 128
@@ -82,12 +82,11 @@ def tile_attend_gsqh_wx_ts_kernel(tc, xT, wT, y, wt, ts, xm, offs, out_0, out_1)
         nc.sync.dma_start(w_planes[1][:], w_view[1])
         nc.sync.dma_start(w_planes[2][:], w_view[2])
         nc.sync.dma_start(w_planes[3][:], w_view[3])
-        nc.sync.dma_start(x_raw[0][:, :, 0:256], x_view[0][:, :, 0:256])
-        nc.sync.dma_start(x_raw[0][:, :, 256:512], x_view[0][:, :, 256:512])
+        nc.sync.dma_start(x_raw[0][:], x_view[0])
         nc.sync.dma_start(y_sb[0][:, 0:2, :], y_view[0][:, 0:2, :])
-        nc.sync.dma_start(x_raw[1][:], x_view[1])
         nc.sync.dma_start(y_sb[0][:, 2:4, :], y_view[0][:, 2:4, :])
         nc.sync.dma_start(y_sb[1][:, 0:2, :], y_view[1][:, 0:2, :])
+        nc.sync.dma_start(x_raw[1][:], x_view[1])
         nc.sync.dma_start(y_sb[1][:, 2:4, :], y_view[1][:, 2:4, :])
         nc.sync.dma_start(xm_raw[0][:], xm_view[0])
         nc.sync.dma_start(xm_raw[1][:], xm_view[1])
@@ -101,7 +100,7 @@ def tile_attend_gsqh_wx_ts_kernel(tc, xT, wT, y, wt, ts, xm, offs, out_0, out_1)
         wt_step = sb("wt_step", [P, G, 4], F32)
         minus_sign = sb("minus_sign", [P, G, 4], F32)
         nc.vector.tensor_scalar(wt_step[:], wt_sb[:], 0.0, -2.0, IS_GE, MULT)
-        nc.vector.scalar_tensor_tensor(wt_abs[:], wt_sb[:], -1.0, wt_sb[:], MULT, MAX)
+        nc.scalar.activation(wt_abs[:], wt_sb[:], ABS)
         nc.vector.tensor_scalar(minus_sign[:], wt_step[:], 1.0, None, ADD)
 
         bank = ps_t.tile([P, P], F32, name="turn")
@@ -180,10 +179,10 @@ def tile_attend_gsqh_wx_ts_kernel(tc, xT, wT, y, wt, ts, xm, offs, out_0, out_1)
                 dw_ps[b] = ps_w.tile([P, N], F32, name=f"dw_ps{b}", tag=f"dw_bank{b % 2}")
             mx(dw_ps[b][:], xm_q[g], b, E4, h_q[g], E5, g == 0, g == G - 1)
 
-        def turn_words(src_il, dst_il, pattern):
+        def turn_words(src_il, dst_il, pattern, pool, tag):
             words = src_il[:].rearrange("p i j -> p (i j)").bitcast(F32)
             for u in range(2):
-                bank = ps_t.tile([P, 4, P], F32, name="turn")
+                bank = pool.tile([P, 4, P], F32, name=tag)
                 for e in range(4):
                     nc.tensor.transpose(bank[:, e, :], words[:, 2 * e + u : 2 * N : 8], ident[:])
                 nc.scalar.copy(
@@ -197,10 +196,10 @@ def tile_attend_gsqh_wx_ts_kernel(tc, xT, wT, y, wt, ts, xm, offs, out_0, out_1)
         hs_q = [mx_tiles(f"hs{g}") for g in range(G)]
 
         def turn_w():
-            turn_words(w_il, ws_il, "p (e q v) -> p q v e")
+            turn_words(w_il, ws_il, "p (e q v) -> p q v e", ps_t, "turn")
 
         def turn_h(g):
-            turn_words(h_il[g], hs_il[g], "p (e q v) -> p v q e")
+            turn_words(h_il[g], hs_il[g], "p (e q v) -> p v q e", ps_a, "acc")
 
         def quantise_ws():
             quantise(ws_q, whole, ws_il[:].rearrange("p u q v e -> p (u q v e)"), E4)
@@ -210,32 +209,29 @@ def tile_attend_gsqh_wx_ts_kernel(tc, xT, wT, y, wt, ts, xm, offs, out_0, out_1)
 
         nc.vector.tensor_copy(w_il[:, :, 3], w_planes[3][:].indirect(offsets[:]))
         quantise(w_q, whole, w_il[:].rearrange("p i j -> p (i j)"), E4)
-        x_interleave(sc, 0, 0, 64)
-        x_interleave(ve, 0, 64, 104)
-        x_interleave(sc, 0, 104, 128)
+        x_interleave(ve, 0, 0, 80)
+        x_interleave(sc, 0, 80, 128)
         quantise_x(0)
         factor(0, 0)
         factor(0, 1)
         front(0, 0)
         front(0, 1)
-        x_interleave(sc, 1, 0, 64)
-        x_interleave(sc, 1, 64, 128)
         factor(0, 2)
         factor(0, 3)
         front(0, 2)
         front(0, 3)
-        quantise_x(1)
+        x_interleave(sc, 1, 0, 64)
+        x_interleave(sc, 1, 64, 128)
         factor(1, 0)
         factor(1, 1)
         gradient(0)
-        xm_interleave(sc, 0, 0)
-        xm_interleave(sc, 0, 1)
-        front(1, 0)
-        front(1, 1)
+        quantise_x(1)
         factor(1, 2)
         factor(1, 3)
-        front(1, 2)
-        front(1, 3)
+        xm_interleave(sc, 0, 0)
+        xm_interleave(sc, 0, 1)
+        for t in range(4):
+            front(1, t)
         xm_interleave(sc, 1, 0)
         xm_interleave(sc, 1, 1)
         quantise_h(0)

@@ -114,8 +114,9 @@ def tile_attend_gsqh_wx_ts_kernel(tc, xT, wT, y, wt, ts, xm, offs, out_0, out_1)
                 nc.tensor.transpose(bank[:, s, :], ts_col[:, k : k + 1].to_broadcast([P, P]), ident[:])
             nc.scalar.copy(ts_table[:, quarter * 512 : (quarter + 1) * 512], bank[:].rearrange("p s k -> p (s k)"))
         w_il = sb("w_il", [P, N, 4], BF16)
+        w_bf = sb("w_bf", [P, 4, N], BF16)
         for j in range(3):
-            nc.vector.tensor_copy(w_il[:, :, j], w_planes[j][:].indirect(offsets[:]))
+            nc.vector.tensor_copy(w_bf[:, j, :], w_planes[j][:].indirect(offsets[:]))
         ts_all = sb("ts_all", [P, N], F32, "w_plane1")
         nc.vector.tensor_copy(ts_all[:], ts_table[:].indirect(offsets[:]))
 
@@ -135,12 +136,14 @@ def tile_attend_gsqh_wx_ts_kernel(tc, xT, wT, y, wt, ts, xm, offs, out_0, out_1)
                 x_raw[g][:].rearrange("p j (m t) -> p m j t", t=4)[:, lo:hi],
             )
 
-        def xm_interleave(copy, g, half):
-            cols = slice(half * 64, (half + 1) * 64)
+        def interleave(copy, dst, src, lo, hi):
             copy(
-                xm_il[g][:].rearrange("p (c i) t -> p c t i", i=4)[:, cols],
-                xm_raw[g][:].rearrange("p t (c i) -> p c t i", i=4)[:, cols],
+                dst[:].rearrange("p (c i) t -> p c t i", i=4)[:, lo:hi],
+                src[:].rearrange("p t (c i) -> p c t i", i=4)[:, lo:hi],
             )
+
+        def xm_interleave(copy, g, half):
+            interleave(copy, xm_il[g], xm_raw[g], half * 64, (half + 1) * 64)
 
         def quantise_x(g):
             quantise(x_q[g], whole, x_il[g][:].rearrange("p t m j -> p (t m j)"), E4)
@@ -179,35 +182,40 @@ def tile_attend_gsqh_wx_ts_kernel(tc, xT, wT, y, wt, ts, xm, offs, out_0, out_1)
                 dw_ps[b] = ps_w.tile([P, N], F32, name=f"dw_ps{b}", tag=f"dw_bank{b % 2}")
             mx(dw_ps[b][:], xm_q[g], b, E4, h_q[g], E5, g == 0, g == G - 1)
 
-        def turn_words(src_il, dst_il, pattern, pool, tag):
-            words = src_il[:].rearrange("p i j -> p (i j)").bitcast(F32)
-            for u in range(2):
-                bank = pool.tile([P, 4, P], F32, name=tag)
-                for e in range(4):
-                    nc.tensor.transpose(bank[:, e, :], words[:, 2 * e + u : 2 * N : 8], ident[:])
-                nc.scalar.copy(
-                    dst_il[:, u],
-                    bank[:].rearrange("p e q -> p (e q)").bitcast(BF16).rearrange(pattern, e=4, v=2),
-                )
-
-        ws_il = sb("ws_il", [P, 2, P, 2, 4], BF16, "x_raw0")
+        ws_il = sb("ws_il", [P, 4, P, 2], F32, "x_raw0")
         hs_il = [sb("hs_il0", [P, 2, 2, P, 4], BF16, "xm_raw1"), sb("hs_il1", [P, 2, 2, P, 4], BF16)]
         ws_q = mx_tiles("ws")
         hs_q = [mx_tiles(f"hs{g}") for g in range(G)]
 
         def turn_w():
-            turn_words(w_il, ws_il, "p (e q v) -> p q v e", ps_t, "turn")
+            for half in range(2):
+                bank = ps_t.tile([P, 2, 2, P], F32, name="turn")
+                for s in range(2):
+                    words = w_bf[:, 2 * half + s, :].bitcast(F32)
+                    for u in range(2):
+                        nc.tensor.transpose(bank[:, s, u, :], words[:, u : N // 2 : 2], ident[:])
+                nc.scalar.copy(ws_il[:, 2 * half : 2 * half + 2, :, :], bank[:].rearrange("p s u q -> p s q u"))
 
         def turn_h(g):
-            turn_words(h_il[g], hs_il[g], "p (e q v) -> p v q e", ps_a, "acc")
+            words = h_il[g][:].rearrange("p i t -> p (i t)").bitcast(F32)
+            for u in range(2):
+                bank = ps_a.tile([P, 4, P], F32, name="acc")
+                for e in range(4):
+                    nc.tensor.transpose(bank[:, e, :], words[:, 2 * e + u : 2 * N : 8], ident[:])
+                nc.scalar.copy(
+                    hs_il[g][:, u],
+                    bank[:].rearrange("p e q -> p (e q)").bitcast(BF16).rearrange("p (e q v) -> p v q e", e=4, v=2),
+                )
 
         def quantise_ws():
-            quantise(ws_q, whole, ws_il[:].rearrange("p u q v e -> p (u q v e)"), E4)
+            quantise(ws_q, whole, ws_il[:].rearrange("p j q u -> p (j q u)").bitcast(BF16), E4)
 
         def quantise_hs(g):
             quantise(hs_q[g], whole, hs_il[g][:].rearrange("p u v q e -> p (u v q e)"), E5)
 
-        nc.vector.tensor_copy(w_il[:, :, 3], w_planes[3][:].indirect(offsets[:]))
+        nc.vector.tensor_copy(w_bf[:, 3, :], w_planes[3][:].indirect(offsets[:]))
+        interleave(ve, w_il, w_bf, 0, 80)
+        interleave(sc, w_il, w_bf, 80, 128)
         quantise(w_q, whole, w_il[:].rearrange("p i j -> p (i j)"), E4)
         x_interleave(ve, 0, 0, 80)
         x_interleave(sc, 0, 80, 128)
@@ -262,8 +270,8 @@ def tile_attend_gsqh_wx_ts_kernel(tc, xT, wT, y, wt, ts, xm, offs, out_0, out_1)
                     acc = ps_a.tile([P, D], F32, name="acc")
                     mx(acc[:], hs_q[g], 2 * pair + k, E5, ws_q, E4, True, True)
                     nc.scalar.copy(
-                        gx[:, k, :].rearrange("p (q u e) -> p q u e", u=2, e=2),
-                        acc[:].rearrange("p (u q e) -> p q u e", u=2, e=2),
+                        gx[:, k, :].rearrange("p (q j) -> p q j", j=4),
+                        acc[:].rearrange("p (j q) -> p q j", j=4),
                     )
                 nc.scalar.dma_start(gx_view[g][:, 2 * pair : 2 * pair + 2, :], gx[:])
 

@@ -117,7 +117,7 @@ def tile_attend_gsqh_wx_ts_kernel(tc, xT, wT, y, wt, ts, xm, offs, out_0, out_1)
         w_bf = sb("w_bf", [P, 4, N], BF16)
         for j in range(3):
             nc.vector.tensor_copy(w_bf[:, j, :], w_planes[j][:].indirect(offsets[:]))
-        ts_all = sb("ts_all", [P, N], F32, "w_plane1")
+        ts_all = sb("ts_all", [P, N], F32)
         nc.vector.tensor_copy(ts_all[:], ts_table[:].indirect(offsets[:]))
 
         x_il = [sb(f"x_il{g}", [P, 4, P, 4], BF16) for g in range(G)]
@@ -130,10 +130,11 @@ def tile_attend_gsqh_wx_ts_kernel(tc, xT, wT, y, wt, ts, xm, offs, out_0, out_1)
         w_q = mx_tiles("w")
         sc, ve = nc.scalar.copy, nc.vector.tensor_copy
 
-        def x_interleave(copy, g, lo, hi):
+        def x_interleave(copy, g, pair, lo, hi):
+            tiles = slice(2 * pair, 2 * pair + 2)
             copy(
-                x_il[g][:].rearrange("p t m j -> p m j t")[:, lo:hi],
-                x_raw[g][:].rearrange("p j (m t) -> p m j t", t=4)[:, lo:hi],
+                x_il[g][:].rearrange("p t m j -> p m j t")[:, lo:hi, :, tiles],
+                x_raw[g][:].rearrange("p j (m t) -> p m j t", t=4)[:, lo:hi, :, tiles],
             )
 
         def interleave(copy, dst, src, lo, hi):
@@ -169,9 +170,9 @@ def tile_attend_gsqh_wx_ts_kernel(tc, xT, wT, y, wt, ts, xm, offs, out_0, out_1)
 
         def gradient(g):
             nc.vector.tensor_tensor(
-                h_il[g][:].rearrange("p (c i) t -> p c t i", i=4),
-                margin[g][:].rearrange("p t (c i) -> p c t i", i=4),
-                y_sb[g][:].rearrange("p t (c i) -> p c t i", i=4),
+                h_il[g][:].rearrange("p (c i) t -> p c t i", i=2),
+                margin[g][:].rearrange("p t (c i) -> p c t i", i=2),
+                y_sb[g][:].rearrange("p t (c i) -> p c t i", i=2),
                 MULT,
             )
 
@@ -217,8 +218,9 @@ def tile_attend_gsqh_wx_ts_kernel(tc, xT, wT, y, wt, ts, xm, offs, out_0, out_1)
         interleave(ve, w_il, w_bf, 0, 80)
         interleave(sc, w_il, w_bf, 80, 128)
         quantise(w_q, whole, w_il[:].rearrange("p i j -> p (i j)"), E4)
-        x_interleave(ve, 0, 0, 80)
-        x_interleave(sc, 0, 80, 128)
+        x_interleave(ve, 0, 0, 0, P)
+        x_interleave(sc, 0, 1, 32, P)
+        x_interleave(ve, 0, 1, 0, 32)
         quantise_x(0)
         factor(0, 0)
         factor(0, 1)
@@ -228,8 +230,8 @@ def tile_attend_gsqh_wx_ts_kernel(tc, xT, wT, y, wt, ts, xm, offs, out_0, out_1)
         factor(0, 3)
         front(0, 2)
         front(0, 3)
-        x_interleave(sc, 1, 0, 64)
-        x_interleave(sc, 1, 64, 128)
+        x_interleave(sc, 1, 0, 0, P)
+        x_interleave(sc, 1, 1, 0, P)
         factor(1, 0)
         factor(1, 1)
         gradient(0)

@@ -125,8 +125,8 @@ def tile_attend_gsqh_wx_ts_kernel(tc, xT, wT, y, wt, ts, xm, offs, out_0, out_1)
         h_il = [sb(f"h_il{g}", [P, N, 4], BF16) for g in range(G)]
         margin = [sb(f"margin{g}", [P, 4, N], F32) for g in range(G)]
         x_q = [mx_tiles("x0"), mx_tiles("x1")]
-        xm_q = [mx_tiles(f"xm{g}") for g in range(G)]
-        h_q = [mx_tiles(f"h{g}") for g in range(G)]
+        xm_q = [None] * G
+        h_q = [None] * G
         w_q = mx_tiles("w")
         sc, ve = nc.scalar.copy, nc.vector.tensor_copy
 
@@ -150,9 +150,11 @@ def tile_attend_gsqh_wx_ts_kernel(tc, xT, wT, y, wt, ts, xm, offs, out_0, out_1)
             quantise(x_q[g], whole, x_il[g][:].rearrange("p t m j -> p (t m j)"), E4)
 
         def quantise_xm(g):
+            xm_q[g] = mx_tiles(f"xm{g}", "z2" if g == 0 else None)
             quantise(xm_q[g], whole, xm_il[g][:].rearrange("p d t -> p (d t)"), E4)
 
         def quantise_h(g):
+            h_q[g] = mx_tiles(f"h{g}", "z1" if g == 0 else None)
             quantise(h_q[g], whole, h_il[g][:].rearrange("p i t -> p (i t)"), E5)
 
         def factor(g, t):
@@ -162,7 +164,7 @@ def tile_attend_gsqh_wx_ts_kernel(tc, xT, wT, y, wt, ts, xm, offs, out_0, out_1)
         def front(g, t):
             a = ps_a.tile([P, N], F32, name="acc")
             mx(a[:], x_q[g], t, E4, w_q, E4, True, True)
-            z = ring.tile([P, N], F32, name="z", bufs=3)
+            z = sb(f"z{t}", [P, N], F32) if g == 1 and t > 0 else ring.tile([P, N], F32, name="z", bufs=3)
             nc.vector.tensor_tensor(z[:], a[:], y_sb[g][:, t, :], MULT)
             nc.scalar.activation(
                 margin[g][:, t, :], z[:], RELU, bias=wt_abs[:, g, t : t + 1], scale=wt_sb[:, g, t : t + 1]
@@ -184,8 +186,7 @@ def tile_attend_gsqh_wx_ts_kernel(tc, xT, wT, y, wt, ts, xm, offs, out_0, out_1)
             mx(dw_ps[b][:], xm_q[g], b, E4, h_q[g], E5, g == 0, g == G - 1)
 
         ws_il = sb("ws_il", [P, 4, P, 2], F32, "x_raw0")
-        hs_il = [sb("hs_il0", [P, 2, 2, P, 4], BF16, "xm_raw1"), sb("hs_il1", [P, 2, 2, P, 4], BF16)]
-        ws_q = mx_tiles("ws")
+        hs_il = [None] * G
         hs_q = [mx_tiles(f"hs{g}") for g in range(G)]
 
         def turn_w():
@@ -198,6 +199,7 @@ def tile_attend_gsqh_wx_ts_kernel(tc, xT, wT, y, wt, ts, xm, offs, out_0, out_1)
                 nc.scalar.copy(ws_il[:, 2 * half : 2 * half + 2, :, :], bank[:].rearrange("p s u q -> p s q u"))
 
         def turn_h(g):
+            hs_il[g] = sb(f"hs_il{g}", [P, 2, 2, P, 4], BF16, "z3" if g == 0 else None)
             words = h_il[g][:].rearrange("p i t -> p (i t)").bitcast(F32)
             for u in range(2):
                 bank = ps_a.tile([P, 4, P], F32, name="acc")
@@ -209,7 +211,9 @@ def tile_attend_gsqh_wx_ts_kernel(tc, xT, wT, y, wt, ts, xm, offs, out_0, out_1)
                 )
 
         def quantise_ws():
+            ws_q = mx_tiles("ws", "xm_il1")
             quantise(ws_q, whole, ws_il[:].rearrange("p j q u -> p (j q u)").bitcast(BF16), E4)
+            return ws_q
 
         def quantise_hs(g):
             quantise(hs_q[g], whole, hs_il[g][:].rearrange("p u v q e -> p (u v q e)"), E5)
@@ -280,7 +284,7 @@ def tile_attend_gsqh_wx_ts_kernel(tc, xT, wT, y, wt, ts, xm, offs, out_0, out_1)
         turn_w()
         turn_h(0)
         finish_dw(0)
-        quantise_ws()
+        ws_q = quantise_ws()
         quantise_hs(0)
         scatter(0)
         rows_out(0)

@@ -64,7 +64,8 @@ def tile_attend_gsqh_wx_ts_kernel(tc, xT, wT, y, wt, ts, xm, offs, out_0, out_1)
         w_planes = [sb(f"w_plane{j}", [P, T], F32) for j in range(4)]
         x_raw = [sb(f"x_raw{g}", [P, 4, 512], F32) for g in range(G)]
         y_sb = [sb(f"y_sb{g}", [P, 4, N], F32) for g in range(G)]
-        xm_raw = [sb(f"xm_raw{g}", [P, 4, D], F32) for g in range(G)]
+        xm_raw = [sb("xm_raw0", [P, 4, D], F32), sb("xm_raw1", [P, 4, D - P], F32)]
+        xm_first = sb("xm_first", [P, 4, P], F32)
         wt_sb = sb("wt_sb", [P, G, 4], F32)
         ts_rows = sb("ts_rows", [P, P], F32)
         ts_table = sb("ts_table", [P, T], F32)
@@ -89,7 +90,8 @@ def tile_attend_gsqh_wx_ts_kernel(tc, xT, wT, y, wt, ts, xm, offs, out_0, out_1)
         nc.sync.dma_start(x_raw[1][:], x_view[1])
         nc.sync.dma_start(y_sb[1][:, 2:4, :], y_view[1][:, 2:4, :])
         nc.sync.dma_start(xm_raw[0][:], xm_view[0])
-        nc.sync.dma_start(xm_raw[1][:], xm_view[1])
+        nc.sync.dma_start(xm_first[:], xm_view[1][:, :, 0:P])
+        nc.sync.dma_start(xm_raw[1][:], xm_view[1][:, :, P:D])
 
         make_identity(nc, ident[:])
         windows = [sb(f"window{b}", [P, T], F32) for b in range(3)]
@@ -114,14 +116,15 @@ def tile_attend_gsqh_wx_ts_kernel(tc, xT, wT, y, wt, ts, xm, offs, out_0, out_1)
                 nc.tensor.transpose(bank[:, s, :], ts_col[:, k : k + 1].to_broadcast([P, P]), ident[:])
             nc.scalar.copy(ts_table[:, quarter * 512 : (quarter + 1) * 512], bank[:].rearrange("p s k -> p (s k)"))
         w_il = sb("w_il", [P, N, 4], BF16)
-        w_bf = sb("w_bf", [P, 4, N], BF16)
+        w_flat = sb("w_bf", [P, 4 * N], BF16)
+        w_bf = w_flat[:].rearrange("p (j i) -> p j i", j=4)
         for j in range(3):
             nc.vector.tensor_copy(w_bf[:, j, :], w_planes[j][:].indirect(offsets[:]))
         ts_all = sb("ts_all", [P, N], F32)
         nc.vector.tensor_copy(ts_all[:], ts_table[:].indirect(offsets[:]))
 
         x_il = [sb(f"x_il{g}", [P, 4, P, 4], BF16) for g in range(G)]
-        xm_il = [sb(f"xm_il{g}", [P, D, 4], BF16) for g in range(G)]
+        xm_il = [None] * G
         h_il = [sb(f"h_il{g}", [P, N, 4], BF16) for g in range(G)]
         margin = [sb(f"margin{g}", [P, 4, N], F32) for g in range(G)]
         x_q = [mx_tiles("x0"), mx_tiles("x1")]
@@ -143,15 +146,19 @@ def tile_attend_gsqh_wx_ts_kernel(tc, xT, wT, y, wt, ts, xm, offs, out_0, out_1)
                 src[:].rearrange("p t (c i) -> p c t i", i=4)[:, lo:hi],
             )
 
-        def xm_interleave(copy, g, half):
-            interleave(copy, xm_il[g], xm_raw[g], half * 64, (half + 1) * 64)
+        def xm_interleave(g, b):
+            if g == 0:
+                interleave(sc, xm_il[0], xm_raw[0], 32 * b, 32 * (b + 1))
+            elif b == 0:
+                interleave(sc, xm_il[1][:, 0:P, :], xm_first, 0, 32)
+            else:
+                interleave(sc, xm_il[1][:, P:D, :], xm_raw[1], 32 * (b - 1), 32 * b)
 
         def quantise_x(g):
             quantise(x_q[g], whole, x_il[g][:].rearrange("p t m j -> p (t m j)"), E4)
 
-        def quantise_xm(g):
-            xm_q[g] = mx_tiles(f"xm{g}", "z2" if g == 0 else None)
-            quantise(xm_q[g], whole, xm_il[g][:].rearrange("p d t -> p (d t)"), E4)
+        def quantise_xm(g, lo, hi):
+            quantise(xm_q[g], slice(lo, hi), xm_il[g][:, lo:hi, :].rearrange("p d t -> p (d t)"), E4)
 
         def quantise_h(g):
             h_q[g] = mx_tiles(f"h{g}", "z1" if g == 0 else None)
@@ -199,10 +206,13 @@ def tile_attend_gsqh_wx_ts_kernel(tc, xT, wT, y, wt, ts, xm, offs, out_0, out_1)
                 nc.scalar.copy(ws_il[:, 2 * half : 2 * half + 2, :, :], bank[:].rearrange("p s u q -> p s q u"))
 
         def turn_h(g):
-            hs_il[g] = sb(f"hs_il{g}", [P, 2, 2, P, 4], BF16, "z3" if g == 0 else None)
+            hs_il[g] = sb(f"hs_il{g}", [P, 2, 2, P, 4], BF16, "xm_first" if g == 0 else None)
             words = h_il[g][:].rearrange("p i t -> p (i t)").bitcast(F32)
             for u in range(2):
-                bank = ps_a.tile([P, 4, P], F32, name="acc")
+                if (g, u) == (1, 0):
+                    bank = ps_w.tile([P, 4, P], F32, name="turn_h", tag="dw_bank0")
+                else:
+                    bank = ps_a.tile([P, 4, P], F32, name="acc")
                 for e in range(4):
                     nc.tensor.transpose(bank[:, e, :], words[:, 2 * e + u : 2 * N : 8], ident[:])
                 nc.scalar.copy(
@@ -211,21 +221,27 @@ def tile_attend_gsqh_wx_ts_kernel(tc, xT, wT, y, wt, ts, xm, offs, out_0, out_1)
                 )
 
         def quantise_ws():
-            ws_q = mx_tiles("ws", "xm_il1")
+            ws_q = mx_tiles("ws", "margin1")
             quantise(ws_q, whole, ws_il[:].rearrange("p j q u -> p (j q u)").bitcast(BF16), E4)
             return ws_q
 
         def quantise_hs(g):
             quantise(hs_q[g], whole, hs_il[g][:].rearrange("p u v q e -> p (u v q e)"), E5)
 
-        nc.vector.tensor_copy(w_bf[:, 3, :], w_planes[3][:].indirect(offsets[:]))
-        interleave(ve, w_il, w_bf, 0, 80)
-        interleave(sc, w_il, w_bf, 80, 128)
-        quantise(w_q, whole, w_il[:].rearrange("p i j -> p (i j)"), E4)
+        for lo, hi in ((0, 256), (256, 384), (384, 512)):
+            nc.vector.tensor_copy(w_bf[:, 3, lo:hi], w_planes[3][:].indirect(offsets[:, lo // 16 : hi // 16]))
+        interleave(sc, w_il, w_bf, 0, 64)
+        interleave(ve, w_il, w_bf, 64, 96)
+        interleave(ve, w_il, w_bf, 96, 128)
+        for half in range(2):
+            slots = slice(half * 256, (half + 1) * 256)
+            quantise(w_q, slots, w_il[:, slots, :].rearrange("p i j -> p (i j)"), E4)
         x_interleave(ve, 0, 0, 0, P)
         x_interleave(sc, 0, 1, 32, P)
         x_interleave(ve, 0, 1, 0, 32)
-        quantise_x(0)
+        for pair in range(2):
+            tiles = x_il[0][:, 2 * pair : 2 * pair + 2]
+            quantise(x_q[0], slice(pair * 256, (pair + 1) * 256), tiles.rearrange("p t m j -> p (t m j)"), E4)
         factor(0, 0)
         factor(0, 1)
         front(0, 0)
@@ -242,18 +258,21 @@ def tile_attend_gsqh_wx_ts_kernel(tc, xT, wT, y, wt, ts, xm, offs, out_0, out_1)
         quantise_x(1)
         factor(1, 2)
         factor(1, 3)
-        xm_interleave(sc, 0, 0)
-        xm_interleave(sc, 0, 1)
+        xm_il[0] = sb("xm_il0", [P, D, 4], BF16)
+        for b in range(4):
+            xm_interleave(0, b)
         for t in range(4):
             front(1, t)
-        xm_interleave(sc, 1, 0)
-        xm_interleave(sc, 1, 1)
+        xm_il[1] = sb("xm_il1", [P, D, 4], BF16, "z3")
+        xm_interleave(1, 0)
         quantise_h(0)
-        quantise_xm(0)
+        xm_q[0] = mx_tiles("xm0", "z2")
+        quantise_xm(0, 0, D)
         for b in range(2):
             dw_pass(0, b)
         gradient(1)
-        quantise_xm(1)
+        xm_q[1] = mx_tiles("xm1")
+        quantise_xm(1, 0, P)
         quantise_h(1)
 
         dw_sb = [None] * 4
@@ -269,31 +288,37 @@ def tile_attend_gsqh_wx_ts_kernel(tc, xT, wT, y, wt, ts, xm, offs, out_0, out_1)
             nc.vector.tensor_copy(windows[b % 3][:].indirect(offsets[:]), dw_sb[b][:])
             nc.sync.dma_start(out_0[block(b), :], windows[b % 3][:])
 
-        def rows_out(g):
-            for pair in range(2):
-                gx = ring.tile([P, 2, D], F32, name="gx", bufs=4)
-                for k in range(2):
-                    acc = ps_a.tile([P, D], F32, name="acc")
-                    mx(acc[:], hs_q[g], 2 * pair + k, E5, ws_q, E4, True, True)
-                    nc.scalar.copy(
-                        gx[:, k, :].rearrange("p (q j) -> p q j", j=4),
-                        acc[:].rearrange("p (j q) -> p q j", j=4),
-                    )
-                nc.scalar.dma_start(gx_view[g][:, 2 * pair : 2 * pair + 2, :], gx[:])
+        def rows_out(g, pair):
+            gx = ring.tile([P, 2, D], F32, name="gx", bufs=4)
+            for k in range(2):
+                acc = ps_a.tile([P, D], F32, name="acc")
+                mx(acc[:], hs_q[g], 2 * pair + k, E5, ws_q, E4, True, True)
+                nc.scalar.copy(
+                    gx[:, k, :].rearrange("p (q j) -> p q j", j=4),
+                    acc[:].rearrange("p (j q) -> p q j", j=4),
+                )
+            nc.scalar.dma_start(gx_view[g][:, 2 * pair : 2 * pair + 2, :], gx[:])
 
         turn_w()
         turn_h(0)
         finish_dw(0)
-        ws_q = quantise_ws()
         quantise_hs(0)
+        ws_q = quantise_ws()
+        xm_interleave(1, 1)
+        quantise_xm(1, P, 2 * P)
         scatter(0)
-        rows_out(0)
+        rows_out(0, 0)
         finish_dw(1)
+        xm_interleave(1, 2)
+        xm_interleave(1, 3)
+        quantise_xm(1, 2 * P, D)
+        rows_out(0, 1)
         scatter(1)
         turn_h(1)
         quantise_hs(1)
         finish_dw(2)
         scatter(2)
         finish_dw(3)
-        rows_out(1)
+        rows_out(1, 0)
+        rows_out(1, 1)
         scatter(3)

@@ -21,7 +21,12 @@ ABS = mybir.ActivationFunctionType.Abs
 RELU = mybir.ActivationFunctionType.Relu
 
 P = 128
-G = R // 512
+PASS = 512
+G = R // PASS
+HALF = PASS // 2
+WINDOWS = 3
+LIST_ROWS = 16
+X_SPLIT = 32
 
 
 def tile_attend_gsqh_wx_ts_kernel(tc, xT, wT, y, wt, ts, xm, offs, out_0, out_1):
@@ -29,18 +34,21 @@ def tile_attend_gsqh_wx_ts_kernel(tc, xT, wT, y, wt, ts, xm, offs, out_0, out_1)
     with ExitStack() as ctx:
         keep = ctx.enter_context(tc.tile_pool(name="keep", bufs=1))
         ring = ctx.enter_context(tc.tile_pool(name="ring", bufs=3))
-        ps_a = ctx.enter_context(tc.psum_pool(name="ps_a", bufs=4))
-        ps_t = ctx.enter_context(tc.psum_pool(name="ps_t", bufs=2))
-        ps_w = ctx.enter_context(tc.psum_pool(name="ps_w", bufs=1))
+        ps_lone = ctx.enter_context(tc.psum_pool(name="ps_lone", bufs=4))
+        ps_turn = ctx.enter_context(tc.psum_pool(name="ps_turn", bufs=2))
+        ps_dw = ctx.enter_context(tc.psum_pool(name="ps_dw", bufs=1))
 
         def sb(name, shape, dtype, tag=None):
             return keep.tile(shape, dtype, name=name, tag=tag or name, align_bytes=64)
 
         def mx_tiles(name, tag=None):
-            return sb(name + "_codes", [P, 512], U32, tag), sb(name + "_scales", [P, 512], U8)
+            return sb(name + "_codes", [P, PASS], U32, tag), sb(name + "_scales", [P, PASS], U8)
 
         def quantise(dst, cols, src, fmt):
             nc.vector.quantize_mx(out=dst[0][:, cols].bitcast(fmt), scales=dst[1][:, cols], in_=src)
+
+        def block(k):
+            return slice(k * P, (k + 1) * P)
 
         def mx(out, lhs, k, lhs_fmt, rhs, rhs_fmt, start, stop):
             nc.tensor.matmul_mx(
@@ -53,21 +61,16 @@ def tile_attend_gsqh_wx_ts_kernel(tc, xT, wT, y, wt, ts, xm, offs, out_0, out_1)
                 stop=stop,
             )
 
-        def block(k):
-            return slice(k * P, (k + 1) * P)
+        whole = slice(0, PASS)
 
-        whole = slice(0, 512)
-
-        offsets = keep.tile([P, N // 16], U16, name="offsets")
-        nc.sync.dma_start(offsets[:], offs)
-
+        offsets = keep.tile([P, N // LIST_ROWS], U16, name="offsets")
         w_planes = [sb(f"w_plane{j}", [P, T], F32) for j in range(4)]
-        x_raw = [sb(f"x_raw{g}", [P, 4, 512], F32) for g in range(G)]
+        x_raw = [sb(f"x_raw{g}", [P, 4, PASS], F32) for g in range(G)]
         y_sb = [sb(f"y_sb{g}", [P, 4, N], F32) for g in range(G)]
         xm_raw = [sb("xm_raw0", [P, 4, D], F32), sb("xm_raw1", [P, 4, D - P], F32)]
         xm_first = sb("xm_first", [P, 4, P], F32)
         wt_sb = sb("wt_sb", [P, G, 4], F32)
-        ts_rows = sb("ts_rows", [P, P], F32)
+        ts_runs = sb("ts_runs", [P, T // P], F32)
         ts_table = sb("ts_table", [P, T], F32)
         ident = sb("ident", [P, P], F32)
 
@@ -77,12 +80,12 @@ def tile_attend_gsqh_wx_ts_kernel(tc, xT, wT, y, wt, ts, xm, offs, out_0, out_1)
         xm_view = xm[0].rearrange("(g p t) d -> g p t d", g=G, t=4)
         gx_view = out_1[0].rearrange("(g p t) d -> g p t d", g=G, t=4)
 
-        nc.sync.dma_start(ts_rows[:], ts[0 : P * P // T, :].rearrange("r (c k) -> (r c) k", k=P))
+        nc.sync.dma_start(ts_runs[:], ts[0].rearrange("(n e) -> n e", n=P))
         nc.scalar.dma_start(wt_sb[:], wt[0].rearrange("(g p t) o -> p g (t o)", g=G, t=4))
         nc.sync.dma_start(w_planes[0][:], w_view[0])
-        nc.sync.dma_start(w_planes[1][:], w_view[1])
-        nc.sync.dma_start(w_planes[2][:], w_view[2])
-        nc.sync.dma_start(w_planes[3][:], w_view[3])
+        nc.sync.dma_start(offsets[:], offs)
+        for j in range(1, 4):
+            nc.sync.dma_start(w_planes[j][:], w_view[j])
         nc.sync.dma_start(x_raw[0][:], x_view[0])
         nc.sync.dma_start(y_sb[0][:, 0:2, :], y_view[0][:, 0:2, :])
         nc.sync.dma_start(y_sb[0][:, 2:4, :], y_view[0][:, 2:4, :])
@@ -94,7 +97,7 @@ def tile_attend_gsqh_wx_ts_kernel(tc, xT, wT, y, wt, ts, xm, offs, out_0, out_1)
         nc.sync.dma_start(xm_raw[1][:], xm_view[1][:, :, P:D])
 
         make_identity(nc, ident[:])
-        windows = [sb(f"window{b}", [P, T], F32) for b in range(3)]
+        windows = [sb(f"window{b}", [P, T], F32) for b in range(WINDOWS)]
         for window in windows:
             nc.vector.memset(window[:].bitcast(I32), 0)
 
@@ -105,16 +108,14 @@ def tile_attend_gsqh_wx_ts_kernel(tc, xT, wT, y, wt, ts, xm, offs, out_0, out_1)
         nc.scalar.activation(wt_abs[:], wt_sb[:], ABS)
         nc.vector.tensor_scalar(minus_sign[:], wt_step[:], 1.0, None, ADD)
 
-        bank = ps_t.tile([P, P], F32, name="turn")
-        nc.tensor.transpose(bank[:], ts_rows[:], ident[:])
-        ts_col = sb("ts_col", [P, T // P], F32)
-        nc.scalar.copy(ts_col[:], bank[:, 0 : T // P])
-        for quarter in range(4):
-            bank = ps_t.tile([P, 4, P], F32, name="turn")
-            for s in range(4):
-                k = 4 * quarter + s
-                nc.tensor.transpose(bank[:, s, :], ts_col[:, k : k + 1].to_broadcast([P, P]), ident[:])
-            nc.scalar.copy(ts_table[:, quarter * 512 : (quarter + 1) * 512], bank[:].rearrange("p s k -> p (s k)"))
+        table_view = ts_table[:].rearrange("p (n k e) -> p k n e", k=4, e=4)
+        for k in range(4):
+            bank = ps_turn.tile([P, 4, P], F32, name="turn")
+            for e in range(4):
+                column = ts_runs[:, 4 * k + e : 4 * k + e + 1]
+                nc.tensor.transpose(bank[:, e, :], column.to_broadcast([P, P]), ident[:])
+            nc.scalar.copy(table_view[:, k], bank[:].rearrange("p e n -> p n e"))
+
         w_il = sb("w_il", [P, N, 4], BF16)
         w_flat = sb("w_bf", [P, 4 * N], BF16)
         w_bf = w_flat[:].rearrange("p (j i) -> p j i", j=4)
@@ -127,11 +128,11 @@ def tile_attend_gsqh_wx_ts_kernel(tc, xT, wT, y, wt, ts, xm, offs, out_0, out_1)
         xm_il = [None] * G
         h_il = [sb(f"h_il{g}", [P, N, 4], BF16) for g in range(G)]
         margin = [sb(f"margin{g}", [P, 4, N], F32) for g in range(G)]
-        x_q = [mx_tiles("x0"), mx_tiles("x1")]
+        x_q = [mx_tiles(f"x{g}") for g in range(G)]
         xm_q = [None] * G
         h_q = [None] * G
         w_q = mx_tiles("w")
-        sc, ve = nc.scalar.copy, nc.vector.tensor_copy
+        on_scalar, on_vector = nc.scalar.copy, nc.vector.tensor_copy
 
         def x_interleave(copy, g, pair, lo, hi):
             tiles = slice(2 * pair, 2 * pair + 2)
@@ -142,37 +143,34 @@ def tile_attend_gsqh_wx_ts_kernel(tc, xT, wT, y, wt, ts, xm, offs, out_0, out_1)
 
         def interleave(copy, dst, src, lo, hi):
             copy(
-                dst[:].rearrange("p (c i) t -> p c t i", i=4)[:, lo:hi],
-                src[:].rearrange("p t (c i) -> p c t i", i=4)[:, lo:hi],
+                dst[:].rearrange("p (c i) t -> p c t i", i=4)[:, lo // 4 : hi // 4],
+                src[:].rearrange("p t (c i) -> p c t i", i=4)[:, lo // 4 : hi // 4],
             )
 
         def xm_interleave(g, b):
             if g == 0:
-                interleave(sc, xm_il[0], xm_raw[0], 32 * b, 32 * (b + 1))
+                interleave(on_scalar, xm_il[0], xm_raw[0], P * b, P * (b + 1))
             elif b == 0:
-                interleave(sc, xm_il[1][:, 0:P, :], xm_first, 0, 32)
+                interleave(on_scalar, xm_il[1][:, 0:P, :], xm_first, 0, P)
             else:
-                interleave(sc, xm_il[1][:, P:D, :], xm_raw[1], 32 * (b - 1), 32 * b)
-
-        def quantise_x(g):
-            quantise(x_q[g], whole, x_il[g][:].rearrange("p t m j -> p (t m j)"), E4)
+                interleave(on_scalar, xm_il[1][:, P:D, :], xm_raw[1], P * (b - 1), P * b)
 
         def quantise_xm(g, lo, hi):
             quantise(xm_q[g], slice(lo, hi), xm_il[g][:, lo:hi, :].rearrange("p d t -> p (d t)"), E4)
 
-        def quantise_h(g):
-            h_q[g] = mx_tiles(f"h{g}", "z1" if g == 0 else None)
+        def quantise_h(g, tag=None):
+            h_q[g] = mx_tiles(f"h{g}", tag)
             quantise(h_q[g], whole, h_il[g][:].rearrange("p i t -> p (i t)"), E5)
 
         def factor(g, t):
             c = y_sb[g][:, t, :]
             nc.vector.scalar_tensor_tensor(c, c, minus_sign[:, g, t : t + 1], ts_all[:], MULT, MULT)
 
-        def front(g, t):
-            a = ps_a.tile([P, N], F32, name="acc")
-            mx(a[:], x_q[g], t, E4, w_q, E4, True, True)
+        def scores(g, t):
+            sums = ps_lone.tile([P, N], F32, name="lone")
+            mx(sums[:], x_q[g], t, E4, w_q, E4, True, True)
             z = sb(f"z{t}", [P, N], F32) if g == 1 and t > 0 else ring.tile([P, N], F32, name="z", bufs=3)
-            nc.vector.tensor_tensor(z[:], a[:], y_sb[g][:, t, :], MULT)
+            nc.vector.tensor_tensor(z[:], sums[:], y_sb[g][:, t, :], MULT)
             nc.scalar.activation(
                 margin[g][:, t, :], z[:], RELU, bias=wt_abs[:, g, t : t + 1], scale=wt_sb[:, g, t : t + 1]
             )
@@ -189,7 +187,7 @@ def tile_attend_gsqh_wx_ts_kernel(tc, xT, wT, y, wt, ts, xm, offs, out_0, out_1)
 
         def dw_pass(g, b):
             if g == 0:
-                dw_ps[b] = ps_w.tile([P, N], F32, name=f"dw_ps{b}", tag=f"dw_bank{b % 2}")
+                dw_ps[b] = ps_dw.tile([P, N], F32, name=f"dw_ps{b}", tag=f"dw_bank{b % 2}")
             mx(dw_ps[b][:], xm_q[g], b, E4, h_q[g], E5, g == 0, g == G - 1)
 
         ws_il = sb("ws_il", [P, 4, P, 2], F32, "x_raw0")
@@ -198,21 +196,21 @@ def tile_attend_gsqh_wx_ts_kernel(tc, xT, wT, y, wt, ts, xm, offs, out_0, out_1)
 
         def turn_w():
             for half in range(2):
-                bank = ps_t.tile([P, 2, 2, P], F32, name="turn")
+                bank = ps_turn.tile([P, 2, 2, P], F32, name="turn")
                 for s in range(2):
                     words = w_bf[:, 2 * half + s, :].bitcast(F32)
                     for u in range(2):
                         nc.tensor.transpose(bank[:, s, u, :], words[:, u : N // 2 : 2], ident[:])
                 nc.scalar.copy(ws_il[:, 2 * half : 2 * half + 2, :, :], bank[:].rearrange("p s u q -> p s q u"))
 
-        def turn_h(g):
-            hs_il[g] = sb(f"hs_il{g}", [P, 2, 2, P, 4], BF16, "xm_first" if g == 0 else None)
+        def turn_h(g, tag=None):
+            hs_il[g] = sb(f"hs_il{g}", [P, 2, 2, P, 4], BF16, tag)
             words = h_il[g][:].rearrange("p i t -> p (i t)").bitcast(F32)
             for u in range(2):
-                if (g, u) == (1, 0):
-                    bank = ps_w.tile([P, 4, P], F32, name="turn_h", tag="dw_bank0")
+                if (g, u) == (G - 1, 0):
+                    bank = ps_dw.tile([P, 4, P], F32, name="turn_h", tag="dw_bank0")
                 else:
-                    bank = ps_a.tile([P, 4, P], F32, name="acc")
+                    bank = ps_lone.tile([P, 4, P], F32, name="lone")
                 for e in range(4):
                     nc.tensor.transpose(bank[:, e, :], words[:, 2 * e + u : 2 * N : 8], ident[:])
                 nc.scalar.copy(
@@ -220,52 +218,47 @@ def tile_attend_gsqh_wx_ts_kernel(tc, xT, wT, y, wt, ts, xm, offs, out_0, out_1)
                     bank[:].rearrange("p e q -> p (e q)").bitcast(BF16).rearrange("p (e q v) -> p v q e", e=4, v=2),
                 )
 
-        def quantise_ws():
-            ws_q = mx_tiles("ws", "margin1")
-            quantise(ws_q, whole, ws_il[:].rearrange("p j q u -> p (j q u)").bitcast(BF16), E4)
-            return ws_q
-
         def quantise_hs(g):
             quantise(hs_q[g], whole, hs_il[g][:].rearrange("p u v q e -> p (u v q e)"), E5)
 
-        for lo, hi in ((0, 256), (256, 384), (384, 512)):
-            nc.vector.tensor_copy(w_bf[:, 3, lo:hi], w_planes[3][:].indirect(offsets[:, lo // 16 : hi // 16]))
-        interleave(sc, w_il, w_bf, 0, 64)
-        interleave(ve, w_il, w_bf, 64, 96)
-        interleave(ve, w_il, w_bf, 96, 128)
+        slices = ((0, HALF), (HALF, HALF + P), (HALF + P, N))
+        for lo, hi in slices:
+            part = offsets[:, lo // LIST_ROWS : hi // LIST_ROWS]
+            nc.vector.tensor_copy(w_bf[:, 3, lo:hi], w_planes[3][:].indirect(part))
+        for copy, (lo, hi) in zip((on_scalar, on_vector, on_vector), slices):
+            interleave(copy, w_il, w_bf, lo, hi)
         for half in range(2):
-            slots = slice(half * 256, (half + 1) * 256)
+            slots = slice(half * HALF, (half + 1) * HALF)
             quantise(w_q, slots, w_il[:, slots, :].rearrange("p i j -> p (i j)"), E4)
-        x_interleave(ve, 0, 0, 0, P)
-        x_interleave(sc, 0, 1, 32, P)
-        x_interleave(ve, 0, 1, 0, 32)
+        x_interleave(on_vector, 0, 0, 0, P)
+        x_interleave(on_scalar, 0, 1, X_SPLIT, P)
+        x_interleave(on_vector, 0, 1, 0, X_SPLIT)
         for pair in range(2):
             tiles = x_il[0][:, 2 * pair : 2 * pair + 2]
-            quantise(x_q[0], slice(pair * 256, (pair + 1) * 256), tiles.rearrange("p t m j -> p (t m j)"), E4)
-        factor(0, 0)
-        factor(0, 1)
-        front(0, 0)
-        front(0, 1)
-        factor(0, 2)
-        factor(0, 3)
-        front(0, 2)
-        front(0, 3)
-        x_interleave(sc, 1, 0, 0, P)
-        x_interleave(sc, 1, 1, 0, P)
+            quantise(x_q[0], slice(pair * HALF, (pair + 1) * HALF), tiles.rearrange("p t m j -> p (t m j)"), E4)
+
+        for pair in range(2):
+            for t in (2 * pair, 2 * pair + 1):
+                factor(0, t)
+            for t in (2 * pair, 2 * pair + 1):
+                scores(0, t)
+        for pair in range(2):
+            x_interleave(on_scalar, 1, pair, 0, P)
         factor(1, 0)
         factor(1, 1)
         gradient(0)
-        quantise_x(1)
+
+        quantise(x_q[1], whole, x_il[1][:].rearrange("p t m j -> p (t m j)"), E4)
         factor(1, 2)
         factor(1, 3)
         xm_il[0] = sb("xm_il0", [P, D, 4], BF16)
         for b in range(4):
             xm_interleave(0, b)
         for t in range(4):
-            front(1, t)
+            scores(1, t)
         xm_il[1] = sb("xm_il1", [P, D, 4], BF16, "z3")
         xm_interleave(1, 0)
-        quantise_h(0)
+        quantise_h(0, "z1")
         xm_q[0] = mx_tiles("xm0", "z2")
         quantise_xm(0, 0, D)
         for b in range(2):
@@ -277,33 +270,34 @@ def tile_attend_gsqh_wx_ts_kernel(tc, xT, wT, y, wt, ts, xm, offs, out_0, out_1)
 
         dw_sb = [None] * 4
 
-        def finish_dw(b, tag=None):
+        def finish_dw(b):
             if b >= 2:
                 dw_pass(0, b)
             dw_pass(1, b)
-            dw_sb[b] = sb(f"dw_sb{b}", [P, N], F32, tag)
+            dw_sb[b] = sb(f"dw_sb{b}", [P, N], F32)
             nc.scalar.copy(dw_sb[b][:], dw_ps[b][:])
 
         def scatter(b):
-            nc.vector.tensor_copy(windows[b % 3][:].indirect(offsets[:]), dw_sb[b][:])
-            nc.sync.dma_start(out_0[block(b), :], windows[b % 3][:])
+            nc.vector.tensor_copy(windows[b % WINDOWS][:].indirect(offsets[:]), dw_sb[b][:])
+            nc.sync.dma_start(out_0[block(b), :], windows[b % WINDOWS][:])
 
         def rows_out(g, pair):
-            gx = ring.tile([P, 2, D], F32, name="gx", bufs=4)
+            gx = ring.tile([P, 2, D], F32, name="gx", bufs=2 * G)
             for k in range(2):
-                acc = ps_a.tile([P, D], F32, name="acc")
-                mx(acc[:], hs_q[g], 2 * pair + k, E5, ws_q, E4, True, True)
+                sums = ps_lone.tile([P, D], F32, name="lone")
+                mx(sums[:], hs_q[g], 2 * pair + k, E5, ws_q, E4, True, True)
                 nc.scalar.copy(
                     gx[:, k, :].rearrange("p (q j) -> p q j", j=4),
-                    acc[:].rearrange("p (j q) -> p q j", j=4),
+                    sums[:].rearrange("p (j q) -> p q j", j=4),
                 )
             nc.scalar.dma_start(gx_view[g][:, 2 * pair : 2 * pair + 2, :], gx[:])
 
         turn_w()
-        turn_h(0)
+        turn_h(0, "xm_first")
         finish_dw(0)
         quantise_hs(0)
-        ws_q = quantise_ws()
+        ws_q = mx_tiles("ws", "margin1")
+        quantise(ws_q, whole, ws_il[:].rearrange("p j q u -> p (j q u)").bitcast(BF16), E4)
         xm_interleave(1, 1)
         quantise_xm(1, P, 2 * P)
         scatter(0)

@@ -41,8 +41,8 @@ def tile_attend_gsqh_wx_ts_kernel(tc, xT, wT, y, wt, ts, xm, offs, out_0, out_1)
         def sb(name, shape, dtype, tag=None):
             return keep.tile(shape, dtype, name=name, tag=tag or name, align_bytes=64)
 
-        def mx_tiles(name, tag=None):
-            return sb(name + "_codes", [P, PASS], U32, tag), sb(name + "_scales", [P, PASS], U8)
+        def mx_tiles(name, tag=None, width=PASS):
+            return sb(name + "_codes", [P, width], U32, tag), sb(name + "_scales", [P, width], U8)
 
         def quantise(dst, cols, src, fmt):
             nc.vector.quantize_mx(out=dst[0][:, cols].bitcast(fmt), scales=dst[1][:, cols], in_=src)
@@ -67,8 +67,7 @@ def tile_attend_gsqh_wx_ts_kernel(tc, xT, wT, y, wt, ts, xm, offs, out_0, out_1)
         w_planes = [sb(f"w_plane{j}", [P, T], F32) for j in range(4)]
         x_raw = [sb(f"x_raw{g}", [P, 4, PASS], F32) for g in range(G)]
         y_sb = [sb(f"y_sb{g}", [P, 4, N], F32) for g in range(G)]
-        xm_raw = [sb("xm_raw0", [P, 4, D], F32), sb("xm_raw1", [P, 4, D - P], F32)]
-        xm_first = sb("xm_first", [P, 4, P], F32)
+        xm_raw = [[sb(f"xm_raw{g}_{half}", [P, 4, HALF], F32) for half in range(2)] for g in range(G)]
         wt_sb = sb("wt_sb", [P, G, 4], F32)
         ts_runs = sb("ts_runs", [P, T // P], F32)
         ts_table = sb("ts_table", [P, T], F32)
@@ -92,9 +91,8 @@ def tile_attend_gsqh_wx_ts_kernel(tc, xT, wT, y, wt, ts, xm, offs, out_0, out_1)
         nc.sync.dma_start(y_sb[1][:, 0:2, :], y_view[1][:, 0:2, :])
         nc.sync.dma_start(x_raw[1][:], x_view[1])
         nc.sync.dma_start(y_sb[1][:, 2:4, :], y_view[1][:, 2:4, :])
-        nc.sync.dma_start(xm_raw[0][:], xm_view[0])
-        nc.sync.dma_start(xm_first[:], xm_view[1][:, :, 0:P])
-        nc.sync.dma_start(xm_raw[1][:], xm_view[1][:, :, P:D])
+        for g, half in ((0, 0), (0, 1), (1, 1), (1, 0)):
+            nc.sync.dma_start(xm_raw[g][half][:], xm_view[g][:, :, half * HALF : (half + 1) * HALF])
 
         make_identity(nc, ident[:])
         windows = [sb(f"window{b}", [P, T], F32) for b in range(WINDOWS)]
@@ -125,11 +123,11 @@ def tile_attend_gsqh_wx_ts_kernel(tc, xT, wT, y, wt, ts, xm, offs, out_0, out_1)
         nc.vector.tensor_copy(ts_all[:], ts_table[:].indirect(offsets[:]))
 
         x_il = [sb(f"x_il{g}", [P, 4, P, 4], BF16) for g in range(G)]
-        xm_il = [None] * G
+        xm_il = [[None, None] for g in range(G)]
         h_il = [sb(f"h_il{g}", [P, N, 4], BF16) for g in range(G)]
         margin = [sb(f"margin{g}", [P, 4, N], F32) for g in range(G)]
         x_q = [mx_tiles(f"x{g}") for g in range(G)]
-        xm_q = [None] * G
+        xm_q = [[None, None] for g in range(G)]
         h_q = [None] * G
         w_q = mx_tiles("w")
         on_scalar, on_vector = nc.scalar.copy, nc.vector.tensor_copy
@@ -148,15 +146,16 @@ def tile_attend_gsqh_wx_ts_kernel(tc, xT, wT, y, wt, ts, xm, offs, out_0, out_1)
             )
 
         def xm_interleave(g, b):
-            if g == 0:
-                interleave(on_scalar, xm_il[0], xm_raw[0], P * b, P * (b + 1))
-            elif b == 0:
-                interleave(on_scalar, xm_il[1][:, 0:P, :], xm_first, 0, P)
+            half, k = divmod(b, 2)
+            if (g, half) != (1, 1):
+                interleave(on_scalar, xm_il[g][half], xm_raw[g][half], P * k, P * (k + 1))
             else:
-                interleave(on_scalar, xm_il[1][:, P:D, :], xm_raw[1], P * (b - 1), P * b)
+                source = xm_raw[g][half][:, :, block(k)].rearrange("p t d -> p d t")
+                nc.gpsimd.tensor_scalar(xm_il[1][half][:, block(k), :], source, 1.0, 0.0, MULT, ADD)
 
-        def quantise_xm(g, lo, hi):
-            quantise(xm_q[g], slice(lo, hi), xm_il[g][:, lo:hi, :].rearrange("p d t -> p (d t)"), E4)
+        def quantise_xm(g, half, lo, hi):
+            source = xm_il[g][half][:, lo:hi, :].rearrange("p d t -> p (d t)")
+            quantise(xm_q[g][half], slice(lo, hi), source, E4)
 
         def quantise_h(g, tag=None):
             h_q[g] = mx_tiles(f"h{g}", tag)
@@ -184,31 +183,39 @@ def tile_attend_gsqh_wx_ts_kernel(tc, xT, wT, y, wt, ts, xm, offs, out_0, out_1)
             )
 
         dw_ps = [None] * 4
+        xm_first = mx_tiles("xm_first", None, P)
 
         def dw_pass(g, b):
-            if g == 0:
-                dw_ps[b] = ps_dw.tile([P, N], F32, name=f"dw_ps{b}", tag=f"dw_bank{b % 2}")
-            mx(dw_ps[b][:], xm_q[g], b, E4, h_q[g], E5, g == 0, g == G - 1)
+            if g == 0 and b < 2:
+                dw_ps[b] = ps_dw.tile([P, N], F32, name=f"dw_ps{b}", tag=f"dw_bank{b}")
+            elif g == 0:
+                dw_ps[b] = ps_turn.tile([P, N], F32, name="turn")
+            lhs, k = (xm_first, 0) if (g, b) == (1, 0) else (xm_q[g][b // 2], b % 2)
+            mx(dw_ps[b][:], lhs, k, E4, h_q[g], E5, g == 0, g == G - 1)
 
-        ws_il = sb("ws_il", [P, 4, P, 2], F32, "x_raw0")
+        ws_il = [sb("ws_il0", [P, 2, P, 2], F32), sb("ws_il1", [P, 2, P, 2], F32, "x_raw0")]
+        ws_q = mx_tiles("ws")
         hs_il = [None] * G
         hs_q = [mx_tiles(f"hs{g}") for g in range(G)]
 
-        def turn_w():
-            for half in range(2):
-                bank = ps_turn.tile([P, 2, 2, P], F32, name="turn")
-                for s in range(2):
-                    words = w_bf[:, 2 * half + s, :].bitcast(F32)
-                    for u in range(2):
-                        nc.tensor.transpose(bank[:, s, u, :], words[:, u : N // 2 : 2], ident[:])
-                nc.scalar.copy(ws_il[:, 2 * half : 2 * half + 2, :, :], bank[:].rearrange("p s u q -> p s q u"))
+        def turn_w(half):
+            bank = ps_turn.tile([P, 2, 2, P], F32, name="turn")
+            for s in range(2):
+                words = w_bf[:, 2 * half + s, :].bitcast(F32)
+                for u in range(2):
+                    nc.tensor.transpose(bank[:, s, u, :], words[:, u : N // 2 : 2], ident[:])
+            nc.scalar.copy(ws_il[half][:], bank[:].rearrange("p s u q -> p s q u"))
+
+        def quantise_ws(half):
+            cols = slice(half * HALF, (half + 1) * HALF)
+            quantise(ws_q, cols, ws_il[half][:].rearrange("p j q u -> p (j q u)").bitcast(BF16), E4)
 
         def turn_h(g, tag=None):
             hs_il[g] = sb(f"hs_il{g}", [P, 2, 2, P, 4], BF16, tag)
             words = h_il[g][:].rearrange("p i t -> p (i t)").bitcast(F32)
             for u in range(2):
-                if (g, u) == (G - 1, 0):
-                    bank = ps_dw.tile([P, 4, P], F32, name="turn_h", tag="dw_bank0")
+                if g == G - 1:
+                    bank = ps_dw.tile([P, 4, P], F32, name="turn_h", tag=f"dw_bank{u}")
                 else:
                     bank = ps_lone.tile([P, 4, P], F32, name="lone")
                 for e in range(4):
@@ -221,6 +228,8 @@ def tile_attend_gsqh_wx_ts_kernel(tc, xT, wT, y, wt, ts, xm, offs, out_0, out_1)
         def quantise_hs(g):
             quantise(hs_q[g], whole, hs_il[g][:].rearrange("p u v q e -> p (u v q e)"), E5)
 
+        turn_w(0)
+        quantise_ws(0)
         slices = ((0, HALF), (HALF, HALF + P), (HALF + P, N))
         for lo, hi in slices:
             part = offsets[:, lo // LIST_ROWS : hi // LIST_ROWS]
@@ -251,28 +260,31 @@ def tile_attend_gsqh_wx_ts_kernel(tc, xT, wT, y, wt, ts, xm, offs, out_0, out_1)
         quantise(x_q[1], whole, x_il[1][:].rearrange("p t m j -> p (t m j)"), E4)
         factor(1, 2)
         factor(1, 3)
-        xm_il[0] = sb("xm_il0", [P, D, 4], BF16)
+        xm_il[0] = [sb(f"xm_il0_{half}", [P, HALF, 4], BF16) for half in range(2)]
         for b in range(4):
             xm_interleave(0, b)
+        xm_il[1][1] = sb("xm_il1_1", [P, HALF, 4], BF16, "ts_all")
+        for b in range(2, 4):
+            xm_interleave(1, b)
         for t in range(4):
             scores(1, t)
-        xm_il[1] = sb("xm_il1", [P, D, 4], BF16, "z3")
+        xm_il[1][0] = sb("xm_il1_0", [P, HALF, 4], BF16, "z3")
         xm_interleave(1, 0)
         quantise_h(0, "z1")
-        xm_q[0] = mx_tiles("xm0", "z2")
-        quantise_xm(0, 0, D)
+        xm_q[0][0] = mx_tiles("xm0_0", "z2", HALF)
+        quantise_xm(0, 0, 0, HALF)
+        turn_w(1)
+        quantise_ws(1)
         for b in range(2):
             dw_pass(0, b)
         gradient(1)
-        xm_q[1] = mx_tiles("xm1")
-        quantise_xm(1, 0, P)
+        xm_q[1][0] = mx_tiles("xm1_0", None, HALF)
+        quantise(xm_first, block(0), xm_il[1][0][:, block(0), :].rearrange("p d t -> p (d t)"), E4)
         quantise_h(1)
 
         dw_sb = [None] * 4
 
         def finish_dw(b):
-            if b >= 2:
-                dw_pass(0, b)
             dw_pass(1, b)
             dw_sb[b] = sb(f"dw_sb{b}", [P, N], F32)
             nc.scalar.copy(dw_sb[b][:], dw_ps[b][:])
@@ -292,20 +304,20 @@ def tile_attend_gsqh_wx_ts_kernel(tc, xT, wT, y, wt, ts, xm, offs, out_0, out_1)
                 )
             nc.scalar.dma_start(gx_view[g][:, 2 * pair : 2 * pair + 2, :], gx[:])
 
-        turn_w()
-        turn_h(0, "xm_first")
+        turn_h(0, "wt_abs")
+        xm_interleave(1, 1)
         finish_dw(0)
         quantise_hs(0)
-        ws_q = mx_tiles("ws", "margin1")
-        quantise(ws_q, whole, ws_il[:].rearrange("p j q u -> p (j q u)").bitcast(BF16), E4)
-        xm_interleave(1, 1)
-        quantise_xm(1, P, 2 * P)
+        xm_q[0][1] = mx_tiles("xm0_1", "xm_first_codes", HALF)
+        quantise_xm(0, 1, 0, HALF)
+        quantise_xm(1, 0, P, HALF)
+        xm_q[1][1] = mx_tiles("xm1_1", "xm_first_scales", HALF)
+        quantise_xm(1, 1, 0, HALF)
         scatter(0)
         rows_out(0, 0)
         finish_dw(1)
-        xm_interleave(1, 2)
-        xm_interleave(1, 3)
-        quantise_xm(1, 2 * P, D)
+        for b in range(2, 4):
+            dw_pass(0, b)
         rows_out(0, 1)
         scatter(1)
         turn_h(1)

@@ -1,7 +1,6 @@
 from contextlib import ExitStack
 
 import concourse.mybir as mybir
-from concourse.masks import make_identity
 
 N, T, D, R = 512, 2048, 512, 1024
 FLOPS = 3 * 2 * N * D * R
@@ -17,6 +16,7 @@ E5 = mybir.dt.float8_e5m2_x4
 MULT = mybir.AluOpType.mult
 ADD = mybir.AluOpType.add
 IS_GE = mybir.AluOpType.is_ge
+NOT_EQUAL = mybir.AluOpType.not_equal
 ABS = mybir.ActivationFunctionType.Abs
 RELU = mybir.ActivationFunctionType.Relu
 
@@ -94,9 +94,14 @@ def tile_attend_gsqh_wx_ts_kernel(tc, xT, wT, y, wt, ts, xm, offs, out_0, out_1)
         for g, half in ((0, 0), (0, 1), (1, 1), (1, 0)):
             nc.sync.dma_start(xm_raw[g][half][:], xm_view[g][:, :, half * HALF : (half + 1) * HALF])
 
-        make_identity(nc, ident[:])
+        zeros = sb("zeros", [P, P], F32, "window2")
+        nc.gpsimd.memset(zeros[:], 0.0)
+        nc.gpsimd.affine_select(
+            out=ident[:], in_=zeros[:], compare_op=NOT_EQUAL, fill=1.0, base=0, pattern=[[-1, P]], channel_multiplier=1
+        )
         windows = [sb(f"window{b}", [P, T], F32) for b in range(WINDOWS)]
-        for window in windows:
+        nc.gpsimd.memset(windows[-1][:].bitcast(I32), 0)
+        for window in windows[:-1]:
             nc.vector.memset(window[:].bitcast(I32), 0)
 
         wt_abs = sb("wt_abs", [P, G, 4], F32)

@@ -18,6 +18,7 @@ ADD = mybir.AluOpType.add
 IS_GE = mybir.AluOpType.is_ge
 NOT_EQUAL = mybir.AluOpType.not_equal
 ABS = mybir.ActivationFunctionType.Abs
+COPY = mybir.ActivationFunctionType.Copy
 RELU = mybir.ActivationFunctionType.Relu
 
 P = 128
@@ -62,6 +63,7 @@ def tile_attend_gsqh_wx_ts_kernel(tc, xT, wT, y, wt, ts, xm, offs, out_0, out_1)
             )
 
         whole = slice(0, PASS)
+        halves = (slice(0, HALF), slice(HALF, PASS))
 
         offsets = keep.tile([P, N // LIST_ROWS], U16, name="offsets")
         w_planes = [sb(f"w_plane{j}", [P, T], F32) for j in range(4)]
@@ -106,10 +108,17 @@ def tile_attend_gsqh_wx_ts_kernel(tc, xT, wT, y, wt, ts, xm, offs, out_0, out_1)
 
         wt_abs = sb("wt_abs", [P, G, 4], F32)
         wt_step = sb("wt_step", [P, G, 4], F32)
-        minus_sign = sb("minus_sign", [P, G, 4], F32)
+        all_signs = sb("all_signs", [P, G, 4], F32)
         nc.vector.tensor_scalar(wt_step[:], wt_sb[:], 0.0, -2.0, IS_GE, MULT)
         nc.scalar.activation(wt_abs[:], wt_sb[:], ABS)
-        nc.vector.tensor_scalar(minus_sign[:], wt_step[:], 1.0, None, ADD)
+        nc.vector.tensor_scalar(all_signs[:], wt_step[:], 1.0, None, ADD)
+        minus_sign = {(0, t): all_signs[:, 0, t : t + 1] for t in range(4)}
+
+        def signs(g, lo, hi, tag):
+            tile = sb(f"minus_sign{g}_{lo}", [P, hi - lo], F32, tag)
+            nc.scalar.copy(tile[:], all_signs[:, g, lo:hi])
+            for t in range(lo, hi):
+                minus_sign[g, t] = tile[:, t - lo : t - lo + 1]
 
         table_view = ts_table[:].rearrange("p (n k e) -> p k n e", k=4, e=4)
         for k in range(4):
@@ -120,14 +129,27 @@ def tile_attend_gsqh_wx_ts_kernel(tc, xT, wT, y, wt, ts, xm, offs, out_0, out_1)
             nc.scalar.copy(table_view[:, k], bank[:].rearrange("p e n -> p n e"))
 
         w_il = sb("w_il", [P, N, 4], BF16)
-        w_flat = sb("w_bf", [P, 4 * N], BF16)
+        ts_all = sb("ts_all", [P, N], F32)
+        nc.vector.tensor_copy(ts_all[:], ts_table[:].indirect(offsets[:]))
+        w_flat = sb("w_bf", [P, 4 * N], BF16, "ts_table")
         w_bf = w_flat[:].rearrange("p (j i) -> p j i", j=4)
         for j in range(3):
             nc.vector.tensor_copy(w_bf[:, j, :], w_planes[j][:].indirect(offsets[:]))
-        ts_all = sb("ts_all", [P, N], F32)
-        nc.vector.tensor_copy(ts_all[:], ts_table[:].indirect(offsets[:]))
 
-        x_il = [sb(f"x_il{g}", [P, 4, P, 4], BF16) for g in range(G)]
+        bank = ps_turn.tile([P, 4, P], F32, name="turn")
+        for k in range(4):
+            nc.tensor.transpose(bank[:, k, :], ts_all[:, block(k)], ident[:])
+        ts_columns = sb("ts_columns", [P, 4], F32)
+        nc.scalar.copy(ts_columns[:], bank[:, :, 0])
+        ts_bank = ps_dw.tile([P, N], F32, name="ts_bank", tag="dw_bank0")
+        for k in range(4):
+            nc.tensor.transpose(ts_bank[:, block(k)], ts_columns[:, k : k + 1].to_broadcast([P, P]), ident[:])
+
+        signed = {t: sb(f"signed{t}", [P, N], F32) for t in (2, 3)}
+        for t in (2, 3):
+            nc.scalar.activation(signed[t][:], ts_all[:], COPY, scale=minus_sign[0, t])
+
+        x_il = [sb("x_il0", [P, 4, P, 4], BF16), None]
         xm_il = [[None, None] for g in range(G)]
         h_il = [sb(f"h_il{g}", [P, N, 4], BF16) for g in range(G)]
         margin = [sb(f"margin{g}", [P, 4, N], F32) for g in range(G)]
@@ -158,9 +180,11 @@ def tile_attend_gsqh_wx_ts_kernel(tc, xT, wT, y, wt, ts, xm, offs, out_0, out_1)
                 source = xm_raw[g][half][:, :, block(k)].rearrange("p t d -> p d t")
                 nc.gpsimd.tensor_scalar(xm_il[1][half][:, block(k), :], source, 1.0, 0.0, MULT, ADD)
 
-        def quantise_xm(g, half, lo, hi):
-            source = xm_il[g][half][:, lo:hi, :].rearrange("p d t -> p (d t)")
-            quantise(xm_q[g][half], slice(lo, hi), source, E4)
+        def quantise_xm(g, lo, hi):
+            half, k = divmod(lo, 2)
+            source = xm_il[g][half][:, k * P : (k + hi - lo) * P, :].rearrange("p d t -> p (d t)")
+            first = max(lo - 1, 0)
+            quantise(xm_q[g][min(lo, 1)], slice(first * P, (first + hi - lo) * P), source, E4)
 
         def quantise_h(g, tag=None):
             h_q[g] = mx_tiles(f"h{g}", tag)
@@ -168,35 +192,36 @@ def tile_attend_gsqh_wx_ts_kernel(tc, xT, wT, y, wt, ts, xm, offs, out_0, out_1)
 
         def factor(g, t):
             c = y_sb[g][:, t, :]
-            nc.vector.scalar_tensor_tensor(c, c, minus_sign[:, g, t : t + 1], ts_all[:], MULT, MULT)
+            scales = ts_bank if g == 0 else ts_all
+            nc.vector.scalar_tensor_tensor(c, c, minus_sign[g, t], scales[:], MULT, MULT)
 
         def scores(g, t):
             sums = ps_lone.tile([P, N], F32, name="lone")
             mx(sums[:], x_q[g], t, E4, w_q, E4, True, True)
-            z = sb(f"z{t}", [P, N], F32) if g == 1 and t > 0 else ring.tile([P, N], F32, name="z", bufs=3)
-            nc.vector.tensor_tensor(z[:], sums[:], y_sb[g][:, t, :], MULT)
-            nc.scalar.activation(
-                margin[g][:, t, :], z[:], RELU, bias=wt_abs[:, g, t : t + 1], scale=wt_sb[:, g, t : t + 1]
-            )
+            z = sb(f"z{g}_{t}", [P, N], F32) if t > 0 else ring.tile([P, N], F32, name="z", bufs=1)
+            for cols in halves if (g, t) == (G - 1, 3) else (whole,):
+                nc.vector.tensor_tensor(z[:, cols], sums[:, cols], y_sb[g][:, t, cols], MULT)
+                nc.scalar.activation(
+                    margin[g][:, t, cols], z[:, cols], RELU, bias=wt_abs[:, g, t : t + 1], scale=wt_sb[:, g, t : t + 1]
+                )
 
         def gradient(g):
-            nc.vector.tensor_tensor(
-                h_il[g][:].rearrange("p (c i) t -> p c t i", i=2),
-                margin[g][:].rearrange("p t (c i) -> p c t i", i=2),
-                y_sb[g][:].rearrange("p t (c i) -> p c t i", i=2),
-                MULT,
-            )
+            for cols in halves if g == G - 1 else (whole,):
+                nc.vector.tensor_tensor(
+                    h_il[g][:, cols, :].rearrange("p (c i) t -> p c t i", i=2),
+                    margin[g][:, :, cols].rearrange("p t (c i) -> p c t i", i=2),
+                    y_sb[g][:, :, cols].rearrange("p t (c i) -> p c t i", i=2),
+                    MULT,
+                )
 
         dw_ps = [None] * 4
-        xm_first = mx_tiles("xm_first", None, P)
 
         def dw_pass(g, b):
             if g == 0 and b < 2:
                 dw_ps[b] = ps_dw.tile([P, N], F32, name=f"dw_ps{b}", tag=f"dw_bank{b}")
             elif g == 0:
                 dw_ps[b] = ps_turn.tile([P, N], F32, name="turn")
-            lhs, k = (xm_first, 0) if (g, b) == (1, 0) else (xm_q[g][b // 2], b % 2)
-            mx(dw_ps[b][:], lhs, k, E4, h_q[g], E5, g == 0, g == G - 1)
+            mx(dw_ps[b][:], xm_q[g][min(b, 1)], max(b - 1, 0), E4, h_q[g], E5, g == 0, g == G - 1)
 
         ws_il = [sb("ws_il0", [P, 2, P, 2], F32), sb("ws_il1", [P, 2, P, 2], F32, "x_raw0")]
         ws_q = mx_tiles("ws")
@@ -251,13 +276,17 @@ def tile_attend_gsqh_wx_ts_kernel(tc, xT, wT, y, wt, ts, xm, offs, out_0, out_1)
             tiles = x_il[0][:, 2 * pair : 2 * pair + 2]
             quantise(x_q[0], slice(pair * HALF, (pair + 1) * HALF), tiles.rearrange("p t m j -> p (t m j)"), E4)
 
-        for pair in range(2):
-            for t in (2 * pair, 2 * pair + 1):
-                factor(0, t)
-            for t in (2 * pair, 2 * pair + 1):
-                scores(0, t)
+        for t in (2, 3):
+            nc.gpsimd.tensor_tensor(y_sb[0][:, t, :], y_sb[0][:, t, :], signed[t][:], MULT)
+        factor(0, 0)
+        factor(0, 1)
+        for t in range(4):
+            scores(0, t)
+        signs(1, 0, 2, "z0_1")
+        x_il[1] = sb("x_il1", [P, 4, P, 4], BF16, "z0_3")
         for pair in range(2):
             x_interleave(on_scalar, 1, pair, 0, P)
+        signs(1, 2, 4, "x_raw1")
         factor(1, 0)
         factor(1, 1)
         gradient(0)
@@ -273,18 +302,17 @@ def tile_attend_gsqh_wx_ts_kernel(tc, xT, wT, y, wt, ts, xm, offs, out_0, out_1)
             xm_interleave(1, b)
         for t in range(4):
             scores(1, t)
-        xm_il[1][0] = sb("xm_il1_0", [P, HALF, 4], BF16, "z3")
+        xm_il[1][0] = sb("xm_il1_0", [P, HALF, 4], BF16, "z1_3")
         xm_interleave(1, 0)
-        quantise_h(0, "z1")
-        xm_q[0][0] = mx_tiles("xm0_0", "z2", HALF)
-        quantise_xm(0, 0, 0, HALF)
+        quantise_h(0, "z1_1")
+        xm_q[0][0] = mx_tiles("xm0_first", "z1_2", P)
+        quantise_xm(0, 0, 1)
         turn_w(1)
         quantise_ws(1)
-        for b in range(2):
-            dw_pass(0, b)
+        dw_pass(0, 0)
         gradient(1)
-        xm_q[1][0] = mx_tiles("xm1_0", None, HALF)
-        quantise(xm_first, block(0), xm_il[1][0][:, block(0), :].rearrange("p d t -> p (d t)"), E4)
+        xm_q[1][0] = mx_tiles("xm1_first", None, P)
+        quantise_xm(1, 0, 1)
         quantise_h(1)
 
         dw_sb = [None] * 4
@@ -313,13 +341,14 @@ def tile_attend_gsqh_wx_ts_kernel(tc, xT, wT, y, wt, ts, xm, offs, out_0, out_1)
         xm_interleave(1, 1)
         finish_dw(0)
         quantise_hs(0)
-        xm_q[0][1] = mx_tiles("xm0_1", "xm_first_codes", HALF)
-        quantise_xm(0, 1, 0, HALF)
-        quantise_xm(1, 0, P, HALF)
-        xm_q[1][1] = mx_tiles("xm1_1", "xm_first_scales", HALF)
-        quantise_xm(1, 1, 0, HALF)
+        for g, tag in enumerate(("xm1_first_codes", "xm1_first_scales")):
+            xm_q[g][1] = mx_tiles(f"xm{g}_rest", tag, D - P)
+            quantise_xm(g, 1, 2)
+        for g in range(G):
+            quantise_xm(g, 2, 4)
         scatter(0)
         rows_out(0, 0)
+        dw_pass(0, 1)
         finish_dw(1)
         for b in range(2, 4):
             dw_pass(0, b)

@@ -90,9 +90,9 @@ def tile_attend_gsqh_wx_ts_kernel(tc, xT, wT, y, wt, ts, xm, offs, out_0, out_1)
         nc.sync.dma_start(x_raw[0][:], x_view[0])
         nc.sync.dma_start(y_sb[0][:, 0:2, :], y_view[0][:, 0:2, :])
         nc.sync.dma_start(y_sb[0][:, 2:4, :], y_view[0][:, 2:4, :])
-        nc.sync.dma_start(y_sb[1][:, 0:2, :], y_view[1][:, 0:2, :])
         nc.sync.dma_start(x_raw[1][:], x_view[1])
         nc.sync.dma_start(y_sb[1][:, 2:4, :], y_view[1][:, 2:4, :])
+        nc.sync.dma_start(y_sb[1][:, 0:2, :], y_view[1][:, 0:2, :])
         for g, half in ((0, 0), (0, 1), (1, 1), (1, 0)):
             nc.sync.dma_start(xm_raw[g][half][:], xm_view[g][:, :, half * HALF : (half + 1) * HALF])
 
@@ -112,13 +112,11 @@ def tile_attend_gsqh_wx_ts_kernel(tc, xT, wT, y, wt, ts, xm, offs, out_0, out_1)
         nc.vector.tensor_scalar(wt_step[:], wt_sb[:], 0.0, -2.0, IS_GE, MULT)
         nc.scalar.activation(wt_abs[:], wt_sb[:], ABS)
         nc.vector.tensor_scalar(all_signs[:], wt_step[:], 1.0, None, ADD)
-        minus_sign = {(0, t): all_signs[:, 0, t : t + 1] for t in range(4)}
+        minus_sign = {(g, t): all_signs[:, g, t : t + 1] for g in range(G) for t in range(4)}
 
-        def signs(g, lo, hi, tag):
-            tile = sb(f"minus_sign{g}_{lo}", [P, hi - lo], F32, tag)
-            nc.scalar.copy(tile[:], all_signs[:, g, lo:hi])
-            for t in range(lo, hi):
-                minus_sign[g, t] = tile[:, t - lo : t - lo + 1]
+        last_wt = [sb(f"last_wt{half}", [P, 1], F32) for half in range(2)]
+        for weight in last_wt:
+            nc.vector.tensor_copy(weight[:], wt_sb[:, G - 1, 3:4])
 
         table_view = ts_table[:].rearrange("p (n k e) -> p k n e", k=4, e=4)
         for k in range(4):
@@ -147,10 +145,11 @@ def tile_attend_gsqh_wx_ts_kernel(tc, xT, wT, y, wt, ts, xm, offs, out_0, out_1)
 
         signed = {t: sb(f"signed{t}", [P, N], F32) for t in (2, 3)}
         for t in (2, 3):
-            nc.scalar.activation(signed[t][:], ts_all[:], COPY, scale=minus_sign[0, t])
+            nc.scalar.activation(signed[t][:], ts_all[:], COPY, scale=minus_sign[1, t])
 
-        x_il = [sb("x_il0", [P, 4, P, 4], BF16), None]
-        xm_il = [[None, None] for g in range(G)]
+        x_il = {(g, pair): sb(f"x_il{g}_{pair}", [P, 2, P, 4], BF16) for g, pair in ((0, 0), (0, 1), (1, 0))}
+        factors = [y_sb[0], None]
+        xm_il = {}
         h_il = [sb(f"h_il{g}", [P, N, 4], BF16) for g in range(G)]
         margin = [sb(f"margin{g}", [P, 4, N], F32) for g in range(G)]
         x_q = [mx_tiles(f"x{g}") for g in range(G)]
@@ -162,7 +161,7 @@ def tile_attend_gsqh_wx_ts_kernel(tc, xT, wT, y, wt, ts, xm, offs, out_0, out_1)
         def x_interleave(copy, g, pair, lo, hi):
             tiles = slice(2 * pair, 2 * pair + 2)
             copy(
-                x_il[g][:].rearrange("p t m j -> p m j t")[:, lo:hi, :, tiles],
+                x_il[g, pair][:].rearrange("p t m j -> p m j t")[:, lo:hi],
                 x_raw[g][:].rearrange("p j (m t) -> p m j t", t=4)[:, lo:hi, :, tiles],
             )
 
@@ -173,16 +172,20 @@ def tile_attend_gsqh_wx_ts_kernel(tc, xT, wT, y, wt, ts, xm, offs, out_0, out_1)
             )
 
         def xm_interleave(g, b):
-            half, k = divmod(b, 2)
-            if (g, half) != (1, 1):
-                interleave(on_scalar, xm_il[g][half], xm_raw[g][half], P * k, P * (k + 1))
+            source = xm_raw[g][b // 2][:, :, block(b % 2)]
+            if g == 0 or b < 2:
+                interleave(on_scalar, xm_il[g, b], source, 0, P)
             else:
-                source = xm_raw[g][half][:, :, block(k)].rearrange("p t d -> p d t")
-                nc.gpsimd.tensor_scalar(xm_il[1][half][:, block(k), :], source, 1.0, 0.0, MULT, ADD)
+                nc.gpsimd.tensor_scalar(xm_il[g, b], source.rearrange("p t d -> p d t"), 1.0, 0.0, MULT, ADD)
+
+        def xm_tile(g, lo, hi, tag=None):
+            tile = sb(f"xm_il{g}_{lo}", [P, (hi - lo) * P, 4], BF16, tag)
+            for b in range(lo, hi):
+                xm_il[g, b] = tile[:, block(b - lo), :]
+            xm_il[g, lo, hi] = tile[:]
 
         def quantise_xm(g, lo, hi):
-            half, k = divmod(lo, 2)
-            source = xm_il[g][half][:, k * P : (k + hi - lo) * P, :].rearrange("p d t -> p (d t)")
+            source = xm_il[g, lo, hi].rearrange("p d t -> p (d t)")
             first = max(lo - 1, 0)
             quantise(xm_q[g][min(lo, 1)], slice(first * P, (first + hi - lo) * P), source, E4)
 
@@ -191,26 +194,28 @@ def tile_attend_gsqh_wx_ts_kernel(tc, xT, wT, y, wt, ts, xm, offs, out_0, out_1)
             quantise(h_q[g], whole, h_il[g][:].rearrange("p i t -> p (i t)"), E5)
 
         def factor(g, t):
-            c = y_sb[g][:, t, :]
-            scales = ts_bank if g == 0 else ts_all
-            nc.vector.scalar_tensor_tensor(c, c, minus_sign[g, t], scales[:], MULT, MULT)
+            nc.vector.scalar_tensor_tensor(factors[g][:, t, :], y_sb[g][:, t, :], minus_sign[g, t], ts_bank[:], MULT, MULT)
 
         def scores(g, t):
             sums = ps_lone.tile([P, N], F32, name="lone")
             mx(sums[:], x_q[g], t, E4, w_q, E4, True, True)
-            z = sb(f"z{g}_{t}", [P, N], F32) if t > 0 else ring.tile([P, N], F32, name="z", bufs=1)
-            for cols in halves if (g, t) == (G - 1, 3) else (whole,):
-                nc.vector.tensor_tensor(z[:, cols], sums[:, cols], y_sb[g][:, t, cols], MULT)
-                nc.scalar.activation(
-                    margin[g][:, t, cols], z[:, cols], RELU, bias=wt_abs[:, g, t : t + 1], scale=wt_sb[:, g, t : t + 1]
-                )
+            size = wt_abs[:, g, t : t + 1]
+            if (g, t) != (G - 1, 3):
+                z = sb("z0_3", [P, N], F32) if t == 3 else ring.tile([P, N], F32, name="z", bufs=3)
+                nc.vector.tensor_tensor(z[:], sums[:], factors[g][:, t, :], MULT)
+                nc.scalar.activation(margin[g][:, t, :], z[:], RELU, bias=size, scale=wt_sb[:, g, t : t + 1])
+                return
+            for half, cols in enumerate(halves):
+                z = sb(f"last_z{half}", [P, HALF], F32)
+                nc.vector.scalar_tensor_tensor(z[:], sums[:, cols], last_wt[half][:], factors[g][:, t, cols], MULT, MULT)
+                nc.scalar.activation(margin[g][:, t, cols], z[:], RELU, bias=size)
 
         def gradient(g):
             for cols in halves if g == G - 1 else (whole,):
                 nc.vector.tensor_tensor(
                     h_il[g][:, cols, :].rearrange("p (c i) t -> p c t i", i=2),
                     margin[g][:, :, cols].rearrange("p t (c i) -> p c t i", i=2),
-                    y_sb[g][:, :, cols].rearrange("p t (c i) -> p c t i", i=2),
+                    factors[g][:, :, cols].rearrange("p t (c i) -> p c t i", i=2),
                     MULT,
                 )
 
@@ -272,43 +277,47 @@ def tile_attend_gsqh_wx_ts_kernel(tc, xT, wT, y, wt, ts, xm, offs, out_0, out_1)
         x_interleave(on_vector, 0, 0, 0, P)
         x_interleave(on_scalar, 0, 1, X_SPLIT, P)
         x_interleave(on_vector, 0, 1, 0, X_SPLIT)
-        for pair in range(2):
-            tiles = x_il[0][:, 2 * pair : 2 * pair + 2]
-            quantise(x_q[0], slice(pair * HALF, (pair + 1) * HALF), tiles.rearrange("p t m j -> p (t m j)"), E4)
 
+        def quantise_x(g, pair):
+            quantise(x_q[g], halves[pair], x_il[g, pair][:].rearrange("p t m j -> p (t m j)"), E4)
+
+        quantise_x(0, 0)
+        quantise_x(0, 1)
+        turn_w(1)
+        quantise_ws(1)
+
+        factors[1] = sb("factors1", [P, 4, N], F32, "x_raw0")
         for t in (2, 3):
-            nc.gpsimd.tensor_tensor(y_sb[0][:, t, :], y_sb[0][:, t, :], signed[t][:], MULT)
-        factor(0, 0)
-        factor(0, 1)
-        for t in range(4):
-            scores(0, t)
-        signs(1, 0, 2, "z0_1")
-        x_il[1] = sb("x_il1", [P, 4, P, 4], BF16, "z0_3")
+            nc.gpsimd.tensor_tensor(factors[1][:, t, :], y_sb[1][:, t, :], signed[t][:], MULT)
         for pair in range(2):
-            x_interleave(on_scalar, 1, pair, 0, P)
-        signs(1, 2, 4, "x_raw1")
+            for t in (2 * pair, 2 * pair + 1):
+                factor(0, t)
+            if pair == 1:
+                x_interleave(on_scalar, 1, 0, 0, P)
+            for t in (2 * pair, 2 * pair + 1):
+                scores(0, t)
+        x_il[1, 1] = sb("x_il1_1", [P, 2, P, 4], BF16, "z0_3")
+        x_interleave(on_scalar, 1, 1, 0, P)
         factor(1, 0)
         factor(1, 1)
+        quantise_x(1, 0)
         gradient(0)
 
-        quantise(x_q[1], whole, x_il[1][:].rearrange("p t m j -> p (t m j)"), E4)
-        factor(1, 2)
-        factor(1, 3)
-        xm_il[0] = [sb(f"xm_il0_{half}", [P, HALF, 4], BF16) for half in range(2)]
+        quantise_x(1, 1)
+        for lo, hi in ((0, 1), (1, 2), (2, 4)):
+            xm_tile(0, lo, hi)
         for b in range(4):
             xm_interleave(0, b)
-        xm_il[1][1] = sb("xm_il1_1", [P, HALF, 4], BF16, "ts_all")
+        xm_tile(1, 2, 4, "z0_3")
         for b in range(2, 4):
             xm_interleave(1, b)
         for t in range(4):
             scores(1, t)
-        xm_il[1][0] = sb("xm_il1_0", [P, HALF, 4], BF16, "z1_3")
+        xm_tile(1, 0, 1, "last_z0")
         xm_interleave(1, 0)
-        quantise_h(0, "z1_1")
-        xm_q[0][0] = mx_tiles("xm0_first", "z1_2", P)
+        quantise_h(0, "last_wt0")
+        xm_q[0][0] = mx_tiles("xm0_first", "last_wt1", P)
         quantise_xm(0, 0, 1)
-        turn_w(1)
-        quantise_ws(1)
         dw_pass(0, 0)
         gradient(1)
         xm_q[1][0] = mx_tiles("xm1_first", None, P)
@@ -338,14 +347,16 @@ def tile_attend_gsqh_wx_ts_kernel(tc, xT, wT, y, wt, ts, xm, offs, out_0, out_1)
             nc.scalar.dma_start(gx_view[g][:, 2 * pair : 2 * pair + 2, :], gx[:])
 
         turn_h(0, "wt_abs")
+        xm_tile(1, 1, 2, "last_z1")
         xm_interleave(1, 1)
         finish_dw(0)
+        xm_q[0][1] = mx_tiles("xm0_rest", "last_z0", D - P)
+        quantise_xm(0, 1, 2)
+        quantise_xm(0, 2, 4)
         quantise_hs(0)
-        for g, tag in enumerate(("xm1_first_codes", "xm1_first_scales")):
-            xm_q[g][1] = mx_tiles(f"xm{g}_rest", tag, D - P)
-            quantise_xm(g, 1, 2)
-        for g in range(G):
-            quantise_xm(g, 2, 4)
+        xm_q[1][1] = mx_tiles("xm1_rest", "xm1_first_codes", D - P)
+        quantise_xm(1, 1, 2)
+        quantise_xm(1, 2, 4)
         scatter(0)
         rows_out(0, 0)
         dw_pass(0, 1)

@@ -69,7 +69,11 @@ def tile_attend_gsqh_wx_ts_kernel(tc, xT, wT, y, wt, ts, xm, offs, out_0, out_1)
         w_planes = [sb(f"w_plane{j}", [P, T], F32) for j in range(4)]
         x_raw = [sb(f"x_raw{g}", [P, 4, PASS], F32) for g in range(G)]
         y_sb = [sb(f"y_sb{g}", [P, 4, N], F32) for g in range(G)]
-        xm_raw = [[sb(f"xm_raw{g}_{half}", [P, 4, HALF], F32) for half in range(2)] for g in range(G)]
+        xm_raw0 = sb("xm_raw0", [P, 4, D], F32)
+        xm_raw = [
+            [xm_raw0[:, :, 0:HALF], xm_raw0[:, :, HALF:D]],
+            [sb(f"xm_raw1_{half}", [P, 4, HALF], F32) for half in range(2)],
+        ]
         wt_sb = sb("wt_sb", [P, G, 4], F32)
         ts_runs = sb("ts_runs", [P, T // P], F32)
         ts_table = sb("ts_table", [P, T], F32)
@@ -90,11 +94,13 @@ def tile_attend_gsqh_wx_ts_kernel(tc, xT, wT, y, wt, ts, xm, offs, out_0, out_1)
         nc.sync.dma_start(x_raw[0][:], x_view[0])
         nc.sync.dma_start(y_sb[0][:, 0:2, :], y_view[0][:, 0:2, :])
         nc.sync.dma_start(y_sb[0][:, 2:4, :], y_view[0][:, 2:4, :])
+        nc.sync.dma_start(y_sb[1][:, 2, :], y_view[1][:, 2, :])
         nc.sync.dma_start(x_raw[1][:], x_view[1])
-        nc.sync.dma_start(y_sb[1][:, 2:4, :], y_view[1][:, 2:4, :])
+        nc.sync.dma_start(y_sb[1][:, 3, :], y_view[1][:, 3, :])
         nc.sync.dma_start(y_sb[1][:, 0:2, :], y_view[1][:, 0:2, :])
-        for g, half in ((0, 0), (0, 1), (1, 1), (1, 0)):
-            nc.sync.dma_start(xm_raw[g][half][:], xm_view[g][:, :, half * HALF : (half + 1) * HALF])
+        nc.sync.dma_start(xm_raw0[:], xm_view[0])
+        for half in (1, 0):
+            nc.sync.dma_start(xm_raw[1][half][:], xm_view[1][:, :, half * HALF : (half + 1) * HALF])
 
         zeros = sb("zeros", [P, P], F32, "window2")
         nc.gpsimd.memset(zeros[:], 0.0)
@@ -114,6 +120,10 @@ def tile_attend_gsqh_wx_ts_kernel(tc, xT, wT, y, wt, ts, xm, offs, out_0, out_1)
         nc.vector.tensor_scalar(all_signs[:], wt_step[:], 1.0, None, ADD)
         minus_sign = {(g, t): all_signs[:, g, t : t + 1] for g in range(G) for t in range(4)}
 
+        for t in (0, 2):
+            early = sb(f"early_sign{t}", [P, 1], F32)
+            nc.vector.tensor_copy(early[:], minus_sign[0, t])
+            minus_sign[0, t] = early[:]
         last_wt = [sb(f"last_wt{half}", [P, 1], F32) for half in range(2)]
         for weight in last_wt:
             nc.vector.tensor_copy(weight[:], wt_sb[:, G - 1, 3:4])
@@ -134,21 +144,12 @@ def tile_attend_gsqh_wx_ts_kernel(tc, xT, wT, y, wt, ts, xm, offs, out_0, out_1)
         for j in range(3):
             nc.vector.tensor_copy(w_bf[:, j, :], w_planes[j][:].indirect(offsets[:]))
 
-        bank = ps_turn.tile([P, 4, P], F32, name="turn")
-        for k in range(4):
-            nc.tensor.transpose(bank[:, k, :], ts_all[:, block(k)], ident[:])
-        ts_columns = sb("ts_columns", [P, 4], F32)
-        nc.scalar.copy(ts_columns[:], bank[:, :, 0])
-        ts_bank = ps_dw.tile([P, N], F32, name="ts_bank", tag="dw_bank0")
-        for k in range(4):
-            nc.tensor.transpose(ts_bank[:, block(k)], ts_columns[:, k : k + 1].to_broadcast([P, P]), ident[:])
-
         signed = {t: sb(f"signed{t}", [P, N], F32) for t in (2, 3)}
         for t in (2, 3):
             nc.scalar.activation(signed[t][:], ts_all[:], COPY, scale=minus_sign[1, t])
 
         x_il = {(g, pair): sb(f"x_il{g}_{pair}", [P, 2, P, 4], BF16) for g, pair in ((0, 0), (0, 1), (1, 0))}
-        factors = [y_sb[0], None]
+        factors = y_sb
         xm_il = {}
         h_il = [sb(f"h_il{g}", [P, N, 4], BF16) for g in range(G)]
         margin = [sb(f"margin{g}", [P, 4, N], F32) for g in range(G)]
@@ -194,7 +195,7 @@ def tile_attend_gsqh_wx_ts_kernel(tc, xT, wT, y, wt, ts, xm, offs, out_0, out_1)
             quantise(h_q[g], whole, h_il[g][:].rearrange("p i t -> p (i t)"), E5)
 
         def factor(g, t):
-            nc.vector.scalar_tensor_tensor(factors[g][:, t, :], y_sb[g][:, t, :], minus_sign[g, t], ts_bank[:], MULT, MULT)
+            nc.vector.scalar_tensor_tensor(factors[g][:, t, :], y_sb[g][:, t, :], minus_sign[g, t], ts_all[:], MULT, MULT)
 
         def scores(g, t):
             sums = ps_lone.tile([P, N], F32, name="lone")
@@ -286,12 +287,14 @@ def tile_attend_gsqh_wx_ts_kernel(tc, xT, wT, y, wt, ts, xm, offs, out_0, out_1)
         turn_w(1)
         quantise_ws(1)
 
-        factors[1] = sb("factors1", [P, 4, N], F32, "x_raw0")
-        for t in (2, 3):
-            nc.gpsimd.tensor_tensor(factors[1][:, t, :], y_sb[1][:, t, :], signed[t][:], MULT)
         for pair in range(2):
             for t in (2 * pair, 2 * pair + 1):
                 factor(0, t)
+            late = sb(f"late_sign{pair}", [P, 1], F32, f"early_sign{2 * pair}")
+            nc.gpsimd.tensor_copy(late[:], minus_sign[1, pair])
+            minus_sign[1, pair] = late[:]
+            c = y_sb[1][:, 2 + pair, :]
+            nc.gpsimd.tensor_tensor(c, c, signed[2 + pair][:], MULT)
             if pair == 1:
                 x_interleave(on_scalar, 1, 0, 0, P)
             for t in (2 * pair, 2 * pair + 1):

@@ -70,10 +70,8 @@ def tile_attend_gsqh_wx_ts_kernel(tc, xT, wT, y, wt, ts, xm, offs, out_0, out_1)
         x_raw = [sb(f"x_raw{g}", [P, 4, PASS], F32) for g in range(G)]
         y_sb = [sb(f"y_sb{g}", [P, 4, N], F32) for g in range(G)]
         xm_raw0 = sb("xm_raw0", [P, 4, D], F32)
-        xm_raw = [
-            [xm_raw0[:, :, 0:HALF], xm_raw0[:, :, HALF:D]],
-            [sb(f"xm_raw1_{half}", [P, 4, HALF], F32) for half in range(2)],
-        ]
+        xm_first = sb("xm_first", [P, 4, P], F32)
+        xm_rest = sb("xm_rest", [P, 4, D - P], F32)
         wt_sb = sb("wt_sb", [P, G, 4], F32)
         ts_runs = sb("ts_runs", [P, T // P], F32)
         ts_table = sb("ts_table", [P, T], F32)
@@ -99,8 +97,8 @@ def tile_attend_gsqh_wx_ts_kernel(tc, xT, wT, y, wt, ts, xm, offs, out_0, out_1)
         nc.sync.dma_start(y_sb[1][:, 3, :], y_view[1][:, 3, :])
         nc.sync.dma_start(y_sb[1][:, 0:2, :], y_view[1][:, 0:2, :])
         nc.sync.dma_start(xm_raw0[:], xm_view[0])
-        for half in (1, 0):
-            nc.sync.dma_start(xm_raw[1][half][:], xm_view[1][:, :, half * HALF : (half + 1) * HALF])
+        nc.sync.dma_start(xm_first[:], xm_view[1][:, :, 0:P])
+        nc.sync.dma_start(xm_rest[:], xm_view[1][:, :, P:D])
 
         zeros = sb("zeros", [P, P], F32, "window2")
         nc.gpsimd.memset(zeros[:], 0.0)
@@ -152,7 +150,7 @@ def tile_attend_gsqh_wx_ts_kernel(tc, xT, wT, y, wt, ts, xm, offs, out_0, out_1)
         factors = y_sb
         xm_il = {}
         h_il = [sb(f"h_il{g}", [P, N, 4], BF16) for g in range(G)]
-        margin = [sb(f"margin{g}", [P, 4, N], F32) for g in range(G)]
+        margin = [sb("margin0", [P, 4, N], F32), None]
         x_q = [mx_tiles(f"x{g}") for g in range(G)]
         xm_q = [[None, None] for g in range(G)]
         h_q = [None] * G
@@ -173,7 +171,10 @@ def tile_attend_gsqh_wx_ts_kernel(tc, xT, wT, y, wt, ts, xm, offs, out_0, out_1)
             )
 
         def xm_interleave(g, b):
-            source = xm_raw[g][b // 2][:, :, block(b % 2)]
+            if g == 0:
+                source = xm_raw0[:, :, block(b)]
+            else:
+                source = xm_rest[:, :, block(b - 1)] if b else xm_first[:]
             if g == 0 or b < 2:
                 interleave(on_scalar, xm_il[g, b], source, 0, P)
             else:
@@ -192,7 +193,8 @@ def tile_attend_gsqh_wx_ts_kernel(tc, xT, wT, y, wt, ts, xm, offs, out_0, out_1)
 
         def quantise_h(g, tag=None):
             h_q[g] = mx_tiles(f"h{g}", tag)
-            quantise(h_q[g], whole, h_il[g][:].rearrange("p i t -> p (i t)"), E5)
+            for cols in halves if g == G - 1 else (whole,):
+                quantise(h_q[g], cols, h_il[g][:, cols, :].rearrange("p i t -> p (i t)"), E5)
 
         def factor(g, t):
             nc.vector.scalar_tensor_tensor(factors[g][:, t, :], y_sb[g][:, t, :], minus_sign[g, t], ts_all[:], MULT, MULT)
@@ -232,7 +234,7 @@ def tile_attend_gsqh_wx_ts_kernel(tc, xT, wT, y, wt, ts, xm, offs, out_0, out_1)
         ws_il = [sb("ws_il0", [P, 2, P, 2], F32), sb("ws_il1", [P, 2, P, 2], F32, "x_raw0")]
         ws_q = mx_tiles("ws")
         hs_il = [None] * G
-        hs_q = [mx_tiles(f"hs{g}") for g in range(G)]
+        hs_q = [None, mx_tiles("hs1")]
 
         def turn_w(half):
             bank = ps_turn.tile([P, 2, 2, P], F32, name="turn")
@@ -307,24 +309,25 @@ def tile_attend_gsqh_wx_ts_kernel(tc, xT, wT, y, wt, ts, xm, offs, out_0, out_1)
         gradient(0)
 
         quantise_x(1, 1)
-        for lo, hi in ((0, 1), (1, 2), (2, 4)):
+        for lo, hi in ((0, 1), (1, 3)):
             xm_tile(0, lo, hi)
-        for b in range(4):
+        for b in range(3):
             xm_interleave(0, b)
+        xm_tile(1, 0, 1)
+        xm_interleave(1, 0)
+        margin[1] = sb("margin1", [P, 4, N], F32, "xm_first")
         xm_tile(1, 2, 4, "z0_3")
         for b in range(2, 4):
             xm_interleave(1, b)
         for t in range(4):
             scores(1, t)
-        xm_tile(1, 0, 1, "last_z0")
-        xm_interleave(1, 0)
         quantise_h(0, "last_wt0")
-        xm_q[0][0] = mx_tiles("xm0_first", "last_wt1", P)
-        quantise_xm(0, 0, 1)
+        firsts = mx_tiles("xm_firsts", "last_wt1", 2 * P)
+        for g in range(G):
+            xm_q[g][0] = (firsts[0][:, block(g)], firsts[1][:, block(g)])
+            quantise_xm(g, 0, 1)
         dw_pass(0, 0)
         gradient(1)
-        xm_q[1][0] = mx_tiles("xm1_first", None, P)
-        quantise_xm(1, 0, 1)
         quantise_h(1)
 
         dw_sb = [None] * 4
@@ -341,7 +344,10 @@ def tile_attend_gsqh_wx_ts_kernel(tc, xT, wT, y, wt, ts, xm, offs, out_0, out_1)
         def rows_out(g, pair):
             gx = ring.tile([P, 2, D], F32, name="gx", bufs=2 * G)
             for k in range(2):
-                sums = ps_lone.tile([P, D], F32, name="lone")
+                if (g, pair) == (0, 0):
+                    sums = ps_turn.tile([P, D], F32, name="turn")
+                else:
+                    sums = ps_lone.tile([P, D], F32, name="lone")
                 mx(sums[:], hs_q[g], 2 * pair + k, E5, ws_q, E4, True, True)
                 nc.scalar.copy(
                     gx[:, k, :].rearrange("p (q j) -> p q j", j=4),
@@ -352,14 +358,17 @@ def tile_attend_gsqh_wx_ts_kernel(tc, xT, wT, y, wt, ts, xm, offs, out_0, out_1)
         turn_h(0, "wt_abs")
         xm_tile(1, 1, 2, "last_z1")
         xm_interleave(1, 1)
+        xm_tile(0, 3, 4, "last_z0")
+        xm_interleave(0, 3)
         finish_dw(0)
-        xm_q[0][1] = mx_tiles("xm0_rest", "last_z0", D - P)
-        quantise_xm(0, 1, 2)
-        quantise_xm(0, 2, 4)
+        hs_q[0] = mx_tiles("hs0", "y_sb1")
         quantise_hs(0)
-        xm_q[1][1] = mx_tiles("xm1_rest", "xm1_first_codes", D - P)
+        xm_q[0][1] = mx_tiles("xm0_rest", "xm_first", D - P)
+        quantise_xm(0, 1, 3)
+        xm_q[1][1] = mx_tiles("xm1_rest", "xm_firsts_scales", D - P)
         quantise_xm(1, 1, 2)
         quantise_xm(1, 2, 4)
+        quantise_xm(0, 3, 4)
         scatter(0)
         rows_out(0, 0)
         dw_pass(0, 1)

@@ -110,11 +110,9 @@ def tile_attend_gsqh_wx_ts_kernel(tc, xT, wT, y, wt, ts, xm, offs, out_0, out_1)
         for window in windows[:-1]:
             nc.vector.memset(window[:].bitcast(I32), 0)
 
-        wt_abs = sb("wt_abs", [P, G, 4], F32)
         wt_step = sb("wt_step", [P, G, 4], F32)
         all_signs = sb("all_signs", [P, G, 4], F32)
         nc.vector.tensor_scalar(wt_step[:], wt_sb[:], 0.0, -2.0, IS_GE, MULT)
-        nc.scalar.activation(wt_abs[:], wt_sb[:], ABS)
         nc.vector.tensor_scalar(all_signs[:], wt_step[:], 1.0, None, ADD)
         minus_sign = {(g, t): all_signs[:, g, t : t + 1] for g in range(G) for t in range(4)}
 
@@ -128,11 +126,14 @@ def tile_attend_gsqh_wx_ts_kernel(tc, xT, wT, y, wt, ts, xm, offs, out_0, out_1)
 
         table_view = ts_table[:].rearrange("p (n k e) -> p k n e", k=4, e=4)
         for k in range(4):
-            bank = ps_turn.tile([P, 4, P], F32, name="turn")
+            bank = ps_lone.tile([P, 4, P], F32, name="lone")
             for e in range(4):
                 column = ts_runs[:, 4 * k + e : 4 * k + e + 1]
                 nc.tensor.transpose(bank[:, e, :], column.to_broadcast([P, P]), ident[:])
             nc.scalar.copy(table_view[:, k], bank[:].rearrange("p e n -> p n e"))
+
+        wt_abs = sb("wt_abs", [P, G, 4], F32, "ts_runs")
+        nc.scalar.activation(wt_abs[:], wt_sb[:], ABS)
 
         w_il = sb("w_il", [P, N, 4], BF16)
         ts_all = sb("ts_all", [P, N], F32)
@@ -355,7 +356,7 @@ def tile_attend_gsqh_wx_ts_kernel(tc, xT, wT, y, wt, ts, xm, offs, out_0, out_1)
                 )
             nc.scalar.dma_start(gx_view[g][:, 2 * pair : 2 * pair + 2, :], gx[:])
 
-        turn_h(0, "wt_abs")
+        turn_h(0, "ts_runs")
         xm_tile(1, 1, 2, "last_z1")
         xm_interleave(1, 1)
         xm_tile(0, 3, 4, "last_z0")

@@ -149,6 +149,7 @@ def tile_attend_gsqh_wx_ts_kernel(tc, xT, wT, y, wt, ts, xm, offs, out_0, out_1)
 
         x_il = {(g, pair): sb(f"x_il{g}_{pair}", [P, 2, P, 4], BF16) for g, pair in ((0, 0), (0, 1), (1, 0))}
         factors = y_sb
+        unit = [None, None]
         xm_il = {}
         h_il = [sb(f"h_il{g}", [P, N, 4], BF16) for g in range(G)]
         margin = [sb("margin0", [P, 4, N], F32), None]
@@ -212,7 +213,7 @@ def tile_attend_gsqh_wx_ts_kernel(tc, xT, wT, y, wt, ts, xm, offs, out_0, out_1)
             for half, cols in enumerate(halves):
                 z = sb(f"last_z{half}", [P, HALF], F32)
                 nc.vector.scalar_tensor_tensor(z[:], sums[:, cols], last_wt[half][:], factors[g][:, t, cols], MULT, MULT)
-                nc.scalar.activation(margin[g][:, t, cols], z[:], RELU, bias=size)
+                nc.scalar.activation(margin[g][:, t, cols], z[:], RELU, bias=size, scale=unit[half][:])
 
         def gradient(g):
             for cols in halves if g == G - 1 else (whole,):
@@ -293,9 +294,8 @@ def tile_attend_gsqh_wx_ts_kernel(tc, xT, wT, y, wt, ts, xm, offs, out_0, out_1)
         for pair in range(2):
             for t in (2 * pair, 2 * pair + 1):
                 factor(0, t)
-            late = sb(f"late_sign{pair}", [P, 1], F32, f"early_sign{2 * pair}")
-            nc.gpsimd.tensor_copy(late[:], minus_sign[1, pair])
-            minus_sign[1, pair] = late[:]
+            unit[pair] = sb(f"unit{pair}", [P, 1], F32, f"early_sign{2 * pair}")
+            nc.gpsimd.memset(unit[pair][:], 1.0)
             c = y_sb[1][:, 2 + pair, :]
             nc.gpsimd.tensor_tensor(c, c, signed[2 + pair][:], MULT)
             if pair == 1:
@@ -317,7 +317,7 @@ def tile_attend_gsqh_wx_ts_kernel(tc, xT, wT, y, wt, ts, xm, offs, out_0, out_1)
         xm_tile(1, 0, 1)
         xm_interleave(1, 0)
         margin[1] = sb("margin1", [P, 4, N], F32, "xm_first")
-        xm_tile(1, 2, 4, "z0_3")
+        xm_tile(1, 2, 4, "margin0")
         for b in range(2, 4):
             xm_interleave(1, b)
         for t in range(4):

@@ -27,7 +27,6 @@ G = R // PASS
 HALF = PASS // 2
 WINDOWS = 3
 LIST_ROWS = 16
-X_SPLIT = 32
 
 
 def tile_attend_gsqh_wx_ts_kernel(tc, xT, wT, y, wt, ts, xm, offs, out_0, out_1):
@@ -154,7 +153,7 @@ def tile_attend_gsqh_wx_ts_kernel(tc, xT, wT, y, wt, ts, xm, offs, out_0, out_1)
         h_il = [sb(f"h_il{g}", [P, N, 4], BF16) for g in range(G)]
         margin = [sb("margin0", [P, 4, N], F32), None]
         x_q = [mx_tiles(f"x{g}") for g in range(G)]
-        xm_q = [[None, None] for g in range(G)]
+        xm_q = {}
         h_q = [None] * G
         w_q = mx_tiles("w")
         on_scalar, on_vector = nc.scalar.copy, nc.vector.tensor_copy
@@ -177,7 +176,7 @@ def tile_attend_gsqh_wx_ts_kernel(tc, xT, wT, y, wt, ts, xm, offs, out_0, out_1)
                 source = xm_raw0[:, :, block(b)]
             else:
                 source = xm_rest[:, :, block(b - 1)] if b else xm_first[:]
-            if g == 0 or b < 2:
+            if b < 3:
                 interleave(on_scalar, xm_il[g, b], source, 0, P)
             else:
                 nc.gpsimd.tensor_scalar(xm_il[g, b], source.rearrange("p t d -> p d t"), 1.0, 0.0, MULT, ADD)
@@ -189,9 +188,8 @@ def tile_attend_gsqh_wx_ts_kernel(tc, xT, wT, y, wt, ts, xm, offs, out_0, out_1)
             xm_il[g, lo, hi] = tile[:]
 
         def quantise_xm(g, lo, hi):
-            source = xm_il[g, lo, hi].rearrange("p d t -> p (d t)")
-            first = max(lo - 1, 0)
-            quantise(xm_q[g][min(lo, 1)], slice(first * P, (first + hi - lo) * P), source, E4)
+            operand, k = xm_q[g, lo]
+            quantise(operand, slice(k * P, (k + hi - lo) * P), xm_il[g, lo, hi].rearrange("p d t -> p (d t)"), E4)
 
         def quantise_h(g, tag=None):
             h_q[g] = mx_tiles(f"h{g}", tag)
@@ -231,9 +229,9 @@ def tile_attend_gsqh_wx_ts_kernel(tc, xT, wT, y, wt, ts, xm, offs, out_0, out_1)
                 dw_ps[b] = ps_dw.tile([P, N], F32, name=f"dw_ps{b}", tag=f"dw_bank{b}")
             elif g == 0:
                 dw_ps[b] = ps_turn.tile([P, N], F32, name="turn")
-            mx(dw_ps[b][:], xm_q[g][min(b, 1)], max(b - 1, 0), E4, h_q[g], E5, g == 0, g == G - 1)
+            mx(dw_ps[b][:], *xm_q[g, b], E4, h_q[g], E5, g == 0, g == G - 1)
 
-        ws_il = [sb("ws_il0", [P, 2, P, 2], F32), sb("ws_il1", [P, 2, P, 2], F32, "x_raw0")]
+        ws_il = [sb("ws_il0", [P, 2, P, 2], F32), sb("ws_il1", [P, 2, P, 2], F32)]
         ws_q = mx_tiles("ws")
         hs_il = [None] * G
         hs_q = [None, mx_tiles("hs1")]
@@ -280,16 +278,15 @@ def tile_attend_gsqh_wx_ts_kernel(tc, xT, wT, y, wt, ts, xm, offs, out_0, out_1)
             slots = slice(half * HALF, (half + 1) * HALF)
             quantise(w_q, slots, w_il[:, slots, :].rearrange("p i j -> p (i j)"), E4)
         x_interleave(on_vector, 0, 0, 0, P)
-        x_interleave(on_scalar, 0, 1, X_SPLIT, P)
-        x_interleave(on_vector, 0, 1, 0, X_SPLIT)
+        turn_w(1)
+        x_interleave(on_scalar, 0, 1, 0, P)
+        quantise_ws(1)
 
         def quantise_x(g, pair):
             quantise(x_q[g], halves[pair], x_il[g, pair][:].rearrange("p t m j -> p (t m j)"), E4)
 
         quantise_x(0, 0)
         quantise_x(0, 1)
-        turn_w(1)
-        quantise_ws(1)
 
         for pair in range(2):
             for t in (2 * pair, 2 * pair + 1):
@@ -310,24 +307,27 @@ def tile_attend_gsqh_wx_ts_kernel(tc, xT, wT, y, wt, ts, xm, offs, out_0, out_1)
         gradient(0)
 
         quantise_x(1, 1)
-        for lo, hi in ((0, 1), (1, 3)):
+        for lo, hi in ((0, 2), (2, 3)):
             xm_tile(0, lo, hi)
-        for b in range(3):
-            xm_interleave(0, b)
+        interleave(on_scalar, xm_il[0, 0, 2], xm_raw0, 0, 2 * P)
+        xm_interleave(0, 2)
         xm_tile(1, 0, 1)
         xm_interleave(1, 0)
         margin[1] = sb("margin1", [P, 4, N], F32, "xm_first")
-        xm_tile(1, 2, 4, "margin0")
-        for b in range(2, 4):
-            xm_interleave(1, b)
+        last_blocks = sb("xm_il_last", [P, G, P, 4], BF16, "margin0")
+        for g in range(G):
+            xm_il[g, 3] = xm_il[g, 3, 4] = last_blocks[:, g]
+            xm_interleave(g, 3)
         for t in range(4):
             scores(1, t)
         quantise_h(0, "last_wt0")
-        firsts = mx_tiles("xm_firsts", "last_wt1", 2 * P)
-        for g in range(G):
-            xm_q[g][0] = (firsts[0][:, block(g)], firsts[1][:, block(g)])
-            quantise_xm(g, 0, 1)
+        early = mx_tiles("xm_early", "last_wt1", 3 * P)
+        for k, key in enumerate(((0, 0), (0, 1), (1, 0))):
+            xm_q[key] = (early, k)
+        quantise_xm(0, 0, 2)
+        quantise_xm(1, 0, 1)
         dw_pass(0, 0)
+        dw_pass(0, 1)
         gradient(1)
         quantise_h(1)
 
@@ -357,22 +357,20 @@ def tile_attend_gsqh_wx_ts_kernel(tc, xT, wT, y, wt, ts, xm, offs, out_0, out_1)
             nc.scalar.dma_start(gx_view[g][:, 2 * pair : 2 * pair + 2, :], gx[:])
 
         turn_h(0, "ts_runs")
-        xm_tile(1, 1, 2, "last_z1")
-        xm_interleave(1, 1)
-        xm_tile(0, 3, 4, "last_z0")
-        xm_interleave(0, 3)
+        xm_tile(1, 1, 3, "last_z1")
+        interleave(on_scalar, xm_il[1, 1, 3], xm_rest, 0, 2 * P)
         finish_dw(0)
         hs_q[0] = mx_tiles("hs0", "y_sb1")
         quantise_hs(0)
-        xm_q[0][1] = mx_tiles("xm0_rest", "xm_first", D - P)
-        quantise_xm(0, 1, 3)
-        xm_q[1][1] = mx_tiles("xm1_rest", "xm_firsts_scales", D - P)
-        quantise_xm(1, 1, 2)
-        quantise_xm(1, 2, 4)
+        late = mx_tiles("xm_late", "xm_first", 5 * P)
+        for k, key in enumerate(((0, 2), (0, 3), (1, 1), (1, 2), (1, 3))):
+            xm_q[key] = (late, k)
+        quantise_xm(0, 2, 3)
         quantise_xm(0, 3, 4)
+        quantise_xm(1, 3, 4)
+        quantise_xm(1, 1, 3)
         scatter(0)
         rows_out(0, 0)
-        dw_pass(0, 1)
         finish_dw(1)
         for b in range(2, 4):
             dw_pass(0, b)

@@ -25,6 +25,8 @@ P = 128
 PASS = 512
 G = R // PASS
 HALF = PASS // 2
+FROM_PSUM = ((0, 2), (0, 3), (1, 0))
+PAIR_BYTES = 2 * P * 4 * 2
 WINDOWS = 3
 LIST_ROWS = 16
 
@@ -33,6 +35,7 @@ def tile_attend_gsqh_wx_ts_kernel(tc, xT, wT, y, wt, ts, xm, offs, out_0, out_1)
     nc = tc.nc
     with ExitStack() as ctx:
         keep = ctx.enter_context(tc.tile_pool(name="keep", bufs=1))
+        placed = ctx.enter_context(tc.tile_pool(name="placed", bufs=1))
         ring = ctx.enter_context(tc.tile_pool(name="ring", bufs=3))
         ps_lone = ctx.enter_context(tc.psum_pool(name="ps_lone", bufs=4))
         ps_turn = ctx.enter_context(tc.psum_pool(name="ps_turn", bufs=2))
@@ -115,10 +118,9 @@ def tile_attend_gsqh_wx_ts_kernel(tc, xT, wT, y, wt, ts, xm, offs, out_0, out_1)
         nc.vector.tensor_scalar(all_signs[:], wt_step[:], 1.0, None, ADD)
         minus_sign = {(g, t): all_signs[:, g, t : t + 1] for g in range(G) for t in range(4)}
 
-        for t in (0, 2):
-            early = sb(f"early_sign{t}", [P, 1], F32)
-            nc.vector.tensor_copy(early[:], minus_sign[0, t])
-            minus_sign[0, t] = early[:]
+        first_sign = placed.tile([P, 1], F32, name="first_sign", offset=PAIR_BYTES, align_bytes=64)
+        nc.vector.tensor_copy(first_sign[:], minus_sign[0, 0])
+        minus_sign[0, 0] = first_sign[:]
         last_wt = [sb(f"last_wt{half}", [P, 1], F32) for half in range(2)]
         for weight in last_wt:
             nc.vector.tensor_copy(weight[:], wt_sb[:, G - 1, 3:4])
@@ -146,9 +148,19 @@ def tile_attend_gsqh_wx_ts_kernel(tc, xT, wT, y, wt, ts, xm, offs, out_0, out_1)
         for t in (2, 3):
             nc.scalar.activation(signed[t][:], ts_all[:], COPY, scale=minus_sign[1, t])
 
-        x_il = {(g, pair): sb(f"x_il{g}_{pair}", [P, 2, P, 4], BF16) for g, pair in ((0, 0), (0, 1), (1, 0))}
+        bank = ps_turn.tile([P, 4, P], F32, name="turn")
+        for k in range(4):
+            nc.tensor.transpose(bank[:, k, :], ts_all[:, block(k)], ident[:])
+        ts_columns = sb("ts_columns", [P, 4], F32)
+        nc.scalar.copy(ts_columns[:], bank[:, :, 0])
+        sign_rows = ps_turn.tile([P, len(FROM_PSUM), P], F32, name="turn")
+        signed_bank = {}
+        for s, key in enumerate(FROM_PSUM):
+            nc.tensor.transpose(sign_rows[:, s, :], minus_sign[key].to_broadcast([P, P]), ident[:])
+
+        x_il = {(g, pair): sb(f"x_il{g}_{pair}", [P, 2, P, 4], BF16) for g, pair in ((0, 0), (1, 0))}
+        x_il[0, 1] = placed.tile([P, 2, P, 4], BF16, name="x_il0_1", offset=0, align_bytes=64)
         factors = y_sb
-        unit = [None, None]
         xm_il = {}
         h_il = [sb(f"h_il{g}", [P, N, 4], BF16) for g in range(G)]
         margin = [sb("margin0", [P, 4, N], F32), None]
@@ -197,7 +209,11 @@ def tile_attend_gsqh_wx_ts_kernel(tc, xT, wT, y, wt, ts, xm, offs, out_0, out_1)
                 quantise(h_q[g], cols, h_il[g][:, cols, :].rearrange("p i t -> p (i t)"), E5)
 
         def factor(g, t):
-            nc.vector.scalar_tensor_tensor(factors[g][:, t, :], y_sb[g][:, t, :], minus_sign[g, t], ts_all[:], MULT, MULT)
+            c = y_sb[g][:, t, :]
+            if (g, t) in FROM_PSUM:
+                nc.vector.tensor_tensor(c, signed_bank[g, t][:], c, MULT)
+            else:
+                nc.vector.scalar_tensor_tensor(c, c, minus_sign[g, t], ts_all[:], MULT, MULT)
 
         def scores(g, t):
             sums = ps_lone.tile([P, N], F32, name="lone")
@@ -211,7 +227,7 @@ def tile_attend_gsqh_wx_ts_kernel(tc, xT, wT, y, wt, ts, xm, offs, out_0, out_1)
             for half, cols in enumerate(halves):
                 z = sb(f"last_z{half}", [P, HALF], F32)
                 nc.vector.scalar_tensor_tensor(z[:], sums[:, cols], last_wt[half][:], factors[g][:, t, cols], MULT, MULT)
-                nc.scalar.activation(margin[g][:, t, cols], z[:], RELU, bias=size, scale=unit[half][:])
+                nc.scalar.activation(margin[g][:, t, cols], z[:], RELU, bias=size, scale=unit)
 
         def gradient(g):
             for cols in halves if g == G - 1 else (whole,):
@@ -288,17 +304,29 @@ def tile_attend_gsqh_wx_ts_kernel(tc, xT, wT, y, wt, ts, xm, offs, out_0, out_1)
         quantise_x(0, 0)
         quantise_x(0, 1)
 
-        for pair in range(2):
-            for t in (2 * pair, 2 * pair + 1):
-                factor(0, t)
-            unit[pair] = sb(f"unit{pair}", [P, 1], F32, f"early_sign{2 * pair}")
-            nc.gpsimd.memset(unit[pair][:], 1.0)
-            c = y_sb[1][:, 2 + pair, :]
-            nc.gpsimd.tensor_tensor(c, c, signed[2 + pair][:], MULT)
-            if pair == 1:
-                x_interleave(on_scalar, 1, 0, 0, P)
-            for t in (2 * pair, 2 * pair + 1):
-                scores(0, t)
+        factor(0, 0)
+        factor(0, 1)
+        unit = placed.tile([P, 17], F32, name="unit", offset=PAIR_BYTES - 64, align_bytes=64)[:, 16:17]
+        nc.gpsimd.memset(unit, 1.0)
+        for t in (2, 3):
+            nc.gpsimd.tensor_tensor(y_sb[1][:, t, :], y_sb[1][:, t, :], signed[t][:], MULT)
+        turned = sb("signed_turned", [P, 4, len(FROM_PSUM), P], F32, "x_raw0")
+        for k in range(4):
+            nc.scalar.activation(turned[:, k], sign_rows[:], COPY, scale=ts_columns[:, k : k + 1])
+        for s, key in enumerate(FROM_PSUM):
+            if s < 2:
+                signed_bank[key] = ps_dw.tile([P, N], F32, name=f"signed_bank{s}", tag=f"dw_bank{s}")
+            else:
+                signed_bank[key] = ps_turn.tile([P, N], F32, name="turn")
+            for k in range(4):
+                nc.tensor.transpose(signed_bank[key][:, block(k)], turned[:, k, s, :], ident[:])
+        scores(0, 0)
+        scores(0, 1)
+        factor(0, 2)
+        factor(0, 3)
+        x_interleave(on_scalar, 1, 0, 0, P)
+        scores(0, 2)
+        scores(0, 3)
         x_il[1, 1] = sb("x_il1_1", [P, 2, P, 4], BF16, "z0_3")
         x_interleave(on_scalar, 1, 1, 0, P)
         factor(1, 0)

@@ -26,7 +26,6 @@ PASS = 512
 G = R // PASS
 HALF = PASS // 2
 FROM_PSUM = ((0, 2), (0, 3), (1, 0))
-PAIR_BYTES = 2 * P * 4 * 2
 WINDOWS = 3
 LIST_ROWS = 16
 
@@ -35,7 +34,6 @@ def tile_attend_gsqh_wx_ts_kernel(tc, xT, wT, y, wt, ts, xm, offs, out_0, out_1)
     nc = tc.nc
     with ExitStack() as ctx:
         keep = ctx.enter_context(tc.tile_pool(name="keep", bufs=1))
-        placed = ctx.enter_context(tc.tile_pool(name="placed", bufs=1))
         ring = ctx.enter_context(tc.tile_pool(name="ring", bufs=3))
         ps_lone = ctx.enter_context(tc.psum_pool(name="ps_lone", bufs=4))
         ps_turn = ctx.enter_context(tc.psum_pool(name="ps_turn", bufs=2))
@@ -118,9 +116,6 @@ def tile_attend_gsqh_wx_ts_kernel(tc, xT, wT, y, wt, ts, xm, offs, out_0, out_1)
         nc.vector.tensor_scalar(all_signs[:], wt_step[:], 1.0, None, ADD)
         minus_sign = {(g, t): all_signs[:, g, t : t + 1] for g in range(G) for t in range(4)}
 
-        first_sign = placed.tile([P, 1], F32, name="first_sign", offset=PAIR_BYTES, align_bytes=64)
-        nc.vector.tensor_copy(first_sign[:], minus_sign[0, 0])
-        minus_sign[0, 0] = first_sign[:]
         last_wt = [sb(f"last_wt{half}", [P, 1], F32) for half in range(2)]
         for weight in last_wt:
             nc.vector.tensor_copy(weight[:], wt_sb[:, G - 1, 3:4])
@@ -158,9 +153,8 @@ def tile_attend_gsqh_wx_ts_kernel(tc, xT, wT, y, wt, ts, xm, offs, out_0, out_1)
         for s, key in enumerate(FROM_PSUM):
             nc.tensor.transpose(sign_rows[:, s, :], minus_sign[key].to_broadcast([P, P]), ident[:])
 
-        x_il = {(g, pair): sb(f"x_il{g}_{pair}", [P, 2, P, 4], BF16) for g, pair in ((0, 0), (1, 0))}
-        x_il[0, 1] = placed.tile([P, 2, P, 4], BF16, name="x_il0_1", offset=0, align_bytes=64)
-        factors = y_sb
+        x_il = {(g, pair): sb(f"x_il{g}_{pair}", [P, 2, P, 4], BF16) for g, pair in ((0, 0), (0, 1), (1, 0))}
+        factors = [y_sb[0], None]
         xm_il = {}
         h_il = [sb(f"h_il{g}", [P, N, 4], BF16) for g in range(G)]
         margin = [sb("margin0", [P, 4, N], F32), None]
@@ -209,11 +203,11 @@ def tile_attend_gsqh_wx_ts_kernel(tc, xT, wT, y, wt, ts, xm, offs, out_0, out_1)
                 quantise(h_q[g], cols, h_il[g][:, cols, :].rearrange("p i t -> p (i t)"), E5)
 
         def factor(g, t):
-            c = y_sb[g][:, t, :]
+            c, labels = factors[g][:, t, :], y_sb[g][:, t, :]
             if (g, t) in FROM_PSUM:
-                nc.vector.tensor_tensor(c, signed_bank[g, t][:], c, MULT)
+                nc.vector.tensor_tensor(c, signed_bank[g, t][:], labels, MULT)
             else:
-                nc.vector.scalar_tensor_tensor(c, c, minus_sign[g, t], ts_all[:], MULT, MULT)
+                nc.vector.scalar_tensor_tensor(c, labels, minus_sign[g, t], ts_all[:], MULT, MULT)
 
         def scores(g, t):
             sums = ps_lone.tile([P, N], F32, name="lone")
@@ -227,7 +221,7 @@ def tile_attend_gsqh_wx_ts_kernel(tc, xT, wT, y, wt, ts, xm, offs, out_0, out_1)
             for half, cols in enumerate(halves):
                 z = sb(f"last_z{half}", [P, HALF], F32)
                 nc.vector.scalar_tensor_tensor(z[:], sums[:, cols], last_wt[half][:], factors[g][:, t, cols], MULT, MULT)
-                nc.scalar.activation(margin[g][:, t, cols], z[:], RELU, bias=size, scale=unit)
+                nc.scalar.activation(margin[g][:, t, cols], z[:], RELU, bias=size)
 
         def gradient(g):
             for cols in halves if g == G - 1 else (whole,):
@@ -306,10 +300,9 @@ def tile_attend_gsqh_wx_ts_kernel(tc, xT, wT, y, wt, ts, xm, offs, out_0, out_1)
 
         factor(0, 0)
         factor(0, 1)
-        unit = placed.tile([P, 17], F32, name="unit", offset=PAIR_BYTES - 64, align_bytes=64)[:, 16:17]
-        nc.gpsimd.memset(unit, 1.0)
+        factors[1] = sb("factors1", [P, 4, N], F32, "x_il0_1")
         for t in (2, 3):
-            nc.gpsimd.tensor_tensor(y_sb[1][:, t, :], y_sb[1][:, t, :], signed[t][:], MULT)
+            nc.gpsimd.tensor_tensor(factors[1][:, t, :], y_sb[1][:, t, :], signed[t][:], MULT)
         turned = sb("signed_turned", [P, 4, len(FROM_PSUM), P], F32, "x_raw0")
         for k in range(4):
             nc.scalar.activation(turned[:, k], sign_rows[:], COPY, scale=ts_columns[:, k : k + 1])
@@ -388,7 +381,7 @@ def tile_attend_gsqh_wx_ts_kernel(tc, xT, wT, y, wt, ts, xm, offs, out_0, out_1)
         xm_tile(1, 1, 3, "last_z1")
         interleave(on_scalar, xm_il[1, 1, 3], xm_rest, 0, 2 * P)
         finish_dw(0)
-        hs_q[0] = mx_tiles("hs0", "y_sb1")
+        hs_q[0] = mx_tiles("hs0", "x_il0_1")
         quantise_hs(0)
         late = mx_tiles("xm_late", "xm_first", 5 * P)
         for k, key in enumerate(((0, 2), (0, 3), (1, 1), (1, 2), (1, 3))):

@@ -25,7 +25,7 @@ P = 128
 PASS = 512
 G = R // PASS
 HALF = PASS // 2
-FROM_PSUM = ((0, 2), (0, 3), (1, 0))
+ON_GPSIMD = ((0, 3), (1, 0), (1, 1), (1, 3))
 WINDOWS = 3
 LIST_ROWS = 16
 
@@ -34,10 +34,10 @@ def tile_attend_gsqh_wx_ts_kernel(tc, xT, wT, y, wt, ts, xm, offs, out_0, out_1)
     nc = tc.nc
     with ExitStack() as ctx:
         keep = ctx.enter_context(tc.tile_pool(name="keep", bufs=1))
-        ring = ctx.enter_context(tc.tile_pool(name="ring", bufs=3))
-        ps_lone = ctx.enter_context(tc.psum_pool(name="ps_lone", bufs=4))
-        ps_turn = ctx.enter_context(tc.psum_pool(name="ps_turn", bufs=2))
-        ps_dw = ctx.enter_context(tc.psum_pool(name="ps_dw", bufs=1))
+        psum = ctx.enter_context(tc.psum_pool(name="psum", bufs=1))
+
+        def in_bank(b, name, shape):
+            return psum.tile(shape, F32, name=name, tag=f"bank{b}")
 
         def sb(name, shape, dtype, tag=None):
             return keep.tile(shape, dtype, name=name, tag=tag or name, align_bytes=64)
@@ -48,28 +48,36 @@ def tile_attend_gsqh_wx_ts_kernel(tc, xT, wT, y, wt, ts, xm, offs, out_0, out_1)
         def quantise(dst, cols, src, fmt):
             nc.vector.quantize_mx(out=dst[0][:, cols].bitcast(fmt), scales=dst[1][:, cols], in_=src)
 
-        def block(k):
-            return slice(k * P, (k + 1) * P)
+        def block(k, count=1):
+            return slice(k * P, (k + count) * P)
 
-        def mx(out, lhs, k, lhs_fmt, rhs, rhs_fmt, start, stop):
+        def mx(out, lhs, k, lhs_fmt, rhs, rhs_fmt, start, stop, cols=slice(0, PASS)):
             nc.tensor.matmul_mx(
                 out=out,
                 lhsT=lhs[0][:, block(k)].bitcast(lhs_fmt),
                 lhsT_scale=lhs[1][:, block(k)],
-                rhs=rhs[0][:].bitcast(rhs_fmt),
-                rhs_scale=rhs[1][:],
+                rhs=rhs[0][:, cols].bitcast(rhs_fmt),
+                rhs_scale=rhs[1][:, cols],
                 start=start,
                 stop=stop,
             )
 
+        def part(lo, hi):
+            return offsets[:, lo // LIST_ROWS : hi // LIST_ROWS]
+
         whole = slice(0, PASS)
         halves = (slice(0, HALF), slice(HALF, PASS))
+        on_scalar, on_vector = nc.scalar.copy, nc.vector.tensor_copy
+
+        def on_gpsimd(dst, src):
+            nc.gpsimd.tensor_scalar(dst, src, 1.0, 0.0, MULT, ADD)
 
         offsets = keep.tile([P, N // LIST_ROWS], U16, name="offsets")
         w_planes = [sb(f"w_plane{j}", [P, T], F32) for j in range(4)]
-        x_raw = [sb(f"x_raw{g}", [P, 4, PASS], F32) for g in range(G)]
+        x0_raw = [sb(f"x0_raw{half}", [P, 4, HALF], F32) for half in range(2)]
+        x1_raw = sb("x1_raw", [P, 4, PASS], F32)
         y_sb = [sb(f"y_sb{g}", [P, 4, N], F32) for g in range(G)]
-        xm_raw0 = sb("xm_raw0", [P, 4, D], F32)
+        xm0_raw = [sb(f"xm0_raw{half}", [P, 4, HALF], F32) for half in range(2)]
         xm_first = sb("xm_first", [P, 4, P], F32)
         xm_rest = sb("xm_rest", [P, 4, D - P], F32)
         wt_sb = sb("wt_sb", [P, G, 4], F32)
@@ -89,16 +97,17 @@ def tile_attend_gsqh_wx_ts_kernel(tc, xT, wT, y, wt, ts, xm, offs, out_0, out_1)
         nc.sync.dma_start(offsets[:], offs)
         for j in range(1, 4):
             nc.sync.dma_start(w_planes[j][:], w_view[j])
-        nc.sync.dma_start(x_raw[0][:], x_view[0])
+        for half in range(2):
+            nc.sync.dma_start(x0_raw[half][:], x_view[0][:, :, halves[half]])
         nc.sync.dma_start(y_sb[0][:, 0:2, :], y_view[0][:, 0:2, :])
         nc.sync.dma_start(y_sb[0][:, 2:4, :], y_view[0][:, 2:4, :])
-        nc.sync.dma_start(y_sb[1][:, 2, :], y_view[1][:, 2, :])
-        nc.sync.dma_start(x_raw[1][:], x_view[1])
-        nc.sync.dma_start(y_sb[1][:, 3, :], y_view[1][:, 3, :])
         nc.sync.dma_start(y_sb[1][:, 0:2, :], y_view[1][:, 0:2, :])
-        nc.sync.dma_start(xm_raw0[:], xm_view[0])
+        nc.sync.dma_start(x1_raw[:], x_view[1])
+        nc.sync.dma_start(y_sb[1][:, 2:4, :], y_view[1][:, 2:4, :])
+        nc.sync.dma_start(xm0_raw[0][:], xm_view[0][:, :, halves[0]])
         nc.sync.dma_start(xm_first[:], xm_view[1][:, :, 0:P])
         nc.sync.dma_start(xm_rest[:], xm_view[1][:, :, P:D])
+        nc.sync.dma_start(xm0_raw[1][:], xm_view[0][:, :, halves[1]])
 
         zeros = sb("zeros", [P, P], F32, "window2")
         nc.gpsimd.memset(zeros[:], 0.0)
@@ -111,18 +120,17 @@ def tile_attend_gsqh_wx_ts_kernel(tc, xT, wT, y, wt, ts, xm, offs, out_0, out_1)
             nc.vector.memset(window[:].bitcast(I32), 0)
 
         wt_step = sb("wt_step", [P, G, 4], F32)
-        all_signs = sb("all_signs", [P, G, 4], F32)
+        minus_sign = sb("minus_sign", [P, G, 4], F32)
         nc.vector.tensor_scalar(wt_step[:], wt_sb[:], 0.0, -2.0, IS_GE, MULT)
-        nc.vector.tensor_scalar(all_signs[:], wt_step[:], 1.0, None, ADD)
-        minus_sign = {(g, t): all_signs[:, g, t : t + 1] for g in range(G) for t in range(4)}
+        nc.vector.tensor_scalar(minus_sign[:], wt_step[:], 1.0, None, ADD)
 
-        last_wt = [sb(f"last_wt{half}", [P, 1], F32) for half in range(2)]
-        for weight in last_wt:
-            nc.vector.tensor_copy(weight[:], wt_sb[:, G - 1, 3:4])
+        last_wt = [sb(f"last_wt{g}", [P, 1], F32) for g in range(G)]
+        for g in range(G):
+            nc.vector.tensor_copy(last_wt[g][:], wt_sb[:, g, 3:4])
 
         table_view = ts_table[:].rearrange("p (n k e) -> p k n e", k=4, e=4)
         for k in range(4):
-            bank = ps_lone.tile([P, 4, P], F32, name="lone")
+            bank = in_bank(k, f"spread{k}", [P, 4, P])
             for e in range(4):
                 column = ts_runs[:, 4 * k + e : 4 * k + e + 1]
                 nc.tensor.transpose(bank[:, e, :], column.to_broadcast([P, P]), ident[:])
@@ -131,277 +139,252 @@ def tile_attend_gsqh_wx_ts_kernel(tc, xT, wT, y, wt, ts, xm, offs, out_0, out_1)
         wt_abs = sb("wt_abs", [P, G, 4], F32, "ts_runs")
         nc.scalar.activation(wt_abs[:], wt_sb[:], ABS)
 
-        w_il = sb("w_il", [P, N, 4], BF16)
         ts_all = sb("ts_all", [P, N], F32)
-        nc.vector.tensor_copy(ts_all[:], ts_table[:].indirect(offsets[:]))
+        nc.scalar.activation(ts_all[:], ts_table[:].indirect(offsets[:]), COPY)
         w_flat = sb("w_bf", [P, 4 * N], BF16, "ts_table")
         w_bf = w_flat[:].rearrange("p (j i) -> p j i", j=4)
         for j in range(3):
             nc.vector.tensor_copy(w_bf[:, j, :], w_planes[j][:].indirect(offsets[:]))
 
-        signed = {t: sb(f"signed{t}", [P, N], F32) for t in (2, 3)}
-        for t in (2, 3):
-            nc.scalar.activation(signed[t][:], ts_all[:], COPY, scale=minus_sign[1, t])
-
-        bank = ps_turn.tile([P, 4, P], F32, name="turn")
+        bank = in_bank(4, "ts_turned", [P, 4, P])
         for k in range(4):
             nc.tensor.transpose(bank[:, k, :], ts_all[:, block(k)], ident[:])
         ts_columns = sb("ts_columns", [P, 4], F32)
         nc.scalar.copy(ts_columns[:], bank[:, :, 0])
-        sign_rows = ps_turn.tile([P, len(FROM_PSUM), P], F32, name="turn")
-        signed_bank = {}
-        for s, key in enumerate(FROM_PSUM):
-            nc.tensor.transpose(sign_rows[:, s, :], minus_sign[key].to_broadcast([P, P]), ident[:])
+        ts_bank = in_bank(6, "ts_bank", [P, N])
+        for k in range(4):
+            nc.tensor.transpose(ts_bank[:, block(k)], ts_columns[:, k : k + 1].to_broadcast([P, P]), ident[:])
+        signed = {}
+        for g, t in ON_GPSIMD:
+            signed[g, t] = sb(f"signed{g}_{t}", [P, N], F32)
+            nc.gpsimd.tensor_scalar(signed[g, t][:], ts_all[:], minus_sign[:, g, t : t + 1], 0.0, MULT, ADD)
 
-        x_il = {(g, pair): sb(f"x_il{g}_{pair}", [P, 2, P, 4], BF16) for g, pair in ((0, 0), (0, 1), (1, 0))}
-        factors = [y_sb[0], None]
-        xm_il = {}
-        h_il = [sb(f"h_il{g}", [P, N, 4], BF16) for g in range(G)]
-        margin = [sb("margin0", [P, 4, N], F32), None]
+        w_il = sb("w_il", [P, N, 4], BF16)
+        ws_il = [None, None]
+        x0_il = sb("x0_il", [P, 4, P, 4], BF16)
+        factors1 = sb("factors1", [P, 4 * N], F32)
+        factors = [None, factors1[:].rearrange("p (t i) -> p t i", t=4)]
+        x1_il = [None, factors1[:, 3 * N : 4 * N].bitcast(BF16)]
+        h_il = [sb("h_il0", [P, N, 4], BF16)[:], None]
+        margin = [sb("margin0", [P, 4, N], F32, "w_plane0"), None]
         x_q = [mx_tiles(f"x{g}") for g in range(G)]
-        xm_q = {}
-        h_q = [None] * G
         w_q = mx_tiles("w")
-        on_scalar, on_vector = nc.scalar.copy, nc.vector.tensor_copy
-
-        def x_interleave(copy, g, pair, lo, hi):
-            tiles = slice(2 * pair, 2 * pair + 2)
-            copy(
-                x_il[g, pair][:].rearrange("p t m j -> p m j t")[:, lo:hi],
-                x_raw[g][:].rearrange("p j (m t) -> p m j t", t=4)[:, lo:hi, :, tiles],
-            )
+        h_q = [None] * G
+        hs_il = {}
+        hs_q = [None] * G
+        xm_q = {}
 
         def interleave(copy, dst, src, lo, hi):
             copy(
-                dst[:].rearrange("p (c i) t -> p c t i", i=4)[:, lo // 4 : hi // 4],
-                src[:].rearrange("p t (c i) -> p c t i", i=4)[:, lo // 4 : hi // 4],
+                dst.rearrange("p (c i) t -> p c t i", i=4)[:, lo // 4 : hi // 4],
+                src.rearrange("p t (c i) -> p c t i", i=4)[:, lo // 4 : hi // 4],
             )
 
-        def xm_interleave(g, b):
-            if g == 0:
-                source = xm_raw0[:, :, block(b)]
-            else:
-                source = xm_rest[:, :, block(b - 1)] if b else xm_first[:]
-            if b < 3:
-                interleave(on_scalar, xm_il[g, b], source, 0, P)
-            else:
-                nc.gpsimd.tensor_scalar(xm_il[g, b], source.rearrange("p t d -> p d t"), 1.0, 0.0, MULT, ADD)
-
-        def xm_tile(g, lo, hi, tag=None):
-            tile = sb(f"xm_il{g}_{lo}", [P, (hi - lo) * P, 4], BF16, tag)
-            for b in range(lo, hi):
-                xm_il[g, b] = tile[:, block(b - lo), :]
-            xm_il[g, lo, hi] = tile[:]
-
-        def quantise_xm(g, lo, hi):
-            operand, k = xm_q[g, lo]
-            quantise(operand, slice(k * P, (k + hi - lo) * P), xm_il[g, lo, hi].rearrange("p d t -> p (d t)"), E4)
-
-        def quantise_h(g, tag=None):
-            h_q[g] = mx_tiles(f"h{g}", tag)
-            for cols in halves if g == G - 1 else (whole,):
-                quantise(h_q[g], cols, h_il[g][:, cols, :].rearrange("p i t -> p (i t)"), E5)
-
-        def factor(g, t):
-            c, labels = factors[g][:, t, :], y_sb[g][:, t, :]
-            if (g, t) in FROM_PSUM:
-                nc.vector.tensor_tensor(c, signed_bank[g, t][:], labels, MULT)
-            else:
-                nc.vector.scalar_tensor_tensor(c, labels, minus_sign[g, t], ts_all[:], MULT, MULT)
-
-        def scores(g, t):
-            sums = ps_lone.tile([P, N], F32, name="lone")
-            mx(sums[:], x_q[g], t, E4, w_q, E4, True, True)
-            size = wt_abs[:, g, t : t + 1]
-            if (g, t) != (G - 1, 3):
-                z = sb("z0_3", [P, N], F32) if t == 3 else ring.tile([P, N], F32, name="z", bufs=3)
-                nc.vector.tensor_tensor(z[:], sums[:], factors[g][:, t, :], MULT)
-                nc.scalar.activation(margin[g][:, t, :], z[:], RELU, bias=size, scale=wt_sb[:, g, t : t + 1])
-                return
-            for half, cols in enumerate(halves):
-                z = sb(f"last_z{half}", [P, HALF], F32)
-                nc.vector.scalar_tensor_tensor(z[:], sums[:, cols], last_wt[half][:], factors[g][:, t, cols], MULT, MULT)
-                nc.scalar.activation(margin[g][:, t, cols], z[:], RELU, bias=size)
-
-        def gradient(g):
-            for cols in halves if g == G - 1 else (whole,):
-                nc.vector.tensor_tensor(
-                    h_il[g][:, cols, :].rearrange("p (c i) t -> p c t i", i=2),
-                    margin[g][:, :, cols].rearrange("p t (c i) -> p c t i", i=2),
-                    factors[g][:, :, cols].rearrange("p t (c i) -> p c t i", i=2),
-                    MULT,
-                )
-
-        dw_ps = [None] * 4
-
-        def dw_pass(g, b):
-            if g == 0 and b < 2:
-                dw_ps[b] = ps_dw.tile([P, N], F32, name=f"dw_ps{b}", tag=f"dw_bank{b}")
-            elif g == 0:
-                dw_ps[b] = ps_turn.tile([P, N], F32, name="turn")
-            mx(dw_ps[b][:], *xm_q[g, b], E4, h_q[g], E5, g == 0, g == G - 1)
-
-        ws_il = [sb("ws_il0", [P, 2, P, 2], F32), sb("ws_il1", [P, 2, P, 2], F32)]
-        ws_q = mx_tiles("ws")
-        hs_il = [None] * G
-        hs_q = [None, mx_tiles("hs1")]
+        def x_interleave(copy, dst, src):
+            copy(dst.rearrange("p t m j -> p m j t"), src.rearrange("p j m t -> p m j t"))
 
         def turn_w(half):
-            bank = ps_turn.tile([P, 2, 2, P], F32, name="turn")
+            bank = in_bank(5 - half, f"w_turned{half}", [P, 2, 2, P])
             for s in range(2):
                 words = w_bf[:, 2 * half + s, :].bitcast(F32)
                 for u in range(2):
                     nc.tensor.transpose(bank[:, s, u, :], words[:, u : N // 2 : 2], ident[:])
             nc.scalar.copy(ws_il[half][:], bank[:].rearrange("p s u q -> p s q u"))
 
-        def quantise_ws(half):
-            cols = slice(half * HALF, (half + 1) * HALF)
-            quantise(ws_q, cols, ws_il[half][:].rearrange("p j q u -> p (j q u)").bitcast(BF16), E4)
-
-        def turn_h(g, tag=None):
-            hs_il[g] = sb(f"hs_il{g}", [P, 2, 2, P, 4], BF16, tag)
-            words = h_il[g][:].rearrange("p i t -> p (i t)").bitcast(F32)
-            for u in range(2):
-                if g == G - 1:
-                    bank = ps_dw.tile([P, 4, P], F32, name="turn_h", tag=f"dw_bank{u}")
-                else:
-                    bank = ps_lone.tile([P, 4, P], F32, name="lone")
-                for e in range(4):
-                    nc.tensor.transpose(bank[:, e, :], words[:, 2 * e + u : 2 * N : 8], ident[:])
-                nc.scalar.copy(
-                    hs_il[g][:, u],
-                    bank[:].rearrange("p e q -> p (e q)").bitcast(BF16).rearrange("p (e q v) -> p v q e", e=4, v=2),
-                )
-
-        def quantise_hs(g):
-            quantise(hs_q[g], whole, hs_il[g][:].rearrange("p u v q e -> p (u v q e)"), E5)
-
-        turn_w(0)
-        quantise_ws(0)
-        slices = ((0, HALF), (HALF, HALF + P), (HALF + P, N))
-        for lo, hi in slices:
-            part = offsets[:, lo // LIST_ROWS : hi // LIST_ROWS]
-            nc.vector.tensor_copy(w_bf[:, 3, lo:hi], w_planes[3][:].indirect(part))
-        for copy, (lo, hi) in zip((on_scalar, on_vector, on_vector), slices):
-            interleave(copy, w_il, w_bf, lo, hi)
-        for half in range(2):
-            slots = slice(half * HALF, (half + 1) * HALF)
-            quantise(w_q, slots, w_il[:, slots, :].rearrange("p i j -> p (i j)"), E4)
-        x_interleave(on_vector, 0, 0, 0, P)
-        turn_w(1)
-        x_interleave(on_scalar, 0, 1, 0, P)
-        quantise_ws(1)
-
-        def quantise_x(g, pair):
-            quantise(x_q[g], halves[pair], x_il[g, pair][:].rearrange("p t m j -> p (t m j)"), E4)
-
-        quantise_x(0, 0)
-        quantise_x(0, 1)
-
-        factor(0, 0)
-        factor(0, 1)
-        factors[1] = sb("factors1", [P, 4, N], F32, "x_il0_1")
-        for t in (2, 3):
-            nc.gpsimd.tensor_tensor(factors[1][:, t, :], y_sb[1][:, t, :], signed[t][:], MULT)
-        turned = sb("signed_turned", [P, 4, len(FROM_PSUM), P], F32, "x_raw0")
-        for k in range(4):
-            nc.scalar.activation(turned[:, k], sign_rows[:], COPY, scale=ts_columns[:, k : k + 1])
-        for s, key in enumerate(FROM_PSUM):
-            if s < 2:
-                signed_bank[key] = ps_dw.tile([P, N], F32, name=f"signed_bank{s}", tag=f"dw_bank{s}")
+        def factor(g, t):
+            c, labels = factors[g][:, t, :], y_sb[g][:, t, :]
+            if (g, t) in ON_GPSIMD:
+                nc.gpsimd.tensor_tensor(c, labels, signed[g, t][:], MULT)
             else:
-                signed_bank[key] = ps_turn.tile([P, N], F32, name="turn")
-            for k in range(4):
-                nc.tensor.transpose(signed_bank[key][:, block(k)], turned[:, k, s, :], ident[:])
-        scores(0, 0)
-        scores(0, 1)
-        factor(0, 2)
-        factor(0, 3)
-        x_interleave(on_scalar, 1, 0, 0, P)
-        scores(0, 2)
-        scores(0, 3)
-        x_il[1, 1] = sb("x_il1_1", [P, 2, P, 4], BF16, "z0_3")
-        x_interleave(on_scalar, 1, 1, 0, P)
-        factor(1, 0)
-        factor(1, 1)
-        quantise_x(1, 0)
-        gradient(0)
+                nc.vector.scalar_tensor_tensor(c, ts_bank[:], minus_sign[:, g, t : t + 1], labels, MULT, MULT)
 
-        quantise_x(1, 1)
-        for lo, hi in ((0, 2), (2, 3)):
-            xm_tile(0, lo, hi)
-        interleave(on_scalar, xm_il[0, 0, 2], xm_raw0, 0, 2 * P)
-        xm_interleave(0, 2)
-        xm_tile(1, 0, 1)
-        xm_interleave(1, 0)
-        margin[1] = sb("margin1", [P, 4, N], F32, "xm_first")
-        last_blocks = sb("xm_il_last", [P, G, P, 4], BF16, "margin0")
-        for g in range(G):
-            xm_il[g, 3] = xm_il[g, 3, 4] = last_blocks[:, g]
-            xm_interleave(g, 3)
-        for t in range(4):
-            scores(1, t)
-        quantise_h(0, "last_wt0")
-        early = mx_tiles("xm_early", "last_wt1", 3 * P)
-        for k, key in enumerate(((0, 0), (0, 1), (1, 0))):
-            xm_q[key] = (early, k)
-        quantise_xm(0, 0, 2)
-        quantise_xm(1, 0, 1)
-        dw_pass(0, 0)
-        dw_pass(0, 1)
-        gradient(1)
-        quantise_h(1)
+        z_tag = {(0, 0): 0, (0, 1): 1, (0, 2): 2, (0, 3): 3, (1, 0): 0, (1, 1): 1, (1, 2): 2, (1, 3): 4}
 
-        dw_sb = [None] * 4
+        def scores(g, t):
+            sums = in_bank(t, f"scores{g}_{t}", [P, N])
+            mx(sums[:], x_q[g], t, E4, w_q, E4, True, True)
+            z = sb(f"z{g}_{t}", [P, N], F32, f"z{z_tag[g, t]}")
+            if t == 3:
+                nc.vector.scalar_tensor_tensor(z[:], sums[:], last_wt[g][:], factors[g][:, t, :], MULT, MULT)
+                nc.scalar.activation(margin[g][:, t, :], z[:], RELU, bias=wt_abs[:, g, t : t + 1])
+                return
+            nc.vector.tensor_tensor(z[:], sums[:], factors[g][:, t, :], MULT)
+            nc.scalar.activation(
+                margin[g][:, t, :], z[:], RELU, bias=wt_abs[:, g, t : t + 1], scale=wt_sb[:, g, t : t + 1]
+            )
 
-        def finish_dw(b):
-            dw_pass(1, b)
-            dw_sb[b] = sb(f"dw_sb{b}", [P, N], F32)
-            nc.scalar.copy(dw_sb[b][:], dw_ps[b][:])
+        def gradient(g, cols):
+            nc.vector.tensor_tensor(
+                h_il[g][:, cols, :].rearrange("p (c i) t -> p c t i", i=2),
+                margin[g][:, :, cols].rearrange("p t (c i) -> p c t i", i=2),
+                factors[g][:, :, cols].rearrange("p t (c i) -> p c t i", i=2),
+                MULT,
+            )
 
-        def scatter(b):
-            nc.vector.tensor_copy(windows[b % WINDOWS][:].indirect(offsets[:]), dw_sb[b][:])
+        def quantise_h(g, cols):
+            quantise(h_q[g], cols, h_il[g][:, cols, :].rearrange("p i t -> p (i t)"), E5)
+
+        def xm_source(g, b):
+            if g == 0:
+                return xm0_raw[b // 2][:, :, block(b % 2)]
+            return xm_rest[:, :, block(b - 1)] if b else xm_first[:]
+
+        def quantise_xm(name, keys, tile, tag=None):
+            operand = mx_tiles(name, tag, len(keys) * P)
+            for k, key in enumerate(keys):
+                xm_q[key] = (operand, k)
+            quantise(operand, block(0, len(keys)), tile[:].rearrange("p d t -> p (d t)"), E4)
+
+        def dw_pass(g, b, sums, cols=whole):
+            mx(sums[:], *xm_q[g, b], E4, h_q[g], E5, g == 0, g == G - 1, cols)
+
+        def copy_out(copy, name, sums, tag=None):
+            tile = sb(name, list(sums.shape), F32, tag)
+            copy(tile[:], sums[:])
+            return tile
+
+        def turn_h(g, u, b, copy):
+            words = h_il[g].rearrange("p i t -> p (i t)").bitcast(F32)
+            bank = in_bank(b, f"h_turned{g}_{u}", [P, 4, P])
+            for e in range(4):
+                nc.tensor.transpose(bank[:, e, :], words[:, 2 * e + u : 2 * N : 8], ident[:])
+            copy(
+                hs_il[g, u].rearrange("p (v q e) -> p v q e", v=2, e=4),
+                bank[:].rearrange("p e q -> p (e q)").bitcast(BF16).rearrange("p (e q v) -> p v q e", e=4, v=2),
+            )
+
+        def scatter_on_scalar(window, cols, values):
+            nc.scalar.activation(window[:].indirect(part(cols.start, cols.stop)), values, COPY)
+
+        def store_block(b):
             nc.sync.dma_start(out_0[block(b), :], windows[b % WINDOWS][:])
 
-        def rows_out(g, pair):
-            gx = ring.tile([P, 2, D], F32, name="gx", bufs=2 * G)
+        def rows_out(g, pair, banks, tag):
+            gx = sb(f"gx{g}_{pair}", [P, 2, D], F32, tag)
             for k in range(2):
-                if (g, pair) == (0, 0):
-                    sums = ps_turn.tile([P, D], F32, name="turn")
-                else:
-                    sums = ps_lone.tile([P, D], F32, name="lone")
+                sums = in_bank(banks[k], f"rows{g}_{pair}_{k}", [P, D])
                 mx(sums[:], hs_q[g], 2 * pair + k, E5, ws_q, E4, True, True)
                 nc.scalar.copy(
                     gx[:, k, :].rearrange("p (q j) -> p q j", j=4),
                     sums[:].rearrange("p (j q) -> p q j", j=4),
                 )
-            nc.scalar.dma_start(gx_view[g][:, 2 * pair : 2 * pair + 2, :], gx[:])
+            queue = nc.scalar if g == G - 1 else nc.sync
+            queue.dma_start(gx_view[g][:, 2 * pair : 2 * pair + 2, :], gx[:])
 
-        turn_h(0, "ts_runs")
-        xm_tile(1, 1, 3, "last_z1")
-        interleave(on_scalar, xm_il[1, 1, 3], xm_rest, 0, 2 * P)
-        finish_dw(0)
-        hs_q[0] = mx_tiles("hs0", "x_il0_1")
-        quantise_hs(0)
-        late = mx_tiles("xm_late", "xm_first", 5 * P)
-        for k, key in enumerate(((0, 2), (0, 3), (1, 1), (1, 2), (1, 3))):
-            xm_q[key] = (late, k)
-        quantise_xm(0, 2, 3)
-        quantise_xm(0, 3, 4)
-        quantise_xm(1, 3, 4)
-        quantise_xm(1, 1, 3)
-        scatter(0)
-        rows_out(0, 0)
-        finish_dw(1)
-        for b in range(2, 4):
-            dw_pass(0, b)
-        rows_out(0, 1)
-        scatter(1)
-        turn_h(1)
-        quantise_hs(1)
-        finish_dw(2)
-        scatter(2)
-        finish_dw(3)
-        rows_out(1, 0)
-        rows_out(1, 1)
-        scatter(3)
+        nc.vector.tensor_copy(w_bf[:, 3, halves[0]], w_planes[3][:].indirect(part(0, HALF)))
+        nc.scalar.activation(w_bf[:, 3, halves[1]], w_planes[3][:].indirect(part(HALF, N)), COPY)
+        interleave(on_scalar, w_il[:], w_bf, HALF + P, N)
+        interleave(on_vector, w_il[:], w_bf, 0, HALF)
+        interleave(on_vector, w_il[:], w_bf, HALF, HALF + P)
+        for cols in halves:
+            quantise(w_q, cols, w_il[:, cols, :].rearrange("p i j -> p (i j)"), E4)
+        x0_src = [x0_raw[half][:].rearrange("p j (m t) -> p j m t", t=4) for half in range(2)]
+        x_interleave(on_scalar, x0_il[:, :, 0 : P // 2, :], x0_src[0])
+        for pair in range(2):
+            tiles = slice(2 * pair, 2 * pair + 2)
+            x_interleave(on_vector, x0_il[:, tiles, P // 2 : P, :], x0_src[1][:, :, :, tiles])
+        for pair in range(2):
+            tiles = slice(2 * pair, 2 * pair + 2)
+            quantise(x_q[0], halves[pair], x0_il[:, tiles].rearrange("p t m j -> p (t m j)"), E4)
+        for half in range(2):
+            ws_il[half] = sb(f"ws_il{half}", [P, 2, P, 2], F32, f"x0_raw{half}")
+            turn_w(half)
+
+        factors[0] = sb("factors0", [P, 4, N], F32, "x0_il")
+        factor(0, 0)
+        scores(0, 0)
+        factor(0, 1)
+        scores(0, 1)
+        factor(0, 2)
+        factor(0, 3)
+        scores(0, 2)
+        scores(0, 3)
+        factor(1, 0)
+        factor(1, 1)
+        ws_q = mx_tiles("ws", "last_wt0")
+        for half in range(2):
+            quantise(ws_q, halves[half], ws_il[half][:].rearrange("p j q u -> p (j q u)").bitcast(BF16), E4)
+        x1_il[0] = sb("x1_il0", [P, 2 * P * 4], BF16, "z3")[:]
+        x1_src = x1_raw[:].rearrange("p j (m t) -> p j m t", t=4)
+        for pair in range(2):
+            dst = x1_il[pair].rearrange("p (t m j) -> p t m j", t=2, j=4)
+            x_interleave(on_scalar, dst, x1_src[:, :, :, 2 * pair : 2 * pair + 2])
+        gradient(0, whole)
+
+        for pair in range(2):
+            quantise(x_q[1], halves[pair], x1_il[pair], E4)
+        factor(1, 2)
+        factor(1, 3)
+        xm_il = [sb("xm_il0", [P, 3 * P, 4], BF16), None]
+        interleave(on_scalar, xm_il[0][:, block(0, 2), :], xm0_raw[0][:], 0, HALF)
+        interleave(on_scalar, xm_il[0][:, block(2), :], xm_first[:], 0, P)
+        margin[1] = sb("margin1", [P, 4, N], F32, "xm_first")
+        for t in range(4):
+            scores(1, t)
+        h_q[0] = mx_tiles("h0", "last_wt1")
+        quantise_h(0, whole)
+        quantise_xm("xm0", ((0, 0), (0, 1), (1, 0)), xm_il[0], "z1")
+        first = [in_bank(6 + half, f"dw0_{half}", [P, HALF]) for half in range(2)]
+        for half in range(2):
+            dw_pass(0, 0, first[half], halves[half])
+        h1_flat = sb("h_il1", [P, 4 * N], BF16, "z4")
+        h_il[1] = h1_flat[:].rearrange("p (i t) -> p i t", t=4)
+        hs_il[0, 0] = h1_flat[:, 2 * N : 4 * N]
+        hs_il[0, 1] = sb("hs_il0_1", [P, 2 * N], BF16, "ts_runs")[:]
+        for u in range(2):
+            turn_h(0, u, u, on_scalar)
+        xm_il[1] = sb("xm_il1", [P, P, 4], BF16, "h_il0")
+        interleave(on_scalar, xm_il[1][:], xm_source(1, 1), 0, P)
+        h_q[1] = mx_tiles("h1")
+        hs_q[0] = mx_tiles("hs0")
+        gradient(1, halves[0])
+        quantise(hs_q[0], halves[0], hs_il[0, 0], E5)
+        quantise_h(1, halves[0])
+        gradient(1, halves[1])
+        quantise_xm("xm1", ((1, 1),), xm_il[1])
+        second = in_bank(5, "dw1", [P, N])
+        dw_pass(0, 1, second)
+        quantise(hs_q[0], halves[1], hs_il[0, 1], E5)
+        quantise_h(1, halves[1])
+        rows_out(0, 0, (2, 3), "w_plane2")
+        dw_pass(1, 0, first[0], halves[0])
+        dw0 = [copy_out(on_scalar, "dw0_0", first[0]), None]
+        dw_pass(1, 0, first[1], halves[1])
+        dw_pass(1, 1, second)
+        xm_il.append(sb("xm_il2", [P, G * P, 4], BF16, "ts_runs"))
+        interleave(on_vector, xm_il[2][:, block(0), :], xm_source(0, 2), 0, P)
+        dw0[1] = copy_out(on_vector, "dw0_1", first[1])
+        interleave(on_vector, xm_il[2][:, block(1), :], xm_source(1, 2), 0, P)
+        dw1 = copy_out(on_vector, "dw1", second)
+        quantise_xm("xm2", ((0, 2), (1, 2)), xm_il[2])
+        xm_il.append(sb("xm_il3", [P, G * P, 4], BF16, "ts_runs"))
+        for g in range(G):
+            interleave(on_gpsimd, xm_il[3][:, block(g), :], xm_source(g, 3), 0, P)
+        for half in range(2):
+            scatter_on_scalar(windows[0], halves[half], dw0[half][:])
+        store_block(0)
+        nc.vector.tensor_copy(windows[1][:].indirect(offsets[:]), dw1[:])
+        store_block(1)
+        rows_out(0, 1, (0, 1), "dw0_1")
+        third = in_bank(2, "dw2", [P, N])
+        for g in range(G):
+            dw_pass(g, 2, third)
+        dw2 = copy_out(on_scalar, "dw2", third, "w_plane2")
+        for cols in halves:
+            scatter_on_scalar(windows[2], cols, dw2[:, cols])
+        store_block(2)
+        quantise_xm("xm3", ((0, 3), (1, 3)), xm_il[3])
+        hs1_flat = sb("hs_il1", [P, 4 * N], BF16, "dw1")
+        for u in range(2):
+            hs_il[1, u] = hs1_flat[:, 2 * N * u : 2 * N * (u + 1)]
+            turn_h(1, u, 6 + u, on_vector)
+        fourth = in_bank(5, "dw3", [P, N])
+        for g in range(G):
+            dw_pass(g, 3, fourth)
+        dw3 = copy_out(on_vector, "dw3", fourth)
+        hs_q[1] = mx_tiles("hs1")
+        quantise(hs_q[1], whole, hs1_flat[:], E5)
+        nc.vector.tensor_copy(windows[0][:].indirect(offsets[:]), dw3[:])
+        store_block(3)
+        rows_out(1, 0, (3, 0), "w_plane0")
+        rows_out(1, 1, (1, 2), "w_plane1")

@@ -25,7 +25,7 @@ P = 128
 PASS = 512
 G = R // PASS
 HALF = PASS // 2
-ON_GPSIMD = ((0, 3), (1, 0), (1, 1), (1, 3))
+ON_GPSIMD = ((0, 2), (0, 3), (1, 0), (1, 3))
 WINDOWS = 3
 LIST_ROWS = 16
 
@@ -166,7 +166,7 @@ def tile_attend_gsqh_wx_ts_kernel(tc, xT, wT, y, wt, ts, xm, offs, out_0, out_1)
         factors = [None, factors1[:].rearrange("p (t i) -> p t i", t=4)]
         x1_il = [None, factors1[:, 3 * N : 4 * N].bitcast(BF16)]
         h_il = [sb("h_il0", [P, N, 4], BF16)[:], None]
-        margin = [sb("margin0", [P, 4, N], F32, "w_plane0"), None]
+        margin = [sb("margin0", [P, 4, N], F32, "w_plane0")[:], None]
         x_q = [mx_tiles(f"x{g}") for g in range(G)]
         w_q = mx_tiles("w")
         h_q = [None] * G
@@ -183,13 +183,16 @@ def tile_attend_gsqh_wx_ts_kernel(tc, xT, wT, y, wt, ts, xm, offs, out_0, out_1)
         def x_interleave(copy, dst, src):
             copy(dst.rearrange("p t m j -> p m j t"), src.rearrange("p j m t -> p m j t"))
 
-        def turn_w(half):
-            bank = in_bank(5 - half, f"w_turned{half}", [P, 2, 2, P])
+        def turn_words(copy, dst, rows, b, name):
+            bank = in_bank(b, name + "_turned", [P, 2, 2, P])
             for s in range(2):
-                words = w_bf[:, 2 * half + s, :].bitcast(F32)
+                words = rows[:, s, :].bitcast(F32)
                 for u in range(2):
                     nc.tensor.transpose(bank[:, s, u, :], words[:, u : N // 2 : 2], ident[:])
-            nc.scalar.copy(ws_il[half][:], bank[:].rearrange("p s u q -> p s q u"))
+            copy(dst, bank[:].rearrange("p s u q -> p s q u"))
+
+        def turn_w(half):
+            turn_words(on_scalar, ws_il[half][:], w_bf[:, 2 * half : 2 * half + 2, :], 5 - half, f"w{half}")
 
         def factor(g, t):
             c, labels = factors[g][:, t, :], y_sb[g][:, t, :]
@@ -233,7 +236,7 @@ def tile_attend_gsqh_wx_ts_kernel(tc, xT, wT, y, wt, ts, xm, offs, out_0, out_1)
             operand = mx_tiles(name, tag, len(keys) * P)
             for k, key in enumerate(keys):
                 xm_q[key] = (operand, k)
-            quantise(operand, block(0, len(keys)), tile[:].rearrange("p d t -> p (d t)"), E4)
+            quantise(operand, block(0, len(keys)), tile[:, :, :].rearrange("p d t -> p (d t)"), E4)
 
         def dw_pass(g, b, sums, cols=whole):
             mx(sums[:], *xm_q[g, b], E4, h_q[g], E5, g == 0, g == G - 1, cols)
@@ -273,24 +276,23 @@ def tile_attend_gsqh_wx_ts_kernel(tc, xT, wT, y, wt, ts, xm, offs, out_0, out_1)
 
         nc.vector.tensor_copy(w_bf[:, 3, halves[0]], w_planes[3][:].indirect(part(0, HALF)))
         nc.scalar.activation(w_bf[:, 3, halves[1]], w_planes[3][:].indirect(part(HALF, N)), COPY)
-        interleave(on_scalar, w_il[:], w_bf, HALF + P, N)
+        interleave(on_scalar, w_il[:], w_bf, HALF, N)
         interleave(on_vector, w_il[:], w_bf, 0, HALF)
-        interleave(on_vector, w_il[:], w_bf, HALF, HALF + P)
         for cols in halves:
             quantise(w_q, cols, w_il[:, cols, :].rearrange("p i j -> p (i j)"), E4)
         x0_src = [x0_raw[half][:].rearrange("p j (m t) -> p j m t", t=4) for half in range(2)]
-        x_interleave(on_scalar, x0_il[:, :, 0 : P // 2, :], x0_src[0])
         for pair in range(2):
             tiles = slice(2 * pair, 2 * pair + 2)
+            x_interleave(on_scalar, x0_il[:, tiles, 0 : P // 2, :], x0_src[0][:, :, :, tiles])
             x_interleave(on_vector, x0_il[:, tiles, P // 2 : P, :], x0_src[1][:, :, :, tiles])
         for pair in range(2):
             tiles = slice(2 * pair, 2 * pair + 2)
             quantise(x_q[0], halves[pair], x0_il[:, tiles].rearrange("p t m j -> p (t m j)"), E4)
         for half in range(2):
-            ws_il[half] = sb(f"ws_il{half}", [P, 2, P, 2], F32, f"x0_raw{half}")
+            ws_il[half] = sb(f"ws_il{half}", [P, 2, P, 2], F32, ("x0_raw0", "w_il")[half])
             turn_w(half)
 
-        factors[0] = sb("factors0", [P, 4, N], F32, "x0_il")
+        factors[0] = sb("factors0", [P, 4, N], F32, "x0_raw1")
         factor(0, 0)
         scores(0, 0)
         factor(0, 1)
@@ -318,46 +320,52 @@ def tile_attend_gsqh_wx_ts_kernel(tc, xT, wT, y, wt, ts, xm, offs, out_0, out_1)
         xm_il = [sb("xm_il0", [P, 3 * P, 4], BF16), None]
         interleave(on_scalar, xm_il[0][:, block(0, 2), :], xm0_raw[0][:], 0, HALF)
         interleave(on_scalar, xm_il[0][:, block(2), :], xm_first[:], 0, P)
-        margin[1] = sb("margin1", [P, 4, N], F32, "xm_first")
+        behind_xm = sb("behind_xm", [P, 5 * N], F32, "xm_first")
+        margin[1] = behind_xm[:, 0 : 4 * N].rearrange("p (t i) -> p t i", t=4)
+        hs_il[0, 0] = behind_xm[:, 4 * N :].bitcast(BF16)
+        turn_h(0, 0, 4, on_scalar)
         for t in range(4):
             scores(1, t)
         h_q[0] = mx_tiles("h0", "last_wt1")
         quantise_h(0, whole)
+        hs_q[0] = mx_tiles("hs0")
+        quantise(hs_q[0], halves[0], hs_il[0, 0], E5)
         quantise_xm("xm0", ((0, 0), (0, 1), (1, 0)), xm_il[0], "z1")
         first = [in_bank(6 + half, f"dw0_{half}", [P, HALF]) for half in range(2)]
         for half in range(2):
             dw_pass(0, 0, first[half], halves[half])
         h1_flat = sb("h_il1", [P, 4 * N], BF16, "z4")
         h_il[1] = h1_flat[:].rearrange("p (i t) -> p i t", t=4)
-        hs_il[0, 0] = h1_flat[:, 2 * N : 4 * N]
-        hs_il[0, 1] = sb("hs_il0_1", [P, 2 * N], BF16, "ts_runs")[:]
-        for u in range(2):
-            turn_h(0, u, u, on_scalar)
+        hs_il[0, 1] = h1_flat[:, 2 * N : 4 * N]
+        turn_h(0, 1, 1, on_scalar)
         xm_il[1] = sb("xm_il1", [P, P, 4], BF16, "h_il0")
         interleave(on_scalar, xm_il[1][:], xm_source(1, 1), 0, P)
+        rows_out(0, 0, (2, 3), "w_plane2")
         h_q[1] = mx_tiles("h1")
-        hs_q[0] = mx_tiles("hs0")
         gradient(1, halves[0])
-        quantise(hs_q[0], halves[0], hs_il[0, 0], E5)
+        quantise(hs_q[0], halves[1], hs_il[0, 1], E5)
         quantise_h(1, halves[0])
         gradient(1, halves[1])
         quantise_xm("xm1", ((1, 1),), xm_il[1])
         second = in_bank(5, "dw1", [P, N])
         dw_pass(0, 1, second)
-        quantise(hs_q[0], halves[1], hs_il[0, 1], E5)
         quantise_h(1, halves[1])
-        rows_out(0, 0, (2, 3), "w_plane2")
+        rows_out(0, 1, (0, 1), "w_plane3")
         dw_pass(1, 0, first[0], halves[0])
-        dw0 = [copy_out(on_scalar, "dw0_0", first[0]), None]
+        dw0 = [copy_out(on_vector, "dw0_0", first[0]), None]
         dw_pass(1, 0, first[1], halves[1])
         dw_pass(1, 1, second)
-        xm_il.append(sb("xm_il2", [P, G * P, 4], BF16, "ts_runs"))
+        xm_il.append(sb("xm_il2", [P, G * P, 4], BF16, "h_il0"))
         interleave(on_vector, xm_il[2][:, block(0), :], xm_source(0, 2), 0, P)
         dw0[1] = copy_out(on_vector, "dw0_1", first[1])
         interleave(on_vector, xm_il[2][:, block(1), :], xm_source(1, 2), 0, P)
         dw1 = copy_out(on_vector, "dw1", second)
         quantise_xm("xm2", ((0, 2), (1, 2)), xm_il[2])
-        xm_il.append(sb("xm_il3", [P, G * P, 4], BF16, "ts_runs"))
+        late = sb("late", [P, 4 * N + G * P * 4], BF16, "h_il0")
+        h1_rows = late[:, 0 : 4 * N].rearrange("p (t i) -> p t i", t=4)
+        for u in range(2):
+            on_gpsimd(h1_rows[:, 2 * u : 2 * u + 2, :], h_il[1][:, :, 2 * u : 2 * u + 2].rearrange("p i t -> p t i"))
+        xm_il.append(late[:, 4 * N :].rearrange("p (d t) -> p d t", t=4))
         for g in range(G):
             interleave(on_gpsimd, xm_il[3][:, block(g), :], xm_source(g, 3), 0, P)
         for half in range(2):
@@ -365,7 +373,6 @@ def tile_attend_gsqh_wx_ts_kernel(tc, xT, wT, y, wt, ts, xm, offs, out_0, out_1)
         store_block(0)
         nc.vector.tensor_copy(windows[1][:].indirect(offsets[:]), dw1[:])
         store_block(1)
-        rows_out(0, 1, (0, 1), "dw0_1")
         third = in_bank(2, "dw2", [P, N])
         for g in range(G):
             dw_pass(g, 2, third)
@@ -373,17 +380,16 @@ def tile_attend_gsqh_wx_ts_kernel(tc, xT, wT, y, wt, ts, xm, offs, out_0, out_1)
         for cols in halves:
             scatter_on_scalar(windows[2], cols, dw2[:, cols])
         store_block(2)
-        quantise_xm("xm3", ((0, 3), (1, 3)), xm_il[3])
-        hs1_flat = sb("hs_il1", [P, 4 * N], BF16, "dw1")
+        hs1_words = sb("hs_il1", [P, 4, P, 2], F32, "dw1")
         for u in range(2):
-            hs_il[1, u] = hs1_flat[:, 2 * N * u : 2 * N * (u + 1)]
-            turn_h(1, u, 6 + u, on_vector)
+            turn_words(on_vector, hs1_words[:, 2 * u : 2 * u + 2], h1_rows[:, 2 * u : 2 * u + 2, :], 6 + u, f"h1_{u}")
+        quantise_xm("xm3", ((0, 3), (1, 3)), xm_il[3])
         fourth = in_bank(5, "dw3", [P, N])
         for g in range(G):
             dw_pass(g, 3, fourth)
-        dw3 = copy_out(on_vector, "dw3", fourth)
         hs_q[1] = mx_tiles("hs1")
-        quantise(hs_q[1], whole, hs1_flat[:], E5)
+        quantise(hs_q[1], whole, hs1_words[:].rearrange("p t q u -> p (t q u)").bitcast(BF16), E5)
+        dw3 = copy_out(on_vector, "dw3", fourth)
         nc.vector.tensor_copy(windows[0][:].indirect(offsets[:]), dw3[:])
         store_block(3)
         rows_out(1, 0, (3, 0), "w_plane0")

@@ -16,16 +16,18 @@ E5 = mybir.dt.float8_e5m2_x4
 MULT = mybir.AluOpType.mult
 ADD = mybir.AluOpType.add
 IS_GE = mybir.AluOpType.is_ge
-NOT_EQUAL = mybir.AluOpType.not_equal
+IS_EQUAL = mybir.AluOpType.is_equal
 ABS = mybir.ActivationFunctionType.Abs
 COPY = mybir.ActivationFunctionType.Copy
 RELU = mybir.ActivationFunctionType.Relu
 
 P = 128
+QUAD = 32
 PASS = 512
 G = R // PASS
 HALF = PASS // 2
-ON_GPSIMD = ((0, 2), (0, 3), (1, 0), (1, 3))
+ON_GPSIMD = ((0, 3), (1, 0), (1, 1), (1, 3))
+W_SPLIT = 320
 WINDOWS = 3
 LIST_ROWS = 16
 
@@ -74,7 +76,7 @@ def tile_attend_gsqh_wx_ts_kernel(tc, xT, wT, y, wt, ts, xm, offs, out_0, out_1)
 
         offsets = keep.tile([P, N // LIST_ROWS], U16, name="offsets")
         w_planes = [sb(f"w_plane{j}", [P, T], F32) for j in range(4)]
-        x0_raw = [sb(f"x0_raw{half}", [P, 4, HALF], F32) for half in range(2)]
+        x0_raw = sb("x0_raw0", [P, 4, PASS], F32)
         x1_raw = sb("x1_raw", [P, 4, PASS], F32)
         y_sb = [sb(f"y_sb{g}", [P, 4, N], F32) for g in range(G)]
         xm0_raw = [sb(f"xm0_raw{half}", [P, 4, HALF], F32) for half in range(2)]
@@ -91,14 +93,13 @@ def tile_attend_gsqh_wx_ts_kernel(tc, xT, wT, y, wt, ts, xm, offs, out_0, out_1)
         xm_view = xm[0].rearrange("(g p t) d -> g p t d", g=G, t=4)
         gx_view = out_1[0].rearrange("(g p t) d -> g p t d", g=G, t=4)
 
-        nc.sync.dma_start(ts_runs[:], ts[0].rearrange("(n e) -> n e", n=P))
+        nc.scalar.dma_start(ts_runs[:], ts[0].rearrange("(n e) -> n e", n=P))
         nc.scalar.dma_start(wt_sb[:], wt[0].rearrange("(g p t) o -> p g (t o)", g=G, t=4))
         nc.sync.dma_start(w_planes[0][:], w_view[0])
         nc.sync.dma_start(offsets[:], offs)
         for j in range(1, 4):
             nc.sync.dma_start(w_planes[j][:], w_view[j])
-        for half in range(2):
-            nc.sync.dma_start(x0_raw[half][:], x_view[0][:, :, halves[half]])
+        nc.sync.dma_start(x0_raw[:], x_view[0])
         nc.sync.dma_start(y_sb[0][:, 0:2, :], y_view[0][:, 0:2, :])
         nc.sync.dma_start(y_sb[0][:, 2:4, :], y_view[0][:, 2:4, :])
         nc.sync.dma_start(y_sb[1][:, 0:2, :], y_view[1][:, 0:2, :])
@@ -109,11 +110,16 @@ def tile_attend_gsqh_wx_ts_kernel(tc, xT, wT, y, wt, ts, xm, offs, out_0, out_1)
         nc.sync.dma_start(xm_rest[:], xm_view[1][:, :, P:D])
         nc.sync.dma_start(xm0_raw[1][:], xm_view[0][:, :, halves[1]])
 
-        zeros = sb("zeros", [P, P], F32, "window2")
-        nc.gpsimd.memset(zeros[:], 0.0)
-        nc.gpsimd.affine_select(
-            out=ident[:], in_=zeros[:], compare_op=NOT_EQUAL, fill=1.0, base=0, pattern=[[-1, P]], channel_multiplier=1
-        )
+        ones = sb("ones", [P, QUAD], F32)
+        count = sb("count", [P, QUAD], F32, "window0")
+        count_turned = sb("count_turned", [P, QUAD], F32, "window1")
+        nc.vector.memset(ones[:], 1.0)
+        nc.vector.memset(ident[:], 0.0)
+        nc.vector.tensor_tensor_scan(count[:], ones[:], ones[:], 0.0, MULT, ADD)
+        nc.vector.transpose(count_turned[:], count[:])
+        for q in range(P // QUAD):
+            rows = slice(q * QUAD, (q + 1) * QUAD)
+            nc.vector.tensor_tensor(ident[rows, rows], count[rows, :], count_turned[rows, :], IS_EQUAL)
         windows = [sb(f"window{b}", [P, T], F32) for b in range(WINDOWS)]
         nc.gpsimd.memset(windows[-1][:].bitcast(I32), 0)
         for window in windows[:-1]:
@@ -141,7 +147,7 @@ def tile_attend_gsqh_wx_ts_kernel(tc, xT, wT, y, wt, ts, xm, offs, out_0, out_1)
 
         ts_all = sb("ts_all", [P, N], F32)
         nc.scalar.activation(ts_all[:], ts_table[:].indirect(offsets[:]), COPY)
-        w_flat = sb("w_bf", [P, 4 * N], BF16, "ts_table")
+        w_flat = sb("w_bf", [P, 4 * N], BF16)
         w_bf = w_flat[:].rearrange("p (j i) -> p j i", j=4)
         for j in range(3):
             nc.vector.tensor_copy(w_bf[:, j, :], w_planes[j][:].indirect(offsets[:]))
@@ -161,7 +167,9 @@ def tile_attend_gsqh_wx_ts_kernel(tc, xT, wT, y, wt, ts, xm, offs, out_0, out_1)
 
         w_il = sb("w_il", [P, N, 4], BF16)
         ws_il = [None, None]
-        x0_il = sb("x0_il", [P, 4, P, 4], BF16)
+        factors0 = sb("factors0", [P, 4 * N], F32)
+        x0_flat = [sb("x0_il0", [P, 2 * N], BF16)[:], factors0[:, 3 * N : 4 * N].bitcast(BF16)]
+        x0_il = [flat.rearrange("p (t m j) -> p t m j", t=2, j=4) for flat in x0_flat]
         factors1 = sb("factors1", [P, 4 * N], F32)
         factors = [None, factors1[:].rearrange("p (t i) -> p t i", t=4)]
         x1_il = [None, factors1[:, 3 * N : 4 * N].bitcast(BF16)]
@@ -274,25 +282,24 @@ def tile_attend_gsqh_wx_ts_kernel(tc, xT, wT, y, wt, ts, xm, offs, out_0, out_1)
             queue = nc.scalar if g == G - 1 else nc.sync
             queue.dma_start(gx_view[g][:, 2 * pair : 2 * pair + 2, :], gx[:])
 
-        nc.vector.tensor_copy(w_bf[:, 3, halves[0]], w_planes[3][:].indirect(part(0, HALF)))
+        for k in range(2):
+            nc.vector.tensor_copy(w_bf[:, 3, block(k)], w_planes[3][:].indirect(part(k * P, (k + 1) * P)))
         nc.scalar.activation(w_bf[:, 3, halves[1]], w_planes[3][:].indirect(part(HALF, N)), COPY)
-        interleave(on_scalar, w_il[:], w_bf, HALF, N)
-        interleave(on_vector, w_il[:], w_bf, 0, HALF)
-        for cols in halves:
+        interleave(on_scalar, w_il[:], w_bf, W_SPLIT, N)
+        interleave(on_vector, w_il[:], w_bf, 0, P)
+        interleave(on_vector, w_il[:], w_bf, P, W_SPLIT)
+        for cols in (block(0), block(1), halves[1]):
             quantise(w_q, cols, w_il[:, cols, :].rearrange("p i j -> p (i j)"), E4)
-        x0_src = [x0_raw[half][:].rearrange("p j (m t) -> p j m t", t=4) for half in range(2)]
+        x0_src = x0_raw[:].rearrange("p j (m t) -> p j m t", t=4)
+        x_interleave(on_vector, x0_il[0], x0_src[:, :, :, 0:2])
+        x_interleave(on_scalar, x0_il[1], x0_src[:, :, :, 2:4])
         for pair in range(2):
-            tiles = slice(2 * pair, 2 * pair + 2)
-            x_interleave(on_scalar, x0_il[:, tiles, 0 : P // 2, :], x0_src[0][:, :, :, tiles])
-            x_interleave(on_vector, x0_il[:, tiles, P // 2 : P, :], x0_src[1][:, :, :, tiles])
-        for pair in range(2):
-            tiles = slice(2 * pair, 2 * pair + 2)
-            quantise(x_q[0], halves[pair], x0_il[:, tiles].rearrange("p t m j -> p (t m j)"), E4)
+            quantise(x_q[0], halves[pair], x0_flat[pair], E4)
         for half in range(2):
-            ws_il[half] = sb(f"ws_il{half}", [P, 2, P, 2], F32, ("x0_raw0", "w_il")[half])
+            ws_il[half] = sb(f"ws_il{half}", [P, 2, P, 2], F32, ("x0_raw0", "x0_il0")[half])
             turn_w(half)
 
-        factors[0] = sb("factors0", [P, 4, N], F32, "x0_raw1")
+        factors[0] = factors0[:].rearrange("p (t i) -> p t i", t=4)
         factor(0, 0)
         scores(0, 0)
         factor(0, 1)

@@ -26,7 +26,7 @@ QUAD = 32
 PASS = 512
 G = R // PASS
 HALF = PASS // 2
-ON_GPSIMD = ((0, 3), (1, 0), (1, 1), (1, 3))
+ON_GPSIMD = ((0, 3), (1, 0), (1, 3))
 W_SPLIT = 320
 WINDOWS = 3
 LIST_ROWS = 16
@@ -130,9 +130,8 @@ def tile_attend_gsqh_wx_ts_kernel(tc, xT, wT, y, wt, ts, xm, offs, out_0, out_1)
         nc.vector.tensor_scalar(wt_step[:], wt_sb[:], 0.0, -2.0, IS_GE, MULT)
         nc.vector.tensor_scalar(minus_sign[:], wt_step[:], 1.0, None, ADD)
 
-        last_wt = [sb(f"last_wt{g}", [P, 1], F32) for g in range(G)]
-        for g in range(G):
-            nc.vector.tensor_copy(last_wt[g][:], wt_sb[:, g, 3:4])
+        last_wt = sb("last_wt1", [P, 1], F32)
+        nc.vector.tensor_copy(last_wt[:], wt_sb[:, G - 1, 3:4])
 
         table_view = ts_table[:].rearrange("p (n k e) -> p k n e", k=4, e=4)
         for k in range(4):
@@ -170,12 +169,10 @@ def tile_attend_gsqh_wx_ts_kernel(tc, xT, wT, y, wt, ts, xm, offs, out_0, out_1)
         factors0 = sb("factors0", [P, 4 * N], F32)
         x0_flat = [sb("x0_il0", [P, 2 * N], BF16)[:], factors0[:, 3 * N : 4 * N].bitcast(BF16)]
         x0_il = [flat.rearrange("p (t m j) -> p t m j", t=2, j=4) for flat in x0_flat]
-        factors1 = sb("factors1", [P, 4 * N], F32)
-        factors = [None, factors1[:].rearrange("p (t i) -> p t i", t=4)]
-        x1_il = [None, factors1[:, 3 * N : 4 * N].bitcast(BF16)]
+        factors = [None, None]
         h_il = [sb("h_il0", [P, N, 4], BF16)[:], None]
         margin = [sb("margin0", [P, 4, N], F32, "w_plane0")[:], None]
-        x_q = [mx_tiles(f"x{g}") for g in range(G)]
+        x_q = [mx_tiles("x0"), None]
         w_q = mx_tiles("w")
         h_q = [None] * G
         hs_il = {}
@@ -191,16 +188,16 @@ def tile_attend_gsqh_wx_ts_kernel(tc, xT, wT, y, wt, ts, xm, offs, out_0, out_1)
         def x_interleave(copy, dst, src):
             copy(dst.rearrange("p t m j -> p m j t"), src.rearrange("p j m t -> p m j t"))
 
-        def turn_words(copy, dst, rows, b, name):
+        def turn_words(copy, dst, rows, b, name, walk="s q u"):
             bank = in_bank(b, name + "_turned", [P, 2, 2, P])
             for s in range(2):
                 words = rows[:, s, :].bitcast(F32)
                 for u in range(2):
                     nc.tensor.transpose(bank[:, s, u, :], words[:, u : N // 2 : 2], ident[:])
-            copy(dst, bank[:].rearrange("p s u q -> p s q u"))
+            copy(dst.rearrange("p s q u -> p " + walk), bank[:].rearrange("p s u q -> p " + walk))
 
         def turn_w(half):
-            turn_words(on_scalar, ws_il[half][:], w_bf[:, 2 * half : 2 * half + 2, :], 5 - half, f"w{half}")
+            turn_words(on_scalar, ws_il[half], w_bf[:, 2 * half : 2 * half + 2, :], 5 - half, f"w{half}", "q s u")
 
         def factor(g, t):
             c, labels = factors[g][:, t, :], y_sb[g][:, t, :]
@@ -215,8 +212,8 @@ def tile_attend_gsqh_wx_ts_kernel(tc, xT, wT, y, wt, ts, xm, offs, out_0, out_1)
             sums = in_bank(t, f"scores{g}_{t}", [P, N])
             mx(sums[:], x_q[g], t, E4, w_q, E4, True, True)
             z = sb(f"z{g}_{t}", [P, N], F32, f"z{z_tag[g, t]}")
-            if t == 3:
-                nc.vector.scalar_tensor_tensor(z[:], sums[:], last_wt[g][:], factors[g][:, t, :], MULT, MULT)
+            if (g, t) == (G - 1, 3):
+                nc.vector.scalar_tensor_tensor(z[:], sums[:], last_wt[:], factors[g][:, t, :], MULT, MULT)
                 nc.scalar.activation(margin[g][:, t, :], z[:], RELU, bias=wt_abs[:, g, t : t + 1])
                 return
             nc.vector.tensor_tensor(z[:], sums[:], factors[g][:, t, :], MULT)
@@ -275,10 +272,7 @@ def tile_attend_gsqh_wx_ts_kernel(tc, xT, wT, y, wt, ts, xm, offs, out_0, out_1)
             for k in range(2):
                 sums = in_bank(banks[k], f"rows{g}_{pair}_{k}", [P, D])
                 mx(sums[:], hs_q[g], 2 * pair + k, E5, ws_q, E4, True, True)
-                nc.scalar.copy(
-                    gx[:, k, :].rearrange("p (q j) -> p q j", j=4),
-                    sums[:].rearrange("p (j q) -> p q j", j=4),
-                )
+                nc.scalar.copy(gx[:, k, :], sums[:])
             queue = nc.scalar if g == G - 1 else nc.sync
             queue.dma_start(gx_view[g][:, 2 * pair : 2 * pair + 2, :], gx[:])
 
@@ -295,8 +289,11 @@ def tile_attend_gsqh_wx_ts_kernel(tc, xT, wT, y, wt, ts, xm, offs, out_0, out_1)
         x_interleave(on_scalar, x0_il[1], x0_src[:, :, :, 2:4])
         for pair in range(2):
             quantise(x_q[0], halves[pair], x0_flat[pair], E4)
+        factors1 = sb("factors1", [P, 5 * N], F32, "x0_raw0")
+        factors[1] = factors1[:, 0 : 4 * N].rearrange("p (t i) -> p t i", t=4)
+        ws_words = factors1[:, 3 * N : 5 * N]
         for half in range(2):
-            ws_il[half] = sb(f"ws_il{half}", [P, 2, P, 2], F32, ("x0_raw0", "x0_il0")[half])
+            ws_il[half] = ws_words.rearrange("p (q j u) -> p j q u", j=4, u=2)[:, 2 * half : 2 * half + 2]
             turn_w(half)
 
         factors[0] = factors0[:].rearrange("p (t i) -> p t i", t=4)
@@ -310,19 +307,17 @@ def tile_attend_gsqh_wx_ts_kernel(tc, xT, wT, y, wt, ts, xm, offs, out_0, out_1)
         scores(0, 3)
         factor(1, 0)
         factor(1, 1)
-        ws_q = mx_tiles("ws", "last_wt0")
-        for half in range(2):
-            quantise(ws_q, halves[half], ws_il[half][:].rearrange("p j q u -> p (j q u)").bitcast(BF16), E4)
-        x1_il[0] = sb("x1_il0", [P, 2 * P * 4], BF16, "z3")[:]
+        x1_flat = sb("x1_il", [P, 4 * N], BF16, "z3")[:]
         x1_src = x1_raw[:].rearrange("p j (m t) -> p j m t", t=4)
-        for pair in range(2):
-            dst = x1_il[pair].rearrange("p (t m j) -> p t m j", t=2, j=4)
-            x_interleave(on_scalar, dst, x1_src[:, :, :, 2 * pair : 2 * pair + 2])
+        x_interleave(on_scalar, x1_flat.rearrange("p (t m j) -> p t m j", t=4, j=4), x1_src)
         gradient(0, whole)
 
+        x_q[1] = mx_tiles("x1", "w_plane0")
         for pair in range(2):
-            quantise(x_q[1], halves[pair], x1_il[pair], E4)
-        factor(1, 2)
+            quantise(x_q[1], halves[pair], x1_flat[:, 2 * N * pair : 2 * N * (pair + 1)], E4)
+        ws_q = mx_tiles("ws", "factors0")
+        for half in (1, 0):
+            quantise(ws_q, halves[half], ws_words[:, half * N : (half + 1) * N].bitcast(BF16), E4)
         factor(1, 3)
         xm_il = [sb("xm_il0", [P, 3 * P, 4], BF16), None]
         interleave(on_scalar, xm_il[0][:, block(0, 2), :], xm0_raw[0][:], 0, HALF)
@@ -331,8 +326,13 @@ def tile_attend_gsqh_wx_ts_kernel(tc, xT, wT, y, wt, ts, xm, offs, out_0, out_1)
         margin[1] = behind_xm[:, 0 : 4 * N].rearrange("p (t i) -> p t i", t=4)
         hs_il[0, 0] = behind_xm[:, 4 * N :].bitcast(BF16)
         turn_h(0, 0, 4, on_scalar)
-        for t in range(4):
-            scores(1, t)
+        xm_il[1] = sb("xm_il1", [P, P, 4], BF16, "signed1_3")
+        interleave(on_gpsimd, xm_il[1][:], xm_source(1, 1), 0, P)
+        scores(1, 0)
+        scores(1, 1)
+        factor(1, 2)
+        scores(1, 2)
+        scores(1, 3)
         h_q[0] = mx_tiles("h0", "last_wt1")
         quantise_h(0, whole)
         hs_q[0] = mx_tiles("hs0")
@@ -345,30 +345,28 @@ def tile_attend_gsqh_wx_ts_kernel(tc, xT, wT, y, wt, ts, xm, offs, out_0, out_1)
         h_il[1] = h1_flat[:].rearrange("p (i t) -> p i t", t=4)
         hs_il[0, 1] = h1_flat[:, 2 * N : 4 * N]
         turn_h(0, 1, 1, on_scalar)
-        xm_il[1] = sb("xm_il1", [P, P, 4], BF16, "h_il0")
-        interleave(on_scalar, xm_il[1][:], xm_source(1, 1), 0, P)
         rows_out(0, 0, (2, 3), "w_plane2")
         h_q[1] = mx_tiles("h1")
         gradient(1, halves[0])
         quantise(hs_q[0], halves[1], hs_il[0, 1], E5)
         quantise_h(1, halves[0])
         gradient(1, halves[1])
-        quantise_xm("xm1", ((1, 1),), xm_il[1])
+        quantise_xm("xm1", ((1, 1),), xm_il[1], "ts_runs")
         second = in_bank(5, "dw1", [P, N])
         dw_pass(0, 1, second)
         quantise_h(1, halves[1])
         rows_out(0, 1, (0, 1), "w_plane3")
         dw_pass(1, 0, first[0], halves[0])
-        dw0 = [copy_out(on_vector, "dw0_0", first[0]), None]
+        dw0 = [copy_out(on_scalar, "dw0_0", first[0]), None]
         dw_pass(1, 0, first[1], halves[1])
         dw_pass(1, 1, second)
-        xm_il.append(sb("xm_il2", [P, G * P, 4], BF16, "h_il0"))
+        xm_il.append(sb("xm_il2", [P, G * P, 4], BF16, "signed1_3"))
         interleave(on_vector, xm_il[2][:, block(0), :], xm_source(0, 2), 0, P)
         dw0[1] = copy_out(on_vector, "dw0_1", first[1])
         interleave(on_vector, xm_il[2][:, block(1), :], xm_source(1, 2), 0, P)
         dw1 = copy_out(on_vector, "dw1", second)
         quantise_xm("xm2", ((0, 2), (1, 2)), xm_il[2])
-        late = sb("late", [P, 4 * N + G * P * 4], BF16, "h_il0")
+        late = sb("late", [P, 4 * N + G * P * 4], BF16, "signed1_3")
         h1_rows = late[:, 0 : 4 * N].rearrange("p (t i) -> p t i", t=4)
         for u in range(2):
             on_gpsimd(h1_rows[:, 2 * u : 2 * u + 2, :], h_il[1][:, :, 2 * u : 2 * u + 2].rearrange("p i t -> p t i"))
@@ -396,7 +394,7 @@ def tile_attend_gsqh_wx_ts_kernel(tc, xT, wT, y, wt, ts, xm, offs, out_0, out_1)
             dw_pass(g, 3, fourth)
         hs_q[1] = mx_tiles("hs1")
         quantise(hs_q[1], whole, hs1_words[:].rearrange("p t q u -> p (t q u)").bitcast(BF16), E5)
-        dw3 = copy_out(on_vector, "dw3", fourth)
+        dw3 = copy_out(on_scalar, "dw3", fourth, "w_plane2")
         nc.vector.tensor_copy(windows[0][:].indirect(offsets[:]), dw3[:])
         store_block(3)
         rows_out(1, 0, (3, 0), "w_plane0")

from contextlib import ExitStack

import concourse.mybir as mybir

N, T, D, R = 512, 2048, 512, 1024
FLOPS = 3 * 2 * N * D * R

F32 = mybir.dt.float32
BF16 = mybir.dt.bfloat16
I32 = mybir.dt.int32
U32 = mybir.dt.uint32
U16 = mybir.dt.uint16
U8 = mybir.dt.uint8
E4 = mybir.dt.float8_e4m3fn_x4
E5 = mybir.dt.float8_e5m2_x4
MULT = mybir.AluOpType.mult
ADD = mybir.AluOpType.add
IS_GE = mybir.AluOpType.is_ge
IS_EQUAL = mybir.AluOpType.is_equal
ABS = mybir.ActivationFunctionType.Abs
COPY = mybir.ActivationFunctionType.Copy
RELU = mybir.ActivationFunctionType.Relu

P = 128
QUAD = 32
PASS = 512
G = R // PASS
HALF = PASS // 2
ON_GPSIMD = ((0, 3), (1, 0), (1, 3))
W_SPLIT = 320
WINDOWS = 3
LIST_ROWS = 16


def tile_attend_gsqh_wx_ts_kernel(tc, xT, wT, y, wt, ts, xm, offs, out_0, out_1):
    nc = tc.nc
    with ExitStack() as ctx:
        keep = ctx.enter_context(tc.tile_pool(name="keep", bufs=1))
        psum = ctx.enter_context(tc.psum_pool(name="psum", bufs=1))

        def in_bank(b, name, shape):
            return psum.tile(shape, F32, name=name, tag=f"bank{b}")

        def sb(name, shape, dtype, tag=None):
            return keep.tile(shape, dtype, name=name, tag=tag or name, align_bytes=64)

        def mx_tiles(name, tag=None, width=PASS):
            return sb(name + "_codes", [P, width], U32, tag), sb(name + "_scales", [P, width], U8)

        def quantise(dst, cols, src, fmt):
            nc.vector.quantize_mx(out=dst[0][:, cols].bitcast(fmt), scales=dst[1][:, cols], in_=src)

        def block(k, count=1):
            return slice(k * P, (k + count) * P)

        def mx(out, lhs, k, lhs_fmt, rhs, rhs_fmt, start, stop, cols=slice(0, PASS)):
            nc.tensor.matmul_mx(
                out=out,
                lhsT=lhs[0][:, block(k)].bitcast(lhs_fmt),
                lhsT_scale=lhs[1][:, block(k)],
                rhs=rhs[0][:, cols].bitcast(rhs_fmt),
                rhs_scale=rhs[1][:, cols],
                start=start,
                stop=stop,
            )

        def part(lo, hi):
            return offsets[:, lo // LIST_ROWS : hi // LIST_ROWS]

        whole = slice(0, PASS)
        halves = (slice(0, HALF), slice(HALF, PASS))
        on_scalar, on_vector = nc.scalar.copy, nc.vector.tensor_copy

        def on_gpsimd(dst, src):
            nc.gpsimd.tensor_scalar(dst, src, 1.0, 0.0, MULT, ADD)

        offsets = keep.tile([P, N // LIST_ROWS], U16, name="offsets")
        w_planes = [sb(f"w_plane{j}", [P, T], F32) for j in range(4)]
        x0_raw = sb("x0_raw0", [P, 4, PASS], F32)
        x1_raw = sb("x1_raw", [P, 4, PASS], F32)
        y_sb = [sb(f"y_sb{g}", [P, 4, N], F32) for g in range(G)]
        xm0_raw = [sb(f"xm0_raw{half}", [P, 4, HALF], F32) for half in range(2)]
        xm_first = sb("xm_first", [P, 4, P], F32)
        xm_rest = sb("xm_rest", [P, 4, D - P], F32)
        wt_sb = sb("wt_sb", [P, G, 4], F32)
        ts_runs = sb("ts_runs", [P, T // P], F32)
        ts_table = sb("ts_table", [P, T], F32)
        ident = sb("ident", [P, P], F32)

        w_view = wT.rearrange("(p j) t -> j p t", j=4)
        x_view = xT[0].rearrange("(p j) (g r) -> g p j r", j=4, g=G)
        y_view = y[0].rearrange("(g p t) i -> g p t i", g=G, t=4)
        xm_view = xm[0].rearrange("(g p t) d -> g p t d", g=G, t=4)
        gx_view = out_1[0].rearrange("(g p t) d -> g p t d", g=G, t=4)

        nc.scalar.dma_start(ts_runs[:], ts[0].rearrange("(n e) -> n e", n=P))
        nc.scalar.dma_start(wt_sb[:], wt[0].rearrange("(g p t) o -> p g (t o)", g=G, t=4))
        nc.sync.dma_start(w_planes[0][:], w_view[0])
        nc.sync.dma_start(offsets[:], offs)
        for j in range(1, 4):
            nc.sync.dma_start(w_planes[j][:], w_view[j])
        nc.sync.dma_start(x0_raw[:], x_view[0])
        nc.sync.dma_start(y_sb[0][:, 0:2, :], y_view[0][:, 0:2, :])
        nc.sync.dma_start(y_sb[0][:, 2:4, :], y_view[0][:, 2:4, :])
        nc.sync.dma_start(y_sb[1][:, 0:2, :], y_view[1][:, 0:2, :])
        nc.sync.dma_start(x1_raw[:], x_view[1])
        nc.sync.dma_start(y_sb[1][:, 2:4, :], y_view[1][:, 2:4, :])
        nc.sync.dma_start(xm0_raw[0][:], xm_view[0][:, :, halves[0]])
        nc.sync.dma_start(xm_first[:], xm_view[1][:, :, 0:P])
        nc.sync.dma_start(xm_rest[:], xm_view[1][:, :, P:D])
        nc.sync.dma_start(xm0_raw[1][:], xm_view[0][:, :, halves[1]])

        ones = sb("ones", [P, QUAD], F32)
        count = sb("count", [P, QUAD], F32, "window0")
        count_turned = sb("count_turned", [P, QUAD], F32, "window1")
        nc.vector.memset(ones[:], 1.0)
        nc.vector.memset(ident[:], 0.0)
        nc.vector.tensor_tensor_scan(count[:], ones[:], ones[:], 0.0, MULT, ADD)
        nc.vector.transpose(count_turned[:], count[:])
        for q in range(P // QUAD):
            rows = slice(q * QUAD, (q + 1) * QUAD)
            nc.vector.tensor_tensor(ident[rows, rows], count[rows, :], count_turned[rows, :], IS_EQUAL)
        windows = [sb(f"window{b}", [P, T], F32) for b in range(WINDOWS)]
        nc.gpsimd.memset(windows[-1][:].bitcast(I32), 0)
        for window in windows[:-1]:
            nc.vector.memset(window[:].bitcast(I32), 0)

        wt_step = sb("wt_step", [P, G, 4], F32)
        minus_sign = sb("minus_sign", [P, G, 4], F32)
        nc.vector.tensor_scalar(wt_step[:], wt_sb[:], 0.0, -2.0, IS_GE, MULT)
        nc.vector.tensor_scalar(minus_sign[:], wt_step[:], 1.0, None, ADD)

        last_wt = sb("last_wt1", [P, 1], F32)
        nc.vector.tensor_copy(last_wt[:], wt_sb[:, G - 1, 3:4])

        table_view = ts_table[:].rearrange("p (n k e) -> p k n e", k=4, e=4)
        for k in range(4):
            bank = in_bank(k, f"spread{k}", [P, 4, P])
            for e in range(4):
                column = ts_runs[:, 4 * k + e : 4 * k + e + 1]
                nc.tensor.transpose(bank[:, e, :], column.to_broadcast([P, P]), ident[:])
            nc.scalar.copy(table_view[:, k], bank[:].rearrange("p e n -> p n e"))

        wt_abs = sb("wt_abs", [P, G, 4], F32, "ts_runs")
        nc.scalar.activation(wt_abs[:], wt_sb[:], ABS)

        ts_all = sb("ts_all", [P, N], F32)
        nc.scalar.activation(ts_all[:], ts_table[:].indirect(offsets[:]), COPY)
        w_flat = sb("w_bf", [P, 4 * N], BF16)
        w_bf = w_flat[:].rearrange("p (j i) -> p j i", j=4)
        for j in range(3):
            nc.vector.tensor_copy(w_bf[:, j, :], w_planes[j][:].indirect(offsets[:]))

        bank = in_bank(4, "ts_turned", [P, 4, P])
        for k in range(4):
            nc.tensor.transpose(bank[:, k, :], ts_all[:, block(k)], ident[:])
        ts_columns = sb("ts_columns", [P, 4], F32)
        nc.scalar.copy(ts_columns[:], bank[:, :, 0])
        ts_bank = in_bank(6, "ts_bank", [P, N])
        for k in range(4):
            nc.tensor.transpose(ts_bank[:, block(k)], ts_columns[:, k : k + 1].to_broadcast([P, P]), ident[:])
        signed = {}
        for g, t in ON_GPSIMD:
            signed[g, t] = sb(f"signed{g}_{t}", [P, N], F32)
            nc.gpsimd.tensor_scalar(signed[g, t][:], ts_all[:], minus_sign[:, g, t : t + 1], 0.0, MULT, ADD)

        w_il = sb("w_il", [P, N, 4], BF16)
        ws_il = [None, None]
        factors0 = sb("factors0", [P, 4 * N], F32)
        x0_flat = [sb("x0_il0", [P, 2 * N], BF16)[:], factors0[:, 3 * N : 4 * N].bitcast(BF16)]
        x0_il = [flat.rearrange("p (t m j) -> p t m j", t=2, j=4) for flat in x0_flat]
        factors = [None, None]
        h_il = [sb("h_il0", [P, N, 4], BF16)[:], None]
        margin = [sb("margin0", [P, 4, N], F32, "w_plane0")[:], None]
        x_q = [mx_tiles("x0"), None]
        w_q = mx_tiles("w")
        h_q = [None] * G
        hs_il = {}
        hs_q = [None] * G
        xm_q = {}

        def interleave(copy, dst, src, lo, hi):
            copy(
                dst.rearrange("p (c i) t -> p c t i", i=4)[:, lo // 4 : hi // 4],
                src.rearrange("p t (c i) -> p c t i", i=4)[:, lo // 4 : hi // 4],
            )

        def x_interleave(copy, dst, src):
            copy(dst.rearrange("p t m j -> p m j t"), src.rearrange("p j m t -> p m j t"))

        def turn_words(copy, dst, rows, b, name, walk="s q u"):
            bank = in_bank(b, name + "_turned", [P, 2, 2, P])
            for s in range(2):
                words = rows[:, s, :].bitcast(F32)
                for u in range(2):
                    nc.tensor.transpose(bank[:, s, u, :], words[:, u : N // 2 : 2], ident[:])
            copy(dst.rearrange("p s q u -> p " + walk), bank[:].rearrange("p s u q -> p " + walk))

        def turn_w(half):
            turn_words(on_scalar, ws_il[half], w_bf[:, 2 * half : 2 * half + 2, :], 5 - half, f"w{half}", "q s u")

        def factor(g, t):
            c, labels = factors[g][:, t, :], y_sb[g][:, t, :]
            if (g, t) in ON_GPSIMD:
                nc.gpsimd.tensor_tensor(c, labels, signed[g, t][:], MULT)
            else:
                nc.vector.scalar_tensor_tensor(c, ts_bank[:], minus_sign[:, g, t : t + 1], labels, MULT, MULT)

        z_tag = {(0, 0): 0, (0, 1): 1, (0, 2): 2, (0, 3): 3, (1, 0): 0, (1, 1): 1, (1, 2): 2, (1, 3): 4}

        def scores(g, t):
            sums = in_bank(t, f"scores{g}_{t}", [P, N])
            mx(sums[:], x_q[g], t, E4, w_q, E4, True, True)
            z = sb(f"z{g}_{t}", [P, N], F32, f"z{z_tag[g, t]}")
            if (g, t) == (G - 1, 3):
                nc.vector.scalar_tensor_tensor(z[:], sums[:], last_wt[:], factors[g][:, t, :], MULT, MULT)
                nc.scalar.activation(margin[g][:, t, :], z[:], RELU, bias=wt_abs[:, g, t : t + 1])
                return
            nc.vector.tensor_tensor(z[:], sums[:], factors[g][:, t, :], MULT)
            nc.scalar.activation(
                margin[g][:, t, :], z[:], RELU, bias=wt_abs[:, g, t : t + 1], scale=wt_sb[:, g, t : t + 1]
            )

        def gradient(g, cols):
            nc.vector.tensor_tensor(
                h_il[g][:, cols, :].rearrange("p (c i) t -> p c t i", i=2),
                margin[g][:, :, cols].rearrange("p t (c i) -> p c t i", i=2),
                factors[g][:, :, cols].rearrange("p t (c i) -> p c t i", i=2),
                MULT,
            )

        def quantise_h(g, cols):
            quantise(h_q[g], cols, h_il[g][:, cols, :].rearrange("p i t -> p (i t)"), E5)

        def xm_source(g, b):
            if g == 0:
                return xm0_raw[b // 2][:, :, block(b % 2)]
            return xm_rest[:, :, block(b - 1)] if b else xm_first[:]

        def quantise_xm(name, keys, tile, tag=None):
            operand = mx_tiles(name, tag, len(keys) * P)
            for k, key in enumerate(keys):
                xm_q[key] = (operand, k)
            quantise(operand, block(0, len(keys)), tile[:, :, :].rearrange("p d t -> p (d t)"), E4)

        def dw_pass(g, b, sums, cols=whole):
            mx(sums[:], *xm_q[g, b], E4, h_q[g], E5, g == 0, g == G - 1, cols)

        def copy_out(copy, name, sums, tag=None):
            tile = sb(name, list(sums.shape), F32, tag)
            copy(tile[:], sums[:])
            return tile

        def turn_h(g, u, b, copy):
            words = h_il[g].rearrange("p i t -> p (i t)").bitcast(F32)
            bank = in_bank(b, f"h_turned{g}_{u}", [P, 4, P])
            for e in range(4):
                nc.tensor.transpose(bank[:, e, :], words[:, 2 * e + u : 2 * N : 8], ident[:])
            copy(
                hs_il[g, u].rearrange("p (v q e) -> p v q e", v=2, e=4),
                bank[:].rearrange("p e q -> p (e q)").bitcast(BF16).rearrange("p (e q v) -> p v q e", e=4, v=2),
            )

        def scatter_on_scalar(window, cols, values):
            nc.scalar.activation(window[:].indirect(part(cols.start, cols.stop)), values, COPY)

        def store_block(b):
            nc.sync.dma_start(out_0[block(b), :], windows[b % WINDOWS][:])

        def rows_out(g, pair, banks, tag):
            gx = sb(f"gx{g}_{pair}", [P, 2, D], F32, tag)
            for k in range(2):
                sums = in_bank(banks[k], f"rows{g}_{pair}_{k}", [P, D])
                mx(sums[:], hs_q[g], 2 * pair + k, E5, ws_q, E4, True, True)
                nc.scalar.copy(gx[:, k, :], sums[:])
            queue = nc.scalar if g == G - 1 else nc.sync
            queue.dma_start(gx_view[g][:, 2 * pair : 2 * pair + 2, :], gx[:])

        for k in range(2):
            nc.vector.tensor_copy(w_bf[:, 3, block(k)], w_planes[3][:].indirect(part(k * P, (k + 1) * P)))
        nc.scalar.activation(w_bf[:, 3, halves[1]], w_planes[3][:].indirect(part(HALF, N)), COPY)
        interleave(on_scalar, w_il[:], w_bf, W_SPLIT, N)
        interleave(on_vector, w_il[:], w_bf, 0, P)
        interleave(on_vector, w_il[:], w_bf, P, W_SPLIT)
        for cols in (block(0), block(1), halves[1]):
            quantise(w_q, cols, w_il[:, cols, :].rearrange("p i j -> p (i j)"), E4)
        x0_src = x0_raw[:].rearrange("p j (m t) -> p j m t", t=4)
        x_interleave(on_vector, x0_il[0], x0_src[:, :, :, 0:2])
        x_interleave(on_scalar, x0_il[1], x0_src[:, :, :, 2:4])
        for pair in range(2):
            quantise(x_q[0], halves[pair], x0_flat[pair], E4)
        factors1 = sb("factors1", [P, 5 * N], F32, "x0_raw0")
        factors[1] = factors1[:, 0 : 4 * N].rearrange("p (t i) -> p t i", t=4)
        ws_words = factors1[:, 3 * N : 5 * N]
        for half in range(2):
            ws_il[half] = ws_words.rearrange("p (q j u) -> p j q u", j=4, u=2)[:, 2 * half : 2 * half + 2]
            turn_w(half)

        factors[0] = factors0[:].rearrange("p (t i) -> p t i", t=4)
        factor(0, 0)
        scores(0, 0)
        factor(0, 1)
        scores(0, 1)
        factor(0, 2)
        factor(0, 3)
        scores(0, 2)
        scores(0, 3)
        factor(1, 0)
        factor(1, 1)
        x1_flat = sb("x1_il", [P, 4 * N], BF16, "z3")[:]
        x1_src = x1_raw[:].rearrange("p j (m t) -> p j m t", t=4)
        x_interleave(on_scalar, x1_flat.rearrange("p (t m j) -> p t m j", t=4, j=4), x1_src)
        gradient(0, whole)

        x_q[1] = mx_tiles("x1", "w_plane0")
        for pair in range(2):
            quantise(x_q[1], halves[pair], x1_flat[:, 2 * N * pair : 2 * N * (pair + 1)], E4)
        ws_q = mx_tiles("ws", "factors0")
        for half in (1, 0):
            quantise(ws_q, halves[half], ws_words[:, half * N : (half + 1) * N].bitcast(BF16), E4)
        factor(1, 3)
        xm_il = [sb("xm_il0", [P, 3 * P, 4], BF16), None]
        interleave(on_scalar, xm_il[0][:, block(0, 2), :], xm0_raw[0][:], 0, HALF)
        interleave(on_scalar, xm_il[0][:, block(2), :], xm_first[:], 0, P)
        behind_xm = sb("behind_xm", [P, 5 * N], F32, "xm_first")
        margin[1] = behind_xm[:, 0 : 4 * N].rearrange("p (t i) -> p t i", t=4)
        hs_il[0, 0] = behind_xm[:, 4 * N :].bitcast(BF16)
        turn_h(0, 0, 4, on_scalar)
        xm_il[1] = sb("xm_il1", [P, P, 4], BF16, "signed1_3")
        interleave(on_gpsimd, xm_il[1][:], xm_source(1, 1), 0, P)
        scores(1, 0)
        scores(1, 1)
        factor(1, 2)
        scores(1, 2)
        scores(1, 3)
        h_q[0] = mx_tiles("h0", "last_wt1")
        quantise_h(0, whole)
        hs_q[0] = mx_tiles("hs0")
        quantise(hs_q[0], halves[0], hs_il[0, 0], E5)
        quantise_xm("xm0", ((0, 0), (0, 1), (1, 0)), xm_il[0], "z1")
        first = [in_bank(6 + half, f"dw0_{half}", [P, HALF]) for half in range(2)]
        for half in range(2):
            dw_pass(0, 0, first[half], halves[half])
        h1_flat = sb("h_il1", [P, 4 * N], BF16, "z4")
        h_il[1] = h1_flat[:].rearrange("p (i t) -> p i t", t=4)
        hs_il[0, 1] = h1_flat[:, 2 * N : 4 * N]
        turn_h(0, 1, 1, on_scalar)
        rows_out(0, 0, (2, 3), "w_plane2")
        h_q[1] = mx_tiles("h1")
        gradient(1, halves[0])
        quantise(hs_q[0], halves[1], hs_il[0, 1], E5)
        quantise_h(1, halves[0])
        gradient(1, halves[1])
        quantise_xm("xm1", ((1, 1),), xm_il[1], "ts_runs")
        second = in_bank(5, "dw1", [P, N])
        dw_pass(0, 1, second)
        quantise_h(1, halves[1])
        rows_out(0, 1, (0, 1), "w_plane3")
        dw_pass(1, 0, first[0], halves[0])
        dw0 = [copy_out(on_scalar, "dw0_0", first[0]), None]
        dw_pass(1, 0, first[1], halves[1])
        dw_pass(1, 1, second)
        xm_il.append(sb("xm_il2", [P, G * P, 4], BF16, "signed1_3"))
        interleave(on_vector, xm_il[2][:, block(0), :], xm_source(0, 2), 0, P)
        dw0[1] = copy_out(on_vector, "dw0_1", first[1])
        interleave(on_vector, xm_il[2][:, block(1), :], xm_source(1, 2), 0, P)
        dw1 = copy_out(on_vector, "dw1", second)
        quantise_xm("xm2", ((0, 2), (1, 2)), xm_il[2])
        late = sb("late", [P, 4 * N + G * P * 4], BF16, "signed1_3")
        h1_rows = late[:, 0 : 4 * N].rearrange("p (t i) -> p t i", t=4)
        for u in range(2):
            on_gpsimd(h1_rows[:, 2 * u : 2 * u + 2, :], h_il[1][:, :, 2 * u : 2 * u + 2].rearrange("p i t -> p t i"))
        xm_il.append(late[:, 4 * N :].rearrange("p (d t) -> p d t", t=4))
        for g in range(G):
            interleave(on_gpsimd, xm_il[3][:, block(g), :], xm_source(g, 3), 0, P)
        for half in range(2):
            scatter_on_scalar(windows[0], halves[half], dw0[half][:])
        store_block(0)
        nc.vector.tensor_copy(windows[1][:].indirect(offsets[:]), dw1[:])
        store_block(1)
        third = in_bank(2, "dw2", [P, N])
        for g in range(G):
            dw_pass(g, 2, third)
        dw2 = copy_out(on_scalar, "dw2", third, "w_plane2")
        for cols in halves:
            scatter_on_scalar(windows[2], cols, dw2[:, cols])
        store_block(2)
        hs1_words = sb("hs_il1", [P, 4, P, 2], F32, "dw1")
        for u in range(2):
            turn_words(on_vector, hs1_words[:, 2 * u : 2 * u + 2], h1_rows[:, 2 * u : 2 * u + 2, :], 6 + u, f"h1_{u}")
        quantise_xm("xm3", ((0, 3), (1, 3)), xm_il[3])
        fourth = in_bank(5, "dw3", [P, N])
        for g in range(G):
            dw_pass(g, 3, fourth)
        hs_q[1] = mx_tiles("hs1")
        quantise(hs_q[1], whole, hs1_words[:].rearrange("p t q u -> p (t q u)").bitcast(BF16), E5)
        dw3 = copy_out(on_scalar, "dw3", fourth, "w_plane2")
        nc.vector.tensor_copy(windows[0][:].indirect(offsets[:]), dw3[:])
        store_block(3)
        rows_out(1, 0, (3, 0), "w_plane0")
        rows_out(1, 1, (1, 2), "w_plane1")
